import numpy as np, ml_dtypes
CORES = [24,25,26,27,28,29,30,31]
N = 8
BF = ml_dtypes.bfloat16
def gentries(a):
    return np.ascontiguousarray(a.reshape(8, 16, -1).transpose(0, 2, 1)).reshape(8, -1)
def gtable(e):
    e = np.asarray(e); return np.ascontiguousarray(e.reshape(8, -1, 16).transpose(0, 2, 1)).reshape(128, -1).astype(np.int32)
V, L, RO, LAM, MU, STEP = 2048, 3, 2, 6, 5, 3
def perms(rng):
    return np.argsort(rng.random((N, 8, V)), axis=-1)
def parts(rng):
    sh = (N, 8, 16, V)
    return rng.integers(0, 32, sh, dtype=np.int32), rng.integers(2, 62, sh, dtype=np.int32), rng.integers(0, 100, sh, dtype=np.int32), perms(rng), perms(rng)
def pick(t, ix):
    return np.stack([np.stack([np.take(t[q, g], ix[q, g], axis=-1) for g in range(8)]) for q in range(N)])
def edges(h, a, b):
    hp = np.roll(h, 1, axis=0)
    return np.abs(h - pick(hp, a)), np.abs(h - pick(hp, b))
def forest(f, p, a, b, da, db):
    won = []
    for t in range(L):
        if t: p = np.roll(p, 1, axis=0)
        c0 = pick(p, a) + da; c1 = pick(p, b) + db
        w = np.add.reduce(c1 < c0, axis=2, dtype=np.int32) >= 9
        p = np.where(w[:, :, None, :], c1, c0) + f
        won.append(w)
    return p, won
def entered(wrong, won, a, b):
    m = wrong; u = np.zeros_like(m)
    for t in range(L - 1, 0, -1):
        x = np.zeros_like(m); y = np.zeros_like(m)
        np.put_along_axis(x, a, m & ~won[t], 2); np.put_along_axis(y, b, m & won[t], 2)
        m = np.roll(x | y, -1, axis=0); u = u | m
    return u
def bar(h, e, p, a, b):
    da, db = edges(h, a, b); c, won = forest(e, p, a, b, da, db)
    return np.ascontiguousarray(np.sort(c, axis=2)[:, :, 7, :]).astype(np.int64)
def pack(h, e, p, z, a, b):
    w = lambda x: np.ascontiguousarray(x.reshape(N, 128, V)).astype(np.float32).astype(BF)
    return {"hf": w(h), "toll": w(e), "p0": w(p), "lim": np.clip(z, 0, 1023).astype(np.int32), "sa": np.stack([gtable(x) for x in a]), "sb": np.stack([gtable(x) for x in b])}
def near(rng, q, share, under, over):
    return np.where(rng.random(q.shape) < share, q - 1 - rng.integers(0, under, q.shape), q + rng.integers(0, over, q.shape))
def classes(rng, to):
    x = np.zeros(V, np.int64)
    for c in range(8): x[c::8] = 8 * rng.permutation(V >> 3) + to[c]
    return x
def setup_inputs(rng):
    h, e, p, a, b = parts(rng)
    return pack(h, e, p, near(rng, bar(h, e, p, a, b), 0.2, 12, 24), a, b)
def setup_inputs_spread(rng):
    h, e, p, a, b = parts(rng); col = (N, 8, 1, V)
    h = np.minimum(np.exp2(2 + 3 * rng.random(col)) * rng.random(h.shape), 31).astype(np.int32)
    e = np.minimum(64 * rng.random(col) ** 2 * rng.random(e.shape) + rng.integers(0, 8, e.shape), 63).astype(np.int32)
    p = np.minimum(np.exp2(3 + 5 * rng.random(col)) * rng.random(p.shape), 255).astype(np.int32)
    h[:, :, :, ::5] = rng.integers(0, 32, h[:, :, :, ::5].shape); e[:, :, :, ::3] = rng.integers(0, 64, e[:, :, :, ::3].shape); p[:, :, :, ::7] = rng.integers(0, 256, p[:, :, :, ::7].shape)
    return pack(h, e, p, near(rng, bar(h, e, p, a, b), 0.3, 60, 90), a, b)
def setup_inputs_ends(rng):
    sh = (N, 8, 16, V)
    h = 31 * rng.integers(0, 2, sh, dtype=np.int32); e = 63 * rng.integers(0, 2, sh, dtype=np.int32); p = 255 * rng.integers(0, 2, sh, dtype=np.int32)
    z = 1023 * (rng.random((N, 8, V)) >= 0.25).astype(np.int64)
    a = np.zeros((N, 8, V), np.int64); b = np.zeros((N, 8, V), np.int64)
    hi = np.concatenate([np.arange(16), np.arange(V - 16, V)]); lo = np.arange(16, 48); mid = np.arange(48, V - 16)
    for q in range(N):
        for g in range(8):
            for s in (a, b):
                for x in (hi, lo, mid): s[q, g, x] = x[rng.permutation(len(x))]
            if g % 2: a[q, g, hi] = hi[::-1]; b[q, g, hi] = hi
            if g == 5: a[q, g, lo] = lo[::-1]; b[q, g, lo] = lo
    h[:, :, :, hi] = 31 * (np.arange(N) % 2)[:, None, None, None]; e[:, :, :, hi] = 63; p[:, :, :, hi] = 255
    h[:, :, :, lo] = 0; e[:, :, :, lo] = 0; p[:, :, :, lo] = 0
    z[:, :, V - 1] = 0
    p[:, 5, :, lo] = 1
    z[:, 5, lo] = 1023; z[:, 7, hi[1:31]] = 1023
    for i in range(16):
        x, y = rng.integers(0, 2, 2)
        z[i % N, 5, lo[31 - i if x else i]] = 0
        if i: z[i % N, 7, hi[31 - i if y else i]] = 254 + 94 * L
    return pack(h, e, p, z, a, b)
def setup_inputs_corners(rng):
    h, e, p, a, b = parts(rng); w = rng.permutation(8); k = np.arange(V)
    b[:, w[2]] = a[:, w[2]]
    b[:, w[3]] = a[:, w[3]] ^ 1; e[:, w[3]] = 63 * (k % 2)
    a[:, w[4]] = k; b[:, w[4]] = V - 1 - k
    p[:, w[5]] = rng.integers(0, 256, (N, 1, 1)); e[:, w[5]] = rng.integers(0, 64, (N, 1, 1)); h[:, w[5]] = rng.integers(0, 32, (N, 16, 1))
    lev = rng.integers(0, 2, (N, 1, V)); cut = 7 + rng.integers(0, 3, (N, 1, V))
    p[:, w[6]] = np.where(np.arange(16)[None, :, None] < cut, 10 * lev, 10 - 10 * lev); e[:, w[6]] = 20; h[:, w[6]] = rng.integers(0, 32, (N, 16, 1))
    e[:, w[7]] = 63 * rng.integers(0, 2, (N, 16, V))
    q = bar(h, e, p, a, b); z = q + rng.integers(-1, 2, q.shape)
    odd = (np.arange(N) % 2)[:, None]
    z[:, w[0]] = np.where(odd == 0, 1023, 0); z[:, w[1]] = np.where(odd == 0, 0, 1023)
    return pack(h, e, p, z, a, b)
def setup_inputs_calm(rng):
    h, e, p, a, b = parts(rng); sh = h.shape
    low = (rng.random(sh) < 0.25).astype(np.int64); low[:, 6, ::2] = rng.integers(0, 5, low[:, 6, ::2].shape)
    i = rng.permutation(16)
    for j, (x, y) in enumerate(((3, 0), (5, 5), (5, 4))): low[::2, 3, i[j]] = x; low[1::2, 3, i[j]] = y
    h = np.where((np.arange(N) % 2 == 1)[:, None, None, None], 31 - low, low).astype(np.int32); p = rng.integers(0, 4, sh, dtype=np.int32)
    base = 60 * ((np.arange(N)[:, None] + np.arange(8)[None, :]) % 2)
    base[:, 5] = 60; base[:, 7] = 60; p[:, 5] += 252; p[:, 7] += 128
    e = (base[:, :, None, None] + rng.integers(0, 4, sh)).astype(np.int32)
    z = bar(h, e, p, a, b)
    for q in range(N):
        for g in range(4): z[q, g, rng.permutation(V)[:g]] -= 1
    z[:, 4:] -= (rng.random((N, 4, V)) < 0.15)
    return pack(h, e, p, z, a, b)
def setup_inputs_crowd(rng):
    h, e, p, a, b = parts(rng); k = np.arange(V); first = k[(k & 2) == 0]; k8 = k & 7
    gap = np.array([3, LAM + MU, LAM + MU + 1, 30, 60, 60, 60, 60])[None, :, None, None]; odd = (k % 2)[None, None, None, :]
    h[:, :4] = rng.integers(0, 32, (N, 4, 16, 1)); h[:, 4:] = rng.integers(0, 11, (N, 4, 16, V))
    e = (rng.integers(0, 4, (N, 8, 16, 1)) + gap * odd).astype(np.int32); p = (rng.integers(20, 100, (N, 8, 16, 1)) + gap * odd).astype(np.int32)
    z = np.zeros((N, 8, V), np.int64)
    for q in range(N):
        for g in range(6):
            c = 2 * rng.permutation(V // 2); o = rng.integers(0, 2, V // 2)
            a[q, g, first] = c + o; a[q, g, first + 2] = c + 1 - o
            if g % 2:
                i = 2 * int(rng.integers(0, V // 2)); x = e[q, g]; x[:, [i, i + 1]] = x[:, [i + 1, i]]
                z[q, g, int(rng.integers(0, V))] = 1023
    b[:, :6] = a[:, :6] ^ 1
    step = np.array([0, 0, 0, 25, 25, 25, 25, 55])[k8]
    h[:, 6] = rng.integers(0, 30, (1, 16, 1)) + 2 * (k8 == 4)
    e[:, 6] = rng.integers(0, 4, (N, 16, 1)) + step; p[:, 6] = rng.integers(20, 100, (N, 16, 1)) + step
    h[:, 7] = rng.integers(0, 28, (1, 16, 1)) + (k8 >> 1)
    e[:, 7] = rng.integers(10, 51, (N, 16, 1)); p[:, 7] = rng.integers(20, 100, (N, 16, 1))
    h[:, 4] = rng.integers(0, 11, (N, 16, 1)); p[:, 4] = rng.integers(20, 100, (N, 16, 1))
    e[:, 4] = rng.integers(20, 41, (N, 16, 1)) + np.where(k8 < 6, k8 & 1, 0)
    for q in range(N):
        a[q, 4] = classes(rng, (2, 4, 6, 1, 3, 5, 0, 7)); b[q, 4] = classes(rng, (3, 5, 1, 7, 0, 2, 4, 6))
        a[q, 6] = classes(rng, (2, 0, 4, 1, 6, 7, 5, 3)); b[q, 6] = classes(rng, (7, 3, 0, 5, 1, 2, 6, 4))
        a[q, 7] = classes(rng, (0, 1, 2, 3, 4, 5, 6, 7)); b[q, 7] = classes(rng, (2, 3, 4, 5, 6, 7, 0, 1))
    z[:, 4] = np.where(k8 < 6, bar(h, e, p, a, b)[:, 4] - 1, 1023)
    return pack(h, e, p, z, a, b)
def check_ranges(d):
    bad = []
    for k, lo, hi in (("hf", 0, 31), ("toll", 0, 63), ("p0", 0, 255), ("lim", 0, 1023), ("sa", 0, V - 1), ("sb", 0, V - 1)):
        x = np.asarray(d[k]).astype(np.float64)
        if not np.all((x >= lo) & (x <= hi) & (x == np.floor(x))): bad.append("range of " + k)
    for k in ("sa", "sb"):
        if any(np.any(np.sort(gentries(np.asarray(d[k])[q]), axis=1) != np.arange(V)) for q in range(N)): bad.append("numbers of " + k + " not each once")
    return bad
def reference(hf, toll, p0, lim, sa, sb):
    whole_ = lambda x: x.astype(np.float32).astype(np.int32).reshape(N, 8, 16, V)
    h = whole_(hf); e = whole_(toll); p = whole_(p0); z = lim.astype(np.int32)[:, :, None, :]
    a = np.stack([gentries(x) for x in sa]).astype(np.int64); b = np.stack([gentries(x) for x in sb]).astype(np.int64)
    da, db = edges(h, a, b); tab = np.exp(-0.125 * np.arange(32)); gain = np.zeros((N, 8, 16, V))
    ident = np.broadcast_to(np.arange(V), (N, 8, V))
    for rnd in range(RO):
        last, w1 = forest(e, p, a, b, da, db)
        wrong = np.add.reduce(last > z, axis=2, dtype=np.int32) >= 9
        m1 = entered(wrong, w1, a, b).astype(np.int32)
        f = e + (LAM * m1 + MU * np.roll(m1, -1, axis=1))[:, :, None, :]
        unused, w2 = forest(f, p, a, b, da, db)
        m2 = entered(wrong, w2, a, b).astype(np.int32)
        na = ident; nb = ident; fa = h; fb = h; acc = np.zeros((N, 8, 16, V))
        for t in range(L - 1, 0, -1):
            na = np.roll(pick(np.where(w1[t], b, a), na), -1, axis=0); nb = np.roll(pick(np.where(w2[t], b, a), nb), -1, axis=0)
            oa = np.roll(fa, -1, axis=0); ob = np.roll(fb, -1, axis=0)
            fa = pick(h, na); fb = pick(h, nb)
            acc = np.roll(acc, -1, axis=0) + tab[np.abs(fa - ob)] + 0.5 * tab[np.abs(fb - oa)]
        gain = gain + acc
        e = np.clip(e + STEP * (m1 - m2)[:, :, None, :], 0, 63)
    return {"gain": gain.reshape(N, 128, V).astype(np.float32), "tollout": e.reshape(N, 128, V).astype(np.float32)}

def check_inputs(d):
    bad = list(check_ranges(d))
    if not bad:
        for name, y in reference(**d).items():
            for q in range(N):
                v = np.abs(np.asarray(y[q], np.float64)); s = np.sqrt(np.mean(v * v))
                if v.max() > 4 * s or s < 2.0 ** -4: bad.append('%s of rank %d is uneven or too small' % (name, q))
    return bad

@@ -1,0 +1,716 @@
+import math
+import numpy as np
+from concourse.bass import DstId, RemoteDMATransfer
+from concourse.mybir import AluOpType as A, ActivationFunctionType as AF, AxisListType as AX
+
+V = 2048
+CH = 512
+NC = V // CH
+CENTER = 240.0
+BF, F32, I32, U16, F16 = "bfloat16", "float32", "int32", "uint16", "float16"
+
+SCRATCH = {}
+for _n in ("h", "hm", "p0s", "E0", "E1", "E2", "E0n", "dl", "dl2", "XA", "Fo0", "Fo1", "U", "B6",
+           "P1", "W", "gx", "gy", "q", "dA", "dB", "Bc", "t0", "t1"):
+    SCRATCH[_n] = ("sbuf", [128, V], BF)
+for _n in ("NQ", "DD", "SS1", "DD1", "DD2", "CC"):
+    SCRATCH[_n] = ("sbuf", [128, 2 * V], BF)
+SCRATCH["IND"] = ("sbuf", [128, 3, V], BF)
+for _n in ("cx", "cy"):
+    SCRATCH[_n] = ("sbuf", [128, V], F16)
+for _n in ("J", "SCa", "SCb", "eb", "to", "Ub"):
+    SCRATCH[_n] = ("sbuf", [128, V], F32)
+for _n in ("tab", "tab1", "tab2"):
+    SCRATCH[_n] = ("sbuf", [128, 384], I32)
+for _n in ("u0", "u1", "u2", "inv", "inv1", "inv2"):
+    SCRATCH[_n] = ("sbuf", [128, 256], U16)
+for _n in ("sel0", "selA", "selB", "lA", "lB"):
+    SCRATCH[_n] = ("sbuf", [128, 128], U16)
+for _n in ("I", "nI", "Msh", "ones", "s1", "s2", "tt", "wr", "ws1", "wsA0", "wsB0", "wsA1", "wsB1", "qc", "cb", "ca", "ent", "ent3", "Mt", "dm",
+           "mo0", "mo1", "mo2", "mo3", "mi0", "mi1", "mi2", "mi3"):
+    SCRATCH[_n] = ("sbuf", [128, 128], BF)
+SCRATCH["b3"] = ("sbuf", [128, 384], BF)
+SCRATCH["nz"] = ("sbuf", [128, 128], F16)
+SCRATCH["Tl"] = ("sbuf", [128, 160], BF)
+SCRATCH["T2"] = ("sbuf", [128, 160], BF)
+SCRATCH["Tr"] = ("sbuf", [128, 160], BF)
+SCRATCH["Tf"] = ("sbuf", [128, 160], F32)
+SCRATCH["g8"] = ("sbuf", [128, 16], BF)
+for _n in ("io16", "ioL", "f1", "f2", "f3", "f4", "a2f", "dab"):
+    SCRATCH[_n] = ("sbuf", [128, 128], F32)
+SCRATCH["vf"] = ("sbuf", [128, 256], F32)
+SCRATCH["vi"] = ("sbuf", [128, 256], I32)
+SCRATCH["pi"] = ("sbuf", [128, 8], I32)
+SCRATCH["pm"] = ("sbuf", [128, 8], I32)
+SCRATCH["pf"] = ("sbuf", [128, 8], F32)
+for _k in range(8):
+    SCRATCH["ps%d" % _k] = ("psum", [128, CH], F32)
+
+SEMAPHORES = ["ev", "es", "ep", "eg", "sent", "left"] + ["d%d" % _k for _k in range(40)] + ["r%d" % _k for _k in range(30)]
+
+CYC, PCY, GA, SC, LAT = 1.0, 0.5, 1.56, 3.8, 120.0
+FW = 512
+PAR = {"fe": ("vs",) * 8, "cuts": (0, 4, 8, 12, 16), "clip": (0, 2), "wd": 0, "gap": 2000.0, "ahead": 0.5, "o1": (3, 2, 1, 0), "oA": (0, 1, 2, 3), "oB": (0, 2, 1, 3), "u": 0, "vs": 1, "ss": (3,), "nq": (), "s1": (3,), "sel": (2, 3), "s2A": (), "s2B": (2, 3), "s0": (3,), "eps": 300.0, "tries": 0, "sigma": 3000.0}
+PAR.update({"wd": 0, "u": 1, "vs": 1, "nq": (3,), "s0": (3,), "ss": (3,), "s1": (3,), "sel": (2, 3), "o1": (0, 1, 2, 3), "oB": (2, 0, 3, 1),
+            "s2B": (2, 3), "gap": 2000.0, "ahead": 0.4, "eps": 300.0, "cuts": (0, 5, 10, 14, 16), "clip": (0, 2),
+            "fe": ("s", "vs", "vs", "vs", "vs", "s", "s", "vs")})
+
+
+def build(T, topo, core):
+    ops = []
+    acc = {}
+    cnt = {"d": 0, "r": 0, "ps": 0, "pf": 0}
+    rank = T.rank_of(core)
+    n = len(T.cores)
+
+    def op(eng, fn, R, Wr, cost, kind="c", lat=0.0, extra=()):
+        o = {"i": len(ops), "eng": eng, "fn": fn, "cost": cost, "kind": kind, "lat": lat, "deps": {}, "W": Wr}
+        for e in extra:
+            o["deps"][e["i"]] = True
+        for lst, isw in ((R, False), (Wr, True)):
+            for (b, lo, hi) in lst:
+                ps = b.startswith("ps")
+                keep = []
+                for (p, l2, h2, w2) in acc.get(b, []):
+                    over = l2 < hi and lo < h2
+                    if p is not o and (over or ps):
+                        if over and (isw or w2):
+                            o["deps"][p["i"]] = True
+                        elif ps and p["i"] not in o["deps"]:
+                            o["deps"][p["i"]] = False
+                    if not (isw and lo <= l2 and h2 <= hi and p is not o):
+                        keep.append((p, l2, h2, w2))
+                keep.append((o, lo, hi, isw))
+                acc[b] = keep
+        ops.append(o)
+        return o
+
+    def r(b, lo=0, hi=1 << 20):
+        return (b, lo, hi)
+
+    def ap(x):
+        b, lo, hi = x
+        return T[b][:, lo:hi]
+
+    def ch(b, c, off=0):
+        return (b, off + c * CH, off + (c + 1) * CH)
+
+    def bank():
+        cnt["ps"] += 1
+        return "ps%d" % (cnt["ps"] % 4)
+
+    def fbank():
+        cnt["pf"] += 1
+        return "ps%d" % (4 + cnt["pf"] % 2)
+
+    def cst(nel, k=1.0):
+        return 60.0 + max(64.0, nel * k) * CYC
+
+    def vop(fn, R, Wr, nel, k=1.0):
+        return op("v", lambda g, e: fn(g.vector), R, Wr, cst(nel, k))
+
+    def sop(out, src, func, bias=0.0, scale=1.0):
+        return op("s", lambda g, e: g.scalar.activation(ap(out), ap(src), func, bias=bias, scale=scale), [src], [out], cst(out[2] - out[1]))
+
+    def ts(out, src, s1, s2, o0, o1=None, k=1.0):
+        if o1 is None:
+            return vop(lambda v: v.tensor_scalar(ap(out), ap(src), s1, None, o0), [src], [out], out[2] - out[1], k)
+        return vop(lambda v: v.tensor_scalar(ap(out), ap(src), s1, s2, o0, o1), [src], [out], out[2] - out[1], k)
+
+    def tt(out, a, b, o, k=2.0):
+        return vop(lambda v: v.tensor_tensor(ap(out), ap(a), ap(b), o), [a, b], [out], out[2] - out[1], k)
+
+    def cp(out, src):
+        return vop(lambda v: v.tensor_copy(ap(out), ap(src)), [src], [out], out[2] - out[1])
+
+    def evac(out, src, eng="vs"):
+        def fn(g, e):
+            if e == "v":
+                return g.vector.tensor_copy(ap(out), ap(src))
+            return g.scalar.activation(ap(out), ap(src), AF.Copy)
+        return op(eng, fn, [src], [out], cst(out[2] - out[1]))
+
+    def ind(win, off):
+        return ap(win).indirect(ap(off))
+
+    def offs(b, c, off=0):
+        return (b, off + c * CH // 16, off + (c + 1) * CH // 16)
+
+    def gather(out, win, off, eng="vs", sign=0):
+        def fn(g, e):
+            if e == "v":
+                if sign:
+                    return g.vector.tensor_scalar(ap(out), ind(win, off), float(sign), 0.0, A.mult, A.max)
+                return g.vector.tensor_copy(ap(out), ind(win, off))
+            if sign:
+                return g.scalar.activation(ap(out), ind(win, off), AF.Relu, scale=float(sign))
+            return g.scalar.activation(ap(out), ind(win, off), AF.Copy)
+        return op(eng, fn, [win, off], [out], cst(out[2] - out[1], GA))
+
+    def gfuse(out, win, off, other, o):
+        return vop(lambda v: v.tensor_tensor(ap(out), ind(win, off), ap(other), o), [win, off, other], [out], out[2] - out[1], GA)
+
+    def mm(mats, R, Wr):
+        def fn(g, e):
+            last = None
+            for (o, l, x, st, sp, nn) in mats:
+                last = g.tensor.matmul(o, l, x, st, sp)
+            return last
+        return op("p", fn, R, Wr, sum(max(64, m[5]) * PCY + 10.0 for m in mats))
+
+    def psum(ps, c, plus, minus=(), table=None, bc="Bc", late=False):
+        mats = [[T[ps][:, :], T.I[:, :], ap(x), False, False, CH] for x in plus]
+        mats += [[T[ps][:, :], T.nI[:, :], ap(x), False, False, CH] for x in minus]
+        alone = not mats
+        R = list(plus) + list(minus) + [r("I"), r("nI")]
+        if not alone:
+            mats[0][3] = True
+        if late:
+            mm(mats, R, [r(ps, 0, CH)])
+            mats, R = [], []
+        if table:
+            R += [r(table), r(bc)]
+            for k in range(CH // 128):
+                qq = c * (CH // 128) + k
+                mats.append([T[ps][:, 128 * k:128 * k + 128], T[bc][:, 128 * qq:128 * qq + 128], T[table][:, :], alone, alone, 128])
+        mats[-1][4] = True
+        return mm(mats, R, [r(ps, 0, CH)])
+
+    def tolist(ps, col, src, row, hf, tl="Tl"):
+        x = T[src]
+        mats = []
+        for i in range(16):
+            s = slice(1024 * hf + i, 1024 * hf + 1024, 16)
+            mats.append([T[ps][:, col + 64 * hf:col + 64 * hf + 64], T[tl][:, 16 - i:144 - i], x[:, row, s], i == 0, i == 15, 64])
+        return mm(mats, [r(src, row * V + 1024 * hf, row * V + 1024 * hf + 1024), r(tl)], [r(ps, col + 64 * hf, col + 64 * hf + 64)])
+
+    def toblock(ps, srcs, c, rows, last, R, tl="Tl", first=0):
+        mats = []
+        for k in range(CH // 128):
+            qq = c * (CH // 128) + k
+            for s in srcs:
+                mats.append([T[ps][:, 0:128 * rows], T[tl][:, 16 - qq:144 - qq], s(128 * qq, 128 * qq + 128), False, False, 128 * rows])
+        mats[0][3] = c == first
+        mats[-1][4] = last
+        return mm(mats, R + [r(tl)], [r(ps, 0, 128 * rows)])
+
+    def dma(eng, out, src, R, Wr, nbytes, add=False):
+        s = "d%d" % cnt["d"]
+        cnt["d"] += 1
+        if add:
+            fn = lambda g, e: g.dma_start(out, src, accum_op=A.add)
+        elif eng == "y":
+            fn = lambda g, e: g.sync.dma_start(out, src)
+        else:
+            fn = lambda g, e: g.scalar.dma_start(out, src)
+        o = op(eng, fn, R, Wr, 1000.0 if eng == "g" else 100.0, "d", 2000.0 + nbytes * (2 if add else 1) / 400.0)
+        o["sem"] = s
+        return o
+
+    def send(items, nbytes, loc="sent"):
+        trs = []
+        for k, (src, sh, dst) in enumerate(items):
+            to = T.cores[(rank + sh) % n]
+            en = topo.engines(core, to)
+            per = len(en) // len(items)
+            mask = sum(1 << x for x in en[k * per:(k + 1) * per])
+            rid, pid = topo.addr(to)[:2]
+            s = "r%d" % cnt["r"]
+            cnt["r"] += 1
+            trs.append((src, dst, mask, rid, pid, s, per))
+
+        def fn(g, e):
+            if len(trs) == 1:
+                src, dst, mask, rid, pid, s, per = trs[0]
+                return g.remote_dma(T[dst][:, :], T[src][:, :], T.sem[s], T.sem[loc], pid, rid, mask)
+            return g.remote_dma_fused([RemoteDMATransfer(dst_ids=[DstId(rid=rid, pnc=pid)], dma_engine_mask=mask, remote_sem=T.sem[s],
+                                                         src=T[src][:, :], dst=T[dst][:, :])
+                                       for (src, dst, mask, rid, pid, s, per) in trs], local_sem=T.sem[loc])
+        o = op("g", fn, [r(x[0]) for x in trs], [], 800.0, "x")
+        o["inc"] = sum(x[6] for x in trs)
+        if loc != "sent":
+            a = op(None, None, [r(x[0]) for x in trs], [], 0.0, "a", 2500.0 + nbytes * len(trs) / 250.0, extra=[o])
+            a["sem"] = loc
+            a["val"] = o["inc"]
+            o["inc"] = 0
+        for x in trs:
+            a = op(None, None, [], [r(x[1])], 0.0, "a", 2500.0 + nbytes * len(trs) / 250.0, extra=[o])
+            a["sem"] = x[5]
+            a["val"] = x[6]
+
+    def gop(fn, R, Wr, nel):
+        return op("g", lambda g, e: fn(g), R, Wr, 170.0 + 2.0 * nel * CYC)
+
+    BIG = 128 * V * 2
+    dma("y", T.h[:, :], T.hf[:, :], [], [r("h")], BIG)
+    dma("s", T.tab[:, 0:128], T.sa[:, :], [], [r("tab", 0, 128)], BIG // 8)
+    dma("s", T.tab[:, 128:256], T.sb[:, :], [], [r("tab", 128, 256)], BIG // 8)
+    dma("s", T.tab[:, 256:384], T.lim[:, :], [], [r("tab", 256, 384)], BIG // 8)
+    dma("y", T.E0[:, :], T.toll[:, :], [], [r("E0")], BIG)
+    dma("y", T.p0s[:, :], T.p0[:, :], [], [r("p0s")], BIG)
+    for lo in (0, 1024):
+        gop(lambda g, lo=lo: g.iota(T.J[:, lo:lo + 1024], [[1, 1024]], 32 + lo, 0, allow_small_or_imprecise_dtypes=True), [], [r("J", lo, lo + 1024)], 1024)
+    send([("h", 1, "hm")], BIG)
+    send([("tab", -1, "tab1"), ("tab", -2, "tab2")], BIG // 3)
+    send([("E0", -1, "E1"), ("E0", -2, "E2")], BIG)
+    vop(lambda v: v.memset(T.ones[:, :], 1.0), [], [r("ones")], 64)
+    vop(lambda v: v.memset(T.Tl[:, :], 0.0), [], [r("Tl")], 80)
+    vop(lambda v: v.memset(T.Bc[:, :], 1.0), [], [r("Bc")], V, 0.5)
+    gop(lambda g: g.affine_select(T.I[:, :], T.ones[:, :], [[-1, 128]], A.is_equal, 0.0, 0, 1), [r("ones")], [r("I")], 128)
+    gop(lambda g: g.affine_select(T.g8[:, 0:8], T.ones[:, 0:8], [[-16, 8]], A.is_ge, 0.0, 0, 1), [r("ones")], [r("g8", 0, 8)], 8)
+    gop(lambda g: g.affine_select(T.g8[:, 8:16], T.g8[:, 0:8], [[16, 8]], A.is_ge, 0.0, 15, -1), [r("g8", 0, 8)], [r("g8", 8, 16)], 8)
+    gop(lambda g: g.iota(T.pi[:, 0:1], [[0, 1]], 0, 1), [], [r("pi")], 1)
+    gop(lambda g: g.iota(T.io16[:, :], [[16, 128]], 0, 0, allow_small_or_imprecise_dtypes=True), [], [r("io16")], 128)
+    gop(lambda g: g.affine_select(T.Bc[:, :], T.Bc[:, :], [[-1, 16], [-16, 8], [0, 16]], A.is_equal, 0.0, 0, 1), [r("Bc")], [r("Bc")], V)
+    vop(lambda v: v.tensor_copy(T.Tl[:, 16:144:16], T.g8[:, 8:16]), [r("g8")], [r("Tl")], 8)
+    ts(r("Tf", 0, 160), r("Tl", 0, 160), 1.0 / 16, None, A.mult)
+    ts(r("nI", 0, 128), r("I", 0, 128), -1.0, None, A.mult)
+    ts(r("T2", 0, 160), r("Tl", 0, 160), 2.0, None, A.mult)
+    if PAR["wd"]:
+        vop(lambda v: v.memset(T.W[:, :], 0.0), [], [r("W")], V, 0.5)
+        vop(lambda v: v.tensor_reduce(T.pf[:, 4:5], T.I[:, 0:128:18], AX.X, A.add), [r("I")], [r("pf", 4, 5)], 8)
+        vop(lambda v: v.tensor_scalar(T.Tr[:, :], T.Tl[:, :], T.pf[:, 4:5], None, A.mult), [r("Tl"), r("pf", 4, 5)], [r("Tr")], 160)
+    vop(lambda v: v.memset(T.B6[:, :], 6.0), [], [r("B6")], V, 0.5)
+    for hf in range(4):
+        lo, hi = 512 * hf, 512 * hf + 512
+        for (cmp, fill, base) in ((A.is_equal, 0.0, 0), (A.not_equal, 5.0, -16), (A.not_equal, 5.0, 112)):
+            gop(lambda g, lo=lo, hi=hi, cmp=cmp, fill=fill, base=base - 4 * hf:
+                g.affine_select(T.B6[:, lo:hi], T.B6[:, lo:hi], [[-1, 4], [-16, 8], [0, 16]], cmp, fill, base, 1), [r("B6", lo, hi)], [r("B6", lo, hi)], 512)
+    ts(r("pm", 0, 1), r("pi", 0, 1), 15, None, A.bitwise_and)
+    cp(r("pf", 0, 1), r("pm", 0, 1))
+    vop(lambda v: v.tensor_scalar(T.ioL[:, :], T.io16[:, :], T.pf[:, 0:1], None, A.add), [r("io16"), r("pf", 0, 1)], [r("ioL")], 128)
+    cp(r("u0", 0, 256), r("tab", 0, 256))
+    for hf in range(2):
+        lo = 1024 * hf
+        vop(lambda v, lo=lo: v.tensor_copy(T.SCa[:, :].indirect(T.u0[:, lo // 16:lo // 16 + 64]), T.J[:, lo:lo + 1024]),
+            [r("J", lo, lo + 1024), r("u0")], [r("SCa")], 1024, SC)
+        op("s", lambda g, e, lo=lo: g.scalar.activation(T.SCb[:, :].indirect(T.u0[:, 128 + lo // 16:128 + lo // 16 + 64]), T.J[:, lo:lo + 1024], AF.Silu),
+           [r("J", lo, lo + 1024), r("u0")], [r("SCb")], cst(1024, SC) + (1300.0 if hf == 0 else 0.0))
+    for c in range(2):
+        ts(r("p0s", 1024 * c, 1024 * c + 1024), r("p0s", 1024 * c, 1024 * c + 1024), -CENTER, None, A.add, k=0.5)
+    for k, b in enumerate(("SCa", "SCb")):
+        for i in range(16):
+            mm([[T.ps5[:, 128 * k:128 * k + 128], T.Tf[:, 16 - i:144 - i], T[b][:, i:V:16], i == 0, i == 15, 512]],
+               [r(b), r("Tf")], [r("ps5", 128 * k, 128 * k + 128)])
+    sop(r("vf", 0, 256), r("ps5", 0, 256), AF.Identity, bias=-32.0)
+    cp(r("vi", 0, 256), r("vf", 0, 256))
+    cp(r("inv", 0, 256), r("vi", 0, 256))
+    send([("inv", -1, "inv1"), ("inv", -2, "inv2")], BIG // 8)
+    cp(r("u1", 0, 256), r("tab1", 0, 256))
+    cp(r("u2", 0, 256), r("tab2", 0, 256))
+    ts(r("nz", 0, 128), r("tab2", 256, 384), -1.0, CENTER, A.mult, A.add)
+    tt(r("f3", 0, 128), r("tab2", 128, 256), r("tab2", 0, 128), A.subtract)
+    sop(r("dab", 0, 128), r("f3", 0, 128), AF.Identity, scale=0.5)
+    tt(r("a2f", 0, 128), r("tab2", 0, 128), r("dab", 0, 128), A.add)
+    for c in range(NC):
+        for k in range(2):
+            if c in PAR["ss"]:
+                gather(ch("t%d" % k, c), r("hm", 0, V), offs("u0", c, 128 * k), "s")
+                ps = bank()
+                psum(ps, c, [ch("t%d" % k, c)], [ch("h", c)])
+                sop(ch("DD", c, k * V), r(ps, 0, CH), AF.Abs)
+                evac(ch("NQ", c, k * V), r(ps, 0, CH), "s")
+            else:
+                gfuse(ch("NQ", c, k * V), r("hm", 0, V), offs("u0", c, 128 * k), ch("h", c), A.subtract)
+                sop(ch("DD", c, k * V), ch("NQ", c, k * V), AF.Abs)
+    send([("DD", -1, "DD1")], 2 * BIG)
+
+    def add_gather(out, win, off, other, c, share, tmp, neg=False):
+        if c not in share:
+            return gfuse(out, win, off, other, A.subtract if neg else A.add)
+        gather(ch(tmp, c), win, off, "s")
+        ps = bank()
+        if neg:
+            psum(ps, c, [ch(tmp, c)], [other])
+        else:
+            psum(ps, c, [ch(tmp, c), other])
+        return evac(out, r(ps, 0, CH), "s")
+
+    def step(win, u, dd, share, sel, nxt, add, ws):
+        for c in share:
+            for k in range(2):
+                add_gather(ch("CC", c, k * V), r(win, 0, V), offs(u, c, 128 * k), ch(dd, c, k * V), c, share, "t%d" % k, dd == "NQ")
+        seen = []
+        for c in PAR["o1"]:
+            seen.append(c)
+            for k in range(2):
+                if c not in share:
+                    add_gather(ch("CC", c, k * V), r(win, 0, V), offs(u, c, 128 * k), ch(dd, c, k * V), c, share, "t%d" % k, dd == "NQ")
+            ps = bank()
+            psum(ps, c, [ch("CC", c)], [ch("CC", c, V)])
+            op("s", lambda g, e, ps=ps, c=c: g.scalar.activation(T.IND[:, 0, c * CH:(c + 1) * CH], T[ps][:, :], AF.Sign, bias=-0.5),
+               [r(ps, 0, CH)], [ch("IND", c)], cst(CH))
+            if c ^ 1 in seen:
+                lo = 64 * (c // 2)
+                pl = "ps%d" % (6 + c // 2)
+                tolist(pl, 0, "IND", 0, c // 2)
+                ts(r("f1", lo, lo + 64), r(pl, lo, lo + 64), 1.0, float(V), A.is_gt, A.mult)
+                tt(r("f2", lo, lo + 64), r("f1", lo, lo + 64), r("ioL", lo, lo + 64), A.add)
+                cp(r(sel, lo, lo + 64), r("f2", lo, lo + 64))
+        if ws:
+            for c in range(NC):
+                toblock("ps7", [lambda a, b: T.IND[:, 0, a:b]], c, 1, c == NC - 1, [ch("IND", c)])
+            sop(r(ws, 0, 128), r("ps7", 0, 128), AF.Sign, bias=-1.0)
+        for c in PAR["o1"]:
+            add_gather(ch(nxt, c), r("CC", 0, 2 * V), offs(sel, c), ch(add, c), c, PAR["sel"], "t0")
+
+    step("p0s", "u0", "DD", PAR["s0"], "sel0", "XA", "E0", None)
+    for c in range(NC):
+        ps = fbank()
+        psum(ps, c, [ch("NQ", c, V)], [ch("NQ", c)])
+        evac(ch("dl", c), r(ps, 0, CH))
+    send([("DD", -2, "DD2"), ("NQ", -1, "SS1")], 2 * BIG, "left")
+    send([("dl", -2, "dl2")], BIG)
+
+    def last_step(first, e2, ws, lst):
+        share = PAR["s2A" if first else "s2B"]
+        rows = 3 if first else 1
+        if first and PAR["u"] == 2:
+            for c in range(NC):
+                for k in range(2):
+                    ps = fbank()
+                    psum(ps, c, [ch(e2, c), ch("DD2", c, k * V)], (), "nz")
+                    evac(ch(("to", "Ub")[k], c), r(ps, 0, CH))
+        if first and PAR["u"] == 1:
+            for c in range(NC):
+                ps = fbank()
+                psum(ps, c, [ch(e2, c)], (), "nz")
+                ts(ch("U", c), r(ps, 0, CH), -256.0, 241.0, A.max, A.min)
+        onv = (not first) and PAR["vs"]
+        order = PAR["oA" if first else "oB"]
+        for c in order:
+            cs = []
+            for k in range(2):
+                o = ch(("gx", "gy")[k], c)
+                if first and PAR["u"] == 2:
+                    o = ch(("cx", "cy")[k], c)
+                    gfuse(o, r("P1", 0, V), offs("u2", c, 128 * k), ch(("to", "Ub")[k], c), A.add)
+                    cs.append([o])
+                elif c in share:
+                    gather(o, r("P1", 0, V), offs("u2", c, 128 * k), "s")
+                    cs.append([o, ch("DD2", c, k * V)])
+                else:
+                    gfuse(o, r("P1", 0, V), offs("u2", c, 128 * k), ch("DD2", c, k * V), A.add)
+                    cs.append([o])
+            for j in range(rows):
+                ps = bank()
+                if j == 0:
+                    psum(ps, c, cs[0], cs[1])
+                elif PAR["u"] == 2:
+                    psum(ps, c, cs[j - 1])
+                elif PAR["u"]:
+                    psum(ps, c, cs[j - 1] + [ch("U", c)])
+                else:
+                    psum(ps, c, cs[j - 1] + [ch(e2, c)], (), "nz")
+                if onv and c < 2:
+                    vop(lambda v, ps=ps, c=c: v.tensor_scalar(T.IND[:, 0, c * CH:(c + 1) * CH], T[ps][:, :], 0.5, 0.5, A.is_gt, A.subtract),
+                        [r(ps, 0, CH)], [ch("IND", c)], CH)
+                else:
+                    op("s", lambda g, e, ps=ps, c=c, j=j: g.scalar.activation(T.IND[:, j, c * CH:(c + 1) * CH], T[ps][:, :], AF.Sign, bias=-0.5),
+                       [r(ps, 0, CH)], [ch("IND", c, j * V)], cst(CH))
+            if first:
+                toblock("ps7", [lambda a, b: T.IND[:, :, a:b]], c, 3, c == order[-1], [ch("IND", c, j * V) for j in range(3)], "Tl", order[0])
+            else:
+                toblock("ps7", [lambda a, b: T.IND[:, 0, a:b]], c, 1, c == order[-1], [ch("IND", c)], "T2" if onv and c < 2 else "Tl", order[0])
+        if first:
+            ts(r("b3", 0, 384), r("ps7", 0, 384), 1.0, None, A.is_gt)
+            tt(r("s1", 0, 128), r("b3", 128, 256), r("b3", 256, 384), A.add)
+            tt(r("s2", 0, 128), r("s1", 0, 128), r("b3", 0, 128), A.mult)
+            tt(r("tt", 0, 128), r("s2", 0, 128), r("b3", 128, 256), A.subtract)
+            sop(r("wr", 0, 128), r("tt", 0, 128), AF.Abs)
+            sop(r(ws, 0, 128), r("b3", 0, 128), AF.Identity, bias=-1.0, scale=2.0)
+        else:
+            sop(r(ws, 0, 128), r("ps7", 0, 128), AF.Sign, bias=-1.0)
+            tt(r("tt", 0, 128), r(ws, 0, 128), r("wr", 0, 128), A.mult)
+        for hf in range(2):
+            tolist("ps6", 0, "IND", 0, hf, "T2" if onv and hf == 0 else "Tl")
+        sop(r("f3", 0, 128), r("ps6", 0, 128), AF.Sign, bias=-1.0)
+        tt(r("f4", 0, 128), r("f3", 0, 128), r("dab", 0, 128), A.mult)
+        tt(r("f3", 0, 128), r("f4", 0, 128), r("a2f", 0, 128), A.add)
+        cp(r(lst, 0, 128), r("f3", 0, 128))
+
+    def level(inv, more):
+        if PAR["wd"]:
+            dma("y", T.W[0:128:18, :], T.tt[:, :], [r("tt")], [r("W")], PAR["wd"])
+        else:
+            for c in range(NC):
+                ps = bank()
+                psum(ps, c, [], (), "tt")
+                evac(ch("W", c), r(ps, 0, CH))
+        tl = "Tr" if PAR["wd"] else "Tl"
+        cuts = PAR["cuts"]
+        for lo, hi in zip(cuts, cuts[1:]):
+            gather(r("gx", 128 * lo, 128 * hi), r("W", 0, V), r(inv, 8 * lo, 8 * hi), sign=-1)
+            gather(r("gy", 128 * lo, 128 * hi), r("W", 0, V), r(inv, 128 + 8 * lo, 128 + 8 * hi), sign=1)
+            if hi == 16 and more:
+                mm([[T.ps7[:, 0:128], T.I[:, :], T[more][:, :], False, False, 128]], [r(more), r("I")], [r("ps7", 0, 128)])
+            mm([[T.ps7[:, 0:128], T[tl][:, 16 - k:144 - k], T[x][:, 128 * k:128 * k + 128], k == 0 and x == "gx", k == 15 and x == "gy", 128]
+                for k in range(lo, hi) for x in ("gx", "gy")], [r("gx", 128 * lo, 128 * hi), r("gy", 128 * lo, 128 * hi), r(tl)], [r("ps7", 0, 128)])
+
+    def above(out):
+        def fn(g, e):
+            if e == "v":
+                return g.vector.tensor_scalar(ap(out), T.ps7[:, 0:128], 0.25, None, A.is_gt)
+            return g.scalar.activation(ap(out), T.ps7[:, 0:128], AF.Sign)
+        return op("vs", fn, [r("ps7", 0, 128)], [out], cst(128))
+
+    def marks(f, between):
+        level("inv2", None)
+        tt(r("tt", 0, 128), r("ps7", 0, 128), r("ws1", 0, 128), A.mult, 1.0)
+        above(r("mo%d" % f, 0, 128))
+        send([("mo%d" % f, 1, "mi%d" % f)], BIG // 16)
+        between()
+        level("inv1", "mi%d" % f)
+
+    outs = {"first": True}
+
+    def add_out(b):
+        for hf in range(2):
+            lo = 1024 * hf
+            first = outs["first"]
+            dma("y" if first else "g", T.gain[:, lo:lo + 1024], T[b][:, lo:lo + 1024], [r(b, lo, lo + 1024)], [r("gain", lo, lo + 1024)], BIG, not first)
+        outs["first"] = False
+
+    def small(ps, plus, minus=()):
+        mats = [[T[ps][:, 0:128], T.I[:, :], T[x][:, :], False, False, 128] for x in plus]
+        mats += [[T[ps][:, 0:128], T.nI[:, :], T[x][:, :], False, False, 128] for x in minus]
+        mats[0][3] = True
+        mats[-1][4] = True
+        return mm(mats, [r(x) for x in list(plus) + list(minus)] + [r("I"), r("nI")], [r(ps, 0, 128)])
+
+    def wide(b, c, off=0):
+        return (b, off + c * FW, off + (c + 1) * FW)
+
+    def woffs(b, c, off=0):
+        return (b, off + c * FW // 16, off + (c + 1) * FW // 16)
+
+    def gain0(rnd):
+        ps = fbank()
+        small(ps, ["wsA%d" % rnd], ["wsB%d" % rnd])
+        sop(r("qc", 0, 128), r(ps, 0, 128), AF.Identity, scale=0.5)
+        for c in range(NC):
+            ps = fbank()
+            psum(ps, c, [], (), "qc")
+            tt(ch("q", c), ch("dl2", c), r(ps, 0, CH), A.mult, 1.0)
+        for (d, s, x, bias) in (("dA", "XA", "J", 0.0), ("dB", "dB", "SCa", -math.log(2.0))):
+            for c in range(NC):
+                ps = fbank()
+                if d == "dA":
+                    psum(ps, c, [ch(s, c), ch("q", c)])
+                else:
+                    psum(ps, c, [ch(s, c)], [ch("q", c)])
+                sop(ch(d, c), r(ps, 0, CH), AF.Abs)
+            for c in range(V // FW):
+                sop(wide(x, c), wide(d, c), AF.Exp, bias=bias, scale=-0.125)
+            add_out(x)
+
+    def gain1():
+        ps = fbank()
+        small(ps, ["wsA0", "wsA0", "wsB0", "wsA1", "wsA1", "wsB1"])
+        sop(r("cb", 0, 128), r(ps, 0, 128), AF.Identity, bias=1.5, scale=0.25)
+        sop(r("ca", 0, 128), r(ps, 0, 128), AF.Identity, bias=1.5, scale=-0.25)
+        for (x, t) in (("SCb", "ca"), ("eb", "cb")):
+            for c in range(NC):
+                ps = fbank()
+                psum(ps, c, [], (), t)
+                tt(ch(x, c), ch(x, c), r(ps, 0, CH), A.mult, 1.0)
+            add_out(x)
+
+    fill = list(PAR["fe"])
+
+    def pick(dst, sel):
+        e = fill.pop(0)
+        for c in range(V // FW):
+            gather(wide(dst, c), r("SS1", 0, 2 * V), woffs(sel, c), e)
+
+    def follow(dst, src, lst):
+        e = fill.pop(0)
+        for c in range(V // FW):
+            gather(wide(dst, c), r(src, 0, V), woffs(lst, c), e)
+
+    for rnd in range(2):
+        e0, e1, e2 = ("E0", "E1", "E2") if rnd == 0 else ("E0n", "E1", "E2")
+        if rnd == 0:
+            step("XA", "u1", "DD1", PAR["s1"], "selA", "P1", e1, "ws1")
+        else:
+            step("E0n", "u1", "NQ", PAR["s1"], "selA", "P1", e1, "ws1")
+        if rnd == 0:
+            for k in range(2):
+                for c in range(NC):
+                    if c in PAR["nq"]:
+                        gather(ch("d" + "AB"[k], c), r("E0", 0, V), offs("u1", c, 128 * k))
+                        ps = fbank()
+                        psum(ps, c, [ch("d" + "AB"[k], c)], [ch("CC", c, k * V)])
+                        evac(ch("NQ", c, k * V), r(ps, 0, CH))
+                    else:
+                        gfuse(ch("NQ", c, k * V), r("E0", 0, V), offs("u1", c, 128 * k), ch("CC", c, k * V), A.subtract)
+            for c in range(V // FW):
+                sop(wide("SCb", c), wide("DD2", c), AF.Exp, scale=-0.125)
+                sop(wide("eb", c), wide("DD2", c, V), AF.Exp, scale=-0.125)
+        else:
+            follow("dB", "p0s", "lB")
+            gain0(0)
+        last_step(True, e2, "wsA%d" % rnd, "lA")
+        marks(2 * rnd, lambda: None)
+        above(r("ent", 0, 128))
+        for c in range(NC):
+            ps = bank()
+            psum(ps, c, [ch(e0, c)], (), "ent", "B6", True)
+            evac(ch("Fo%d" % rnd, c), r(ps, 0, CH))
+        sop(r("ent3", 0, 128), r("ent", 0, 128), AF.Identity, scale=3.0)
+        send([("Fo%d" % rnd, -1, "E1")], BIG)
+        pick("hm", "selA")
+        follow("XA", "hm", "lA")
+        step("Fo%d" % rnd, "u1", "NQ", PAR["s1"], "selB", "P1", "E1", "ws1")
+        pick("p0s", "selB")
+        last_step(False, None, "wsB%d" % rnd, "lB")
+        if rnd == 0:
+            marks(1, lambda: None)
+        else:
+            marks(3, lambda: (gain1(), follow("dB", "p0s", "lB"), gain0(1)))
+        ts(r("s2", 0, 128), r("ps7", 0, 128), 0.25, -3.0, A.is_gt, A.mult)
+        tt(r("dm", 0, 128), r("s2", 0, 128), r("ent3", 0, 128), A.add)
+        for c in range(NC):
+            ps = bank()
+            psum(ps, c, [ch(e0, c)], (), "dm", "Bc", True)
+            if rnd == 0 and c in PAR["clip"]:
+                sop(ch("t0", c), r(ps, 0, CH), AF.Relu)
+                ts(ch("E0n", c), ch("t0", c), 63.0, None, A.min, k=0.5)
+            elif rnd == 0:
+                ts(ch("E0n", c), r(ps, 0, CH), 0.0, 63.0, A.max, A.min)
+            else:
+                ts(ch("to", c), r(ps, 0, CH), 0.0, 63.0, A.max, A.min)
+                dma("y", T.tollout[:, c * CH:(c + 1) * CH], T.to[:, c * CH:(c + 1) * CH], [ch("to", c)], [ch("tollout", c)], BIG // 2)
+        if rnd == 0:
+            send([("E0n", -1, "E1"), ("E0n", -2, "E2")], BIG)
+    return ops
+
+
+def schedule(ops):
+    if "shift" not in PAR:
+        rng = np.random.default_rng(1)
+        best = np.zeros(len(ops))
+        tb = schedule1(ops, best)[1]
+        for k in range(PAR["tries"]):
+            x = best + rng.normal(0.0, PAR["sigma"], len(ops)) * (rng.random(len(ops)) < 0.05)
+            t = schedule1(ops, x)[1]
+            if t <= tb:
+                best, tb = x, t
+        PAR["shift"] = best
+    return schedule1(ops, PAR["shift"])
+
+
+def schedule1(ops, shift):
+    n = len(ops)
+    succ = [[] for _ in ops]
+    for o in ops:
+        for d in o["deps"]:
+            succ[d].append(o["i"])
+    pr = [0.0] * n
+    for o in reversed(ops):
+        i = o["i"]
+        pr[i] = o["cost"] + o["lat"] + max([pr[s] + LAT for s in succ[i]] + [0.0])
+    pr = [p + float(x) for p, x in zip(pr, shift)]
+    left = [len(o["deps"]) for o in ops]
+    ready = [o["i"] for o in ops if not o["deps"]]
+    free = {"v": 0.0, "s": 0.0, "p": 0.0, "g": 0.0, "y": 0.0}
+    fin = [0.0] * n
+    at = [0.0] * n
+    order = []
+    while ready:
+        best = []
+        for i in ready:
+            e = ops[i]["eng"]
+            if e is None:
+                best = [(at[i], i, None)]
+                break
+            for x in e:
+                best.append((max(at[i], free[x]), i, x))
+        t0 = min(b[0] for b in best)
+        st, i, e = max([b for b in best if b[0] <= t0 + PAR["eps"]], key=lambda b: (pr[b[1]], -b[0], b[2] == "s"))
+        soon = [b for b in best if b[2] == e and pr[b[1]] > pr[i] + PAR["gap"] and b[0] < st + PAR["ahead"] * ops[i]["cost"]]
+        if soon:
+            st, i, e = max(soon, key=lambda b: pr[b[1]] - b[0])
+        o = ops[i]
+        o["e"] = e
+        o["t"] = st
+        if e:
+            free[e] = st + o["cost"]
+        fin[i] = st + o["cost"] + o["lat"]
+        order.append(i)
+        ready.remove(i)
+        for s in succ[i]:
+            same = ops[s]["eng"] == e and e == "p"
+            at[s] = max(at[s], fin[i] + (0.0 if same else LAT))
+            left[s] -= 1
+            if left[s] == 0:
+                ready.append(s)
+    return order, max(fin)
+
+
+def rank_program(g, core, T, topo):
+    if T.rank_of(core) is None:
+        return
+    ops = build(T, topo, core)
+    order, total = schedule(ops)
+    Q = {"v": g.vector, "s": g.scalar, "p": g.tensor, "g": g, "y": g.sync}
+    pos = {i: k for k, i in enumerate(order)}
+    seen = {e: {} for e in Q}
+    need = set()
+    waits = {}
+    for i in order:
+        o = ops[i]
+        e = o["e"]
+        if e is None:
+            continue
+        w = []
+        top = {}
+        for d, hard in o["deps"].items():
+            p = ops[d]
+            if p["kind"] in "da":
+                if d not in seen[e]:
+                    seen[e][d] = True
+                    w.append(d)
+            elif p["kind"] == "x":
+                if p["inc"]:
+                    raise ValueError("a buffer that is being sent is written again")
+            elif p["e"] != e or (hard and e != "p"):
+                if p["e"] not in top or pos[d] > pos[top[p["e"]]]:
+                    top[p["e"]] = d
+        for x, d in top.items():
+            if pos[d] > seen[e].get(x, -1):
+                seen[e][x] = pos[d]
+                w.append(d)
+                need.add(d)
+        waits[i] = w
+    count = {e: 0 for e in Q}
+    val = {}
+    sent = 0
+    for i in order:
+        o = ops[i]
+        e = o["e"]
+        if e is None:
+            continue
+        for d in waits[i]:
+            p = ops[d]
+            if p["kind"] == "d":
+                Q[e].wait_ge(T.sem[p["sem"]], 16)
+            elif p["kind"] == "a":
+                Q[e].wait_ge(T.sem[p["sem"]], p["val"])
+            else:
+                Q[e].wait_ge(T.sem["e" + p["e"]], val[d])
+        ins = o["fn"](g, e)
+        if o["kind"] == "d":
+            ins.then_inc(T.sem[o["sem"]], 16)
+        elif o["kind"] == "x":
+            sent += o["inc"]
+        elif i in need:
+            count[e] += 1
+            val[i] = count[e]
+            ins.then_inc(T.sem["e" + e], 1)
+    g.wait_ge(T.sem.sent, sent)
+    for o in ops:
+        if o["kind"] == "d":
+            g.wait_ge(T.sem[o["sem"]], 16)
+        elif o["kind"] == "a":
+            g.wait_ge(T.sem[o["sem"]], o["val"])

@@ -1,70 +1,80 @@
 import math
 import numpy as np
 from concourse.bass import DstId, RemoteDMATransfer
-from concourse.mybir import AluOpType as A, ActivationFunctionType as AF, AxisListType as AX
+from concourse.mybir import AluOpType as A, ActivationFunctionType as AF
 
 V = 2048
 CH = 512
-NC = V // CH
-CENTER = 240.0
+CENTER = 220.0
+STEEP = 8192.0
+OFF = 8.5 * STEEP
 BF, F32, I32, U16, F16 = "bfloat16", "float32", "int32", "uint16", "float16"
 
 SCRATCH = {}
-for _n in ("h", "hm", "p0s", "E0", "E1", "E2", "E0n", "dl", "dl2", "XA", "Fo0", "Fo1", "U", "B6",
-           "P1", "W", "gx", "gy", "q", "dA", "dB", "Bc", "t0", "t1"):
+for _n in ("h", "hm", "p0s", "E0", "E0n", "O1", "O2", "nU", "ndb", "nsa", "dd1", "dd2", "dl2", "P1", "T2", "IND1",
+           "W2", "W1a", "W1b", "gx", "gy", "Bc", "B6", "Bw", "fA", "fB", "q", "t0", "t1"):
     SCRATCH[_n] = ("sbuf", [128, V], BF)
-for _n in ("NQ", "DD", "SS1", "DD1", "DD2", "CC"):
+for _n in ("SS", "DD", "SS1", "DD2", "YA", "YB"):
     SCRATCH[_n] = ("sbuf", [128, 2 * V], BF)
-SCRATCH["IND"] = ("sbuf", [128, 3, V], BF)
-for _n in ("cx", "cy"):
-    SCRATCH[_n] = ("sbuf", [128, V], F16)
-for _n in ("J", "SCa", "SCb", "eb", "to", "Ub"):
+SCRATCH["IND"] = ("sbuf", [128, 3 * V], BF)
+for _n in ("J", "SCa", "SCb", "eb"):
     SCRATCH[_n] = ("sbuf", [128, V], F32)
 for _n in ("tab", "tab1", "tab2"):
     SCRATCH[_n] = ("sbuf", [128, 384], I32)
-for _n in ("u0", "u1", "u2", "inv", "inv1", "inv2"):
-    SCRATCH[_n] = ("sbuf", [128, 256], U16)
-for _n in ("sel0", "selA", "selB", "lA", "lB"):
+for _n in ("u0", "u1", "u2"):
+    SCRATCH[_n] = ("sbuf", [128, 512], U16)
+for _n in ("sel", "selA", "selB", "lA", "lB"):
     SCRATCH[_n] = ("sbuf", [128, 128], U16)
-for _n in ("I", "nI", "Msh", "ones", "s1", "s2", "tt", "wr", "ws1", "wsA0", "wsB0", "wsA1", "wsB1", "qc", "cb", "ca", "ent", "ent3", "Mt", "dm",
+for _n in ("I", "nI", "ones", "s2", "ws1", "wsA0", "nsB0", "wsA1", "nsB1", "kp", "qc", "ent0", "ent1", "eni0", "eni1", "ent3", "dm",
            "mo0", "mo1", "mo2", "mo3", "mi0", "mi1", "mi2", "mi3"):
     SCRATCH[_n] = ("sbuf", [128, 128], BF)
-SCRATCH["b3"] = ("sbuf", [128, 384], BF)
-SCRATCH["nz"] = ("sbuf", [128, 128], F16)
-SCRATCH["Tl"] = ("sbuf", [128, 160], BF)
-SCRATCH["T2"] = ("sbuf", [128, 160], BF)
-SCRATCH["Tr"] = ("sbuf", [128, 160], BF)
+SCRATCH["MM"] = ("sbuf", [128, 768], BF)
+SCRATCH["TS"] = ("sbuf", [128, 640], BF)
+SCRATCH["zt"] = ("sbuf", [128, 128], F16)
+for _n in ("Tl", "T2w", "TN"):
+    SCRATCH[_n] = ("sbuf", [128, 160], BF)
 SCRATCH["Tf"] = ("sbuf", [128, 160], F32)
-SCRATCH["g8"] = ("sbuf", [128, 16], BF)
-for _n in ("io16", "ioL", "f1", "f2", "f3", "f4", "a2f", "dab"):
+SCRATCH["g8"] = ("sbuf", [128, 32], BF)
+for _n in ("io16", "ioL", "f1A", "f1B", "f2", "f3", "f4", "f5", "a2f", "dab", "Ap", "Bp", "Pp", "If", "nIf"):
     SCRATCH[_n] = ("sbuf", [128, 128], F32)
-SCRATCH["vf"] = ("sbuf", [128, 256], F32)
 SCRATCH["vi"] = ("sbuf", [128, 256], I32)
 SCRATCH["pi"] = ("sbuf", [128, 8], I32)
 SCRATCH["pm"] = ("sbuf", [128, 8], I32)
 SCRATCH["pf"] = ("sbuf", [128, 8], F32)
-for _k in range(8):
-    SCRATCH["ps%d" % _k] = ("psum", [128, CH], F32)
+SCRATCH["PS"] = ("psum", [128, 8 * CH], F32)
 
-SEMAPHORES = ["ev", "es", "ep", "eg", "sent", "left"] + ["d%d" % _k for _k in range(40)] + ["r%d" % _k for _k in range(30)]
+SEMAPHORES = ["ev", "es", "ep", "eg", "sent"] + ["d%d" % _k for _k in range(40)] + ["r%d" % _k for _k in range(50)]
 
 CYC, PCY, GA, SC, LAT = 1.0, 0.5, 1.56, 3.8, 120.0
-FW = 512
-PAR = {"fe": ("vs",) * 8, "cuts": (0, 4, 8, 12, 16), "clip": (0, 2), "wd": 0, "gap": 2000.0, "ahead": 0.5, "o1": (3, 2, 1, 0), "oA": (0, 1, 2, 3), "oB": (0, 2, 1, 3), "u": 0, "vs": 1, "ss": (3,), "nq": (), "s1": (3,), "sel": (2, 3), "s2A": (), "s2B": (2, 3), "s0": (3,), "eps": 300.0, "tries": 0, "sigma": 3000.0}
-PAR.update({"wd": 0, "u": 1, "vs": 1, "nq": (3,), "s0": (3,), "ss": (3,), "s1": (3,), "sel": (2, 3), "o1": (0, 1, 2, 3), "oB": (2, 0, 3, 1),
-            "s2B": (2, 3), "gap": 2000.0, "ahead": 0.4, "eps": 300.0, "cuts": (0, 5, 10, 14, 16), "clip": (0, 2),
-            "fe": ("s", "vs", "vs", "vs", "vs", "s", "s", "vs")})
+PAR = {"moves": 30000, "heat": 100.0, "flips": 0.15, "far": 0.6, "passes": 100, "shake": (100.0, 500.0, 2000.0), "span": 3000.0, "part": 0.3,
+       "lean": 100.0, "tilt": (-1e9, 100.0, 100.0, 600.0, 1e9, 1e9), "flip": 0.3, "slack": 300.0, "fit": 1e9, "seed": 1,
+       "ss": "4v4v4v4s", "s0": "4v4v4v4s", "sel0": "4s4v4s4v",
+       "t1": ("8v4s4s",) * 4, "i1": "8v8v", "sel": ("8v4s4v",) * 4, "r2": ("4V4M4V4M",) * 2, "t2": ("8v4v4s",) * 2, "i2": "8v8v",
+       "c2": "4x4x4x4x", "w1": "4x4x4x4x", "c1": "5x5x4x2x", "y": "4x4x4x4x", "clip": "4s4v4s4v", "out": "4v4v4v4v",
+       "fg": "8x8x", "fp": "8x8x", "fe": "8s8s", "terms": "ddvv", "fold": 1, "dm": 1, "halves": 2}
+
+
+def pieces(s):
+    out, at, k = [], 0, ""
+    for x in s:
+        if x.isdigit():
+            k += x
+        else:
+            out.append((at, at + 128 * int(k), x))
+            at, k = at + 128 * int(k), ""
+    return out
 
 
 def build(T, topo, core):
     ops = []
     acc = {}
-    cnt = {"d": 0, "r": 0, "ps": 0, "pf": 0}
+    cnt = {"d": 0, "r": 0, "ps": 0}
     rank = T.rank_of(core)
     n = len(T.cores)
 
     def op(eng, fn, R, Wr, cost, kind="c", lat=0.0, extra=()):
-        o = {"i": len(ops), "eng": eng, "fn": fn, "cost": cost, "kind": kind, "lat": lat, "deps": {}, "W": Wr}
+        on = [(e, cost[e] if isinstance(cost, dict) else cost) for e in eng or ""]
+        o = {"i": len(ops), "eng": eng, "fn": fn, "on": on, "kind": kind, "lat": lat, "deps": {}, "R": R, "W": Wr}
         for e in extra:
             o["deps"][e["i"]] = True
         for lst, isw in ((R, False), (Wr, True)):
@@ -88,20 +98,22 @@ def build(T, topo, core):
     def r(b, lo=0, hi=1 << 20):
         return (b, lo, hi)
 
+    def w(b, lo=0, hi=V, off=0):
+        return (b, off + lo, off + hi)
+
+    def sm(b):
+        return (b, 0, 128)
+
     def ap(x):
         b, lo, hi = x
+        if b.startswith("ps"):
+            at = CH * PAR["banks"][b]
+            return T.PS[:, at + lo:at + hi]
         return T[b][:, lo:hi]
 
-    def ch(b, c, off=0):
-        return (b, off + c * CH, off + (c + 1) * CH)
-
-    def bank():
+    def bank(width=CH):
         cnt["ps"] += 1
-        return "ps%d" % (cnt["ps"] % 4)
-
-    def fbank():
-        cnt["pf"] += 1
-        return "ps%d" % (4 + cnt["pf"] % 2)
+        return "ps%d#%d" % (1 if width <= CH else 2, cnt["ps"])
 
     def cst(nel, k=1.0):
         return 60.0 + max(64.0, nel * k) * CYC
@@ -123,76 +135,101 @@ def build(T, topo, core):
     def cp(out, src):
         return vop(lambda v: v.tensor_copy(ap(out), ap(src)), [src], [out], out[2] - out[1])
 
-    def evac(out, src, eng="vs"):
+    def either(out, src, onv, func, bias=0.0, scale=1.0, eng="vs", k=1.0):
         def fn(g, e):
-            if e == "v":
+            if e == "s":
+                return g.scalar.activation(ap(out), ap(src), func, bias=bias, scale=scale)
+            if onv is None:
                 return g.vector.tensor_copy(ap(out), ap(src))
-            return g.scalar.activation(ap(out), ap(src), AF.Copy)
-        return op(eng, fn, [src], [out], cst(out[2] - out[1]))
+            if len(onv) == 2:
+                return g.vector.tensor_scalar(ap(out), ap(src), onv[0], None, onv[1])
+            return g.vector.tensor_scalar(ap(out), ap(src), onv[0], onv[1], onv[2], onv[3])
+        return op(eng, fn, [src], [out], {"v": cst(out[2] - out[1], k), "s": cst(out[2] - out[1])})
+
+    def evac(out, src, eng="vs"):
+        return either(out, src, None, AF.Copy, eng=eng)
+
+    def times(out, src, x, k=1.0):
+        return either(out, src, (x, A.mult), AF.Identity, scale=x, k=k)
+
+    def more(out, src, x, k=1.0):
+        return either(out, src, (x, A.add), AF.Identity, bias=x, k=k)
+
+    def unit(out, src):
+        return either(out, src, (-1.0, 1.0, A.max, A.min), AF.Sign)
+
+    def over0(out, src):
+        return either(out, src, (0.5, 0.5, A.is_gt, A.subtract), AF.Sign, bias=-0.5)
+
+    def marked(out, ps):
+        return either(out, sm(ps), (-5.0, A.is_gt), AF.Sign, bias=6.0)
 
     def ind(win, off):
         return ap(win).indirect(ap(off))
 
-    def offs(b, c, off=0):
-        return (b, off + c * CH // 16, off + (c + 1) * CH // 16)
+    def offs(b, lo, hi, k=0):
+        return (b, 128 * k + lo // 16, 128 * k + hi // 16)
 
-    def gather(out, win, off, eng="vs", sign=0):
+    def gather(out, win, off, eng="vs", turn=False):
         def fn(g, e):
-            if e == "v":
-                if sign:
-                    return g.vector.tensor_scalar(ap(out), ind(win, off), float(sign), 0.0, A.mult, A.max)
-                return g.vector.tensor_copy(ap(out), ind(win, off))
-            if sign:
-                return g.scalar.activation(ap(out), ind(win, off), AF.Relu, scale=float(sign))
-            return g.scalar.activation(ap(out), ind(win, off), AF.Copy)
-        return op(eng, fn, [win, off], [out], cst(out[2] - out[1], GA))
+            if e == "s":
+                return g.scalar.activation(ap(out), ind(win, off), AF.Identity if turn else AF.Copy, scale=-1.0 if turn else 1.0)
+            if turn:
+                return g.vector.tensor_scalar(ap(out), ind(win, off), -1.0, None, A.mult)
+            return g.vector.tensor_copy(ap(out), ind(win, off))
+        o = op(eng, fn, [win, off], [out], cst(out[2] - out[1], GA))
+        o["ga"] = out[2] - out[1]
+        return o
 
-    def gfuse(out, win, off, other, o):
-        return vop(lambda v: v.tensor_tensor(ap(out), ind(win, off), ap(other), o), [win, off, other], [out], out[2] - out[1], GA)
+    def gfuse(out, win, off, other, how):
+        o = vop(lambda v: v.tensor_tensor(ap(out), ind(win, off), ap(other), how), [win, off, other], [out], out[2] - out[1], GA)
+        o["ga"] = out[2] - out[1]
+        return o
 
     def mm(mats, R, Wr):
         def fn(g, e):
             last = None
             for (o, l, x, st, sp, nn) in mats:
-                last = g.tensor.matmul(o, l, x, st, sp)
+                last = g.tensor.matmul(ap(o), l[0]() if isinstance(l, list) else l, x, st, sp)
             return last
         return op("p", fn, R, Wr, sum(max(64, m[5]) * PCY + 10.0 for m in mats))
 
-    def psum(ps, c, plus, minus=(), table=None, bc="Bc", late=False):
-        mats = [[T[ps][:, :], T.I[:, :], ap(x), False, False, CH] for x in plus]
-        mats += [[T[ps][:, :], T.nI[:, :], ap(x), False, False, CH] for x in minus]
-        alone = not mats
-        R = list(plus) + list(minus) + [r("I"), r("nI")]
-        if not alone:
-            mats[0][3] = True
-        if late:
-            mm(mats, R, [r(ps, 0, CH)])
+    def slide(b, i, off=0):
+        return (b, off + 16 - i, off + 144 - i)
+
+    def psum(ps, lo, hi, plus=(), minus=(), tables=(), by=(), start=True, stop=True, k=1):
+        full = [(sm("I"), x) for x in plus] + [(sm("nI"), x) for x in minus] + list(by)
+        for a in range(0, hi - lo, CH):
+            b = min(a + CH, hi - lo)
             mats, R = [], []
-        if table:
-            R += [r(table), r(bc)]
-            for k in range(CH // 128):
-                qq = c * (CH // 128) + k
-                mats.append([T[ps][:, 128 * k:128 * k + 128], T[bc][:, 128 * qq:128 * qq + 128], T[table][:, :], alone, alone, 128])
-        mats[-1][4] = True
-        return mm(mats, R, [r(ps, 0, CH)])
+            for (l, x) in full:
+                x = (x[0], x[1] + a, x[1] + b)
+                mats.append([(ps, a, b), l if isinstance(l, list) else ap(l), ap(x), False, False, (b - a) * k])
+                R += [x] + ([r("Tl"), r("T2w")] if isinstance(l, list) else [l])
+            alone = start and stop and not mats
+            for j in range(a, b, 128):
+                for t, (bc, table) in enumerate(tables):
+                    R += [sm(table), r(bc)]
+                    mats.append([(ps, j, j + 128), T[bc][:, lo + j:lo + j + 128], T[table][:, :], alone and t == 0, alone and t == len(tables) - 1, 128])
+            mats[0][3] = start
+            if stop:
+                mats[-1][4] = True
+            mm(mats, R, [(ps, a, b)])
 
-    def tolist(ps, col, src, row, hf, tl="Tl"):
-        x = T[src]
-        mats = []
-        for i in range(16):
-            s = slice(1024 * hf + i, 1024 * hf + 1024, 16)
-            mats.append([T[ps][:, col + 64 * hf:col + 64 * hf + 64], T[tl][:, 16 - i:144 - i], x[:, row, s], i == 0, i == 15, 64])
-        return mm(mats, [r(src, row * V + 1024 * hf, row * V + 1024 * hf + 1024), r(tl)], [r(ps, col + 64 * hf, col + 64 * hf + 64)])
+    def tolist(ps, src, lo, hi, tl, to=0):
+        out = (ps, lo // 16, hi // 16)
+        mats = [[out, ap(slide(tl, i, to)), T[src][:, lo + i:hi:16], i == 0, i == 15, (hi - lo) // 16] for i in range(16)]
+        return mm(mats, [r(src, lo, hi), r(tl)], [out])
 
-    def toblock(ps, srcs, c, rows, last, R, tl="Tl", first=0):
-        mats = []
-        for k in range(CH // 128):
-            qq = c * (CH // 128) + k
-            for s in srcs:
-                mats.append([T[ps][:, 0:128 * rows], T[tl][:, 16 - qq:144 - qq], s(128 * qq, 128 * qq + 128), False, False, 128 * rows])
-        mats[0][3] = c == first
-        mats[-1][4] = last
-        return mm(mats, R + [r(tl)], [r(ps, 0, 128 * rows)])
+    def toblock(ps, srcs, lo, hi, start, stop):
+        mats = [[sm(ps), ap(slide(tl, k // 128, to)), T[b][:, k:k + 128], False, False, 128] for k in range(lo, hi, 128) for (b, tl, to) in srcs]
+        mats[0][3] = start
+        mats[-1][4] = stop
+        return mm(mats, [r(b, lo, hi) for (b, tl, to) in srcs] + [r(tl) for (b, tl, to) in srcs], [sm(ps)])
+
+    def small(ps, terms):
+        return mm([[sm(ps), T[m][:, :], T[x][:, :], k == 0, k == len(terms) - 1, 128] for k, (m, x) in enumerate(terms)],
+                  [sm(x) for t in terms for x in t], [sm(ps)])
 
     def dma(eng, out, src, R, Wr, nbytes, add=False):
         s = "d%d" % cnt["d"]
@@ -207,445 +244,678 @@ def build(T, topo, core):
         o["sem"] = s
         return o
 
-    def send(items, nbytes, loc="sent"):
+    def rsem():
+        cnt["r"] += 1
+        return "r%d" % cnt["r"]
+
+    def send(items, nbytes, again=False):
         trs = []
-        for k, (src, sh, dst) in enumerate(items):
+        loc = rsem() if again else "sent"
+        for k, (srcs, sh, dst) in enumerate(items):
             to = T.cores[(rank + sh) % n]
             en = topo.engines(core, to)
             per = len(en) // len(items)
             mask = sum(1 << x for x in en[k * per:(k + 1) * per])
             rid, pid = topo.addr(to)[:2]
-            s = "r%d" % cnt["r"]
-            cnt["r"] += 1
-            trs.append((src, dst, mask, rid, pid, s, per))
+            trs.append((srcs, dst, mask, rid, pid, rsem(), per))
+
+        def one(srcs, dst, mask, rid, pid, s, per):
+            if len(srcs) == 1:
+                return RemoteDMATransfer(dst_ids=[DstId(rid=rid, pnc=pid)], dma_engine_mask=mask, remote_sem=T.sem[s], src=ap(srcs[0]), dst=ap(dst))
+            return RemoteDMATransfer(dst_ids=[DstId(rid=rid, pnc=pid)], dma_engine_mask=mask, remote_sem=T.sem[s],
+                                     srcs=[ap(x) for x in srcs], dsts=[ap(dst)], alu_op=1)
 
         def fn(g, e):
-            if len(trs) == 1:
-                src, dst, mask, rid, pid, s, per = trs[0]
-                return g.remote_dma(T[dst][:, :], T[src][:, :], T.sem[s], T.sem[loc], pid, rid, mask)
-            return g.remote_dma_fused([RemoteDMATransfer(dst_ids=[DstId(rid=rid, pnc=pid)], dma_engine_mask=mask, remote_sem=T.sem[s],
-                                                         src=T[src][:, :], dst=T[dst][:, :])
-                                       for (src, dst, mask, rid, pid, s, per) in trs], local_sem=T.sem[loc])
-        o = op("g", fn, [r(x[0]) for x in trs], [], 800.0, "x")
-        o["inc"] = sum(x[6] for x in trs)
-        if loc != "sent":
-            a = op(None, None, [r(x[0]) for x in trs], [], 0.0, "a", 2500.0 + nbytes * len(trs) / 250.0, extra=[o])
-            a["sem"] = loc
-            a["val"] = o["inc"]
-            o["inc"] = 0
-        for x in trs:
-            a = op(None, None, [], [r(x[1])], 0.0, "a", 2500.0 + nbytes * len(trs) / 250.0, extra=[o])
-            a["sem"] = x[5]
-            a["val"] = x[6]
+            if len(trs) == 1 and len(trs[0][0]) == 1:
+                srcs, dst, mask, rid, pid, s, per = trs[0]
+                return g.remote_dma(ap(dst), ap(srcs[0]), T.sem[s], T.sem[loc], pid, rid, mask)
+            return g.remote_dma_fused([one(*x) for x in trs], local_sem=T.sem[loc])
+        srcs = [y for x in trs for y in x[0]]
+        o = op("g", fn, srcs, [], 800.0, "x")
+        o["inc"] = 0 if again else sum(x[6] for x in trs)
+        for (R, Wr, s, val) in [([], [x[1]], x[5], x[6]) for x in trs] + ([(srcs, [], loc, sum(x[6] for x in trs))] if again else []):
+            a = op(None, None, R, Wr, 0.0, "a", 2500.0 + nbytes * len(srcs) / 250.0, extra=[o])
+            a["sem"] = s
+            a["val"] = val
 
     def gop(fn, R, Wr, nel):
         return op("g", lambda g, e: fn(g), R, Wr, 170.0 + 2.0 * nel * CYC)
+
+    def fill(b, hi, val):
+        return vop(lambda v: v.memset(T[b][:, 0:hi], val), [], [r(b)], hi, 0.5)
 
     BIG = 128 * V * 2
     dma("y", T.h[:, :], T.hf[:, :], [], [r("h")], BIG)
     dma("s", T.tab[:, 0:128], T.sa[:, :], [], [r("tab", 0, 128)], BIG // 8)
     dma("s", T.tab[:, 128:256], T.sb[:, :], [], [r("tab", 128, 256)], BIG // 8)
     dma("s", T.tab[:, 256:384], T.lim[:, :], [], [r("tab", 256, 384)], BIG // 8)
-    dma("y", T.E0[:, :], T.toll[:, :], [], [r("E0")], BIG)
     dma("y", T.p0s[:, :], T.p0[:, :], [], [r("p0s")], BIG)
+    dma("y", T.E0[:, :], T.toll[:, :], [], [r("E0")], BIG)
     for lo in (0, 1024):
         gop(lambda g, lo=lo: g.iota(T.J[:, lo:lo + 1024], [[1, 1024]], 32 + lo, 0, allow_small_or_imprecise_dtypes=True), [], [r("J", lo, lo + 1024)], 1024)
-    send([("h", 1, "hm")], BIG)
-    send([("tab", -1, "tab1"), ("tab", -2, "tab2")], BIG // 3)
-    send([("E0", -1, "E1"), ("E0", -2, "E2")], BIG)
-    vop(lambda v: v.memset(T.ones[:, :], 1.0), [], [r("ones")], 64)
-    vop(lambda v: v.memset(T.Tl[:, :], 0.0), [], [r("Tl")], 80)
-    vop(lambda v: v.memset(T.Bc[:, :], 1.0), [], [r("Bc")], V, 0.5)
+    send([([w("h")], 1, w("hm"))], BIG, True)
+    send([([w("tab", 0, 384)], -1, w("tab1", 0, 384)), ([w("tab", 0, 384)], -2, w("tab2", 0, 384))], BIG // 3)
+    fill("ones", 128, 1.0)
+    fill("Tl", 160, 0.0)
+    fill("Bc", V, 1.0)
+    fill("MM", 768, 0.0)
+    fill("TS", 640, 0.0)
     gop(lambda g: g.affine_select(T.I[:, :], T.ones[:, :], [[-1, 128]], A.is_equal, 0.0, 0, 1), [r("ones")], [r("I")], 128)
+    for (b, val) in (("nI", -1.0), ("If", 1.0 / 12), ("nIf", -1.0)):
+        gop(lambda g, b=b, val=val: g.affine_select(T[b][:, :], T.I[:, :], [[-1, 128]], A.not_equal, val, 0, 1), [r("I")], [r(b)], 128)
     gop(lambda g: g.affine_select(T.g8[:, 0:8], T.ones[:, 0:8], [[-16, 8]], A.is_ge, 0.0, 0, 1), [r("ones")], [r("g8", 0, 8)], 8)
     gop(lambda g: g.affine_select(T.g8[:, 8:16], T.g8[:, 0:8], [[16, 8]], A.is_ge, 0.0, 15, -1), [r("g8", 0, 8)], [r("g8", 8, 16)], 8)
+    gop(lambda g: g.affine_select(T.Tl[:, 16:144:16], T.g8[:, 8:16], [[0, 8]], A.is_ge, 0.0, 0, 0), [r("g8", 8, 16)], [r("Tl")], 8)
     gop(lambda g: g.iota(T.pi[:, 0:1], [[0, 1]], 0, 1), [], [r("pi")], 1)
     gop(lambda g: g.iota(T.io16[:, :], [[16, 128]], 0, 0, allow_small_or_imprecise_dtypes=True), [], [r("io16")], 128)
-    gop(lambda g: g.affine_select(T.Bc[:, :], T.Bc[:, :], [[-1, 16], [-16, 8], [0, 16]], A.is_equal, 0.0, 0, 1), [r("Bc")], [r("Bc")], V)
-    vop(lambda v: v.tensor_copy(T.Tl[:, 16:144:16], T.g8[:, 8:16]), [r("g8")], [r("Tl")], 8)
-    ts(r("Tf", 0, 160), r("Tl", 0, 160), 1.0 / 16, None, A.mult)
-    ts(r("nI", 0, 128), r("I", 0, 128), -1.0, None, A.mult)
-    ts(r("T2", 0, 160), r("Tl", 0, 160), 2.0, None, A.mult)
-    if PAR["wd"]:
-        vop(lambda v: v.memset(T.W[:, :], 0.0), [], [r("W")], V, 0.5)
-        vop(lambda v: v.tensor_reduce(T.pf[:, 4:5], T.I[:, 0:128:18], AX.X, A.add), [r("I")], [r("pf", 4, 5)], 8)
-        vop(lambda v: v.tensor_scalar(T.Tr[:, :], T.Tl[:, :], T.pf[:, 4:5], None, A.mult), [r("Tl"), r("pf", 4, 5)], [r("Tr")], 160)
-    vop(lambda v: v.memset(T.B6[:, :], 6.0), [], [r("B6")], V, 0.5)
-    for hf in range(4):
-        lo, hi = 512 * hf, 512 * hf + 512
-        for (cmp, fill, base) in ((A.is_equal, 0.0, 0), (A.not_equal, 5.0, -16), (A.not_equal, 5.0, 112)):
-            gop(lambda g, lo=lo, hi=hi, cmp=cmp, fill=fill, base=base - 4 * hf:
-                g.affine_select(T.B6[:, lo:hi], T.B6[:, lo:hi], [[-1, 4], [-16, 8], [0, 16]], cmp, fill, base, 1), [r("B6", lo, hi)], [r("B6", lo, hi)], 512)
-    ts(r("pm", 0, 1), r("pi", 0, 1), 15, None, A.bitwise_and)
-    cp(r("pf", 0, 1), r("pm", 0, 1))
-    vop(lambda v: v.tensor_scalar(T.ioL[:, :], T.io16[:, :], T.pf[:, 0:1], None, A.add), [r("io16"), r("pf", 0, 1)], [r("ioL")], 128)
-    cp(r("u0", 0, 256), r("tab", 0, 256))
+    for (b, x) in (("Tf", 1.0 / 16), ("T2w", 2.0), ("TN", -STEEP)):
+        times(w(b, 0, 160), w("Tl", 0, 160), x)
+    times(w("g8", 16, 24), w("g8", 8, 16), -2.0)
+    for (b, src, cmp, val, base) in (("Bc", "Bc", A.is_equal, 0.0, 0), ("B6", "Bc", A.not_equal, 6.0, 0),
+                                     ("B6", "B6", A.not_equal, 5.0, -16), ("B6", "B6", A.not_equal, 5.0, 112)):
+        for hf in range(4):
+            lo, hi = 512 * hf, 512 * hf + 512
+            gop(lambda g, b=b, src=src, lo=lo, hi=hi, cmp=cmp, val=val, base=base - 4 * hf:
+                g.affine_select(T[b][:, lo:hi], T[src][:, lo:hi], [[-1, 4], [-16, 8], [0, 16]], cmp, val, base, 1), [r(src, lo, hi)], [r(b, lo, hi)], 512)
+    for k, val in enumerate((-16.0, 16.0, 0.0, 0.0)):
+        gop(lambda g, k=k, val=val: g.affine_select(T.Bw[:, k:V:4], T.Bc[:, k:V:4], [[-1, 16], [-16, 8], [0, 4]], A.not_equal, val, 0, 1),
+            [r("Bc")], [r("Bw")], 512)
+    for (m, i, width, j, val) in ((0, 1, 4, 0, 16.0), (0, 0, 4, 0, -16.0), (0, 2, 1, 10, 16.0), (0, 0, 1, 10, 16.0), (0, 11, 16, 0, 24.0), (0, 11, 1, 11, -1.0),
+                                  (0, 11, 1, 0, 15.0), (0, 11, 1, 4, 15.0), (0, 11, 1, 1, 49.0), (0, 11, 1, 5, 49.0),
+                                  (1, 2, 4, 1, 16.0), (1, 0, 4, 1, 16.0), (1, 1, 1, 14, 16.0), (1, 0, 1, 14, -16.0),
+                                  (4, 2, 4, 0, 16.0), (4, 10, 4, 0, 16.0), (4, 6, 4, 1, 16.0), (4, 14, 4, 1, 16.0),
+                                  (4, 11, 2, 0, 1.0), (4, 11, 2, 1, 17.0), (4, 11, 2, 2, -33.0), (4, 11, 2, 3, -17.0)):
+        x = w("MM", 128 * m, 128 * m + 128)
+        gop(lambda g, x=x, i=i, width=width, j=j, val=val:
+            g.affine_select(ap(x), ap(x), [[-16, 8], [200, 16 // width], [0, width]], A.not_equal, val, -i - 200 * j, 1), [x], [x], 128)
+    for (m, j, src) in ([(m, j, T.g8[:, 16:24]) for (m, j) in ((2, 0), (2, 1), (2, 2), (5, 0), (5, 4))] +
+                        [(m, j, T.T2w[:, 16:144:16]) for (m, j) in ((3, 4), (3, 5), (3, 6), (5, 1), (5, 5))]):
+        x = w("MM", 128 * m, 128 * m + 128)
+        gop(lambda g, m=m, j=j, src=src: g.affine_select(T.MM[:, 128 * m + j:128 * m + 128:16], src, [[0, 8]], A.is_ge, 0.0, 0, 0),
+            [r("g8"), r("T2w")], [x], 8)
+    for (m, i) in ((0, 0), (0, 4), (1, 1), (1, 5), (2, 2), (2, 6), (3, 0)):
+        x = w("TS", 160 * m, 160 * m + 160)
+        gop(lambda g, m=m, i=i: g.affine_select(T.TS[:, 160 * m + 16:160 * m + 144:16], T.TS[:, 160 * m + 16:160 * m + 144:16], [[-16, 8]], A.not_equal, 1.0, -i, 1),
+            [x], [x], 8)
+    ts(w("pm", 0, 1), w("pi", 0, 1), 15, None, A.bitwise_and)
+    cp(w("pf", 0, 1), w("pm", 0, 1))
+    ts(w("pf", 1, 2), w("pf", 0, 1), 1.0, 16.0, A.is_equal, A.mult)
+    more(w("pf", 2, 3), w("pf", 1, 2), -17.0)
+    op("s", lambda g, e: g.scalar.activation(T.ioL[:, :], T.io16[:, :], AF.Identity, bias=T.pf[:, 0:1]), [r("io16"), r("pf", 0, 1)], [r("ioL")], cst(128))
+    more(sm("Ap"), sm("ioL"), V - OFF)
+    more(sm("Pp"), sm("ioL"), -OFF)
+    cp(w("u0", 0, 256), w("tab", 0, 256))
     for hf in range(2):
         lo = 1024 * hf
         vop(lambda v, lo=lo: v.tensor_copy(T.SCa[:, :].indirect(T.u0[:, lo // 16:lo // 16 + 64]), T.J[:, lo:lo + 1024]),
-            [r("J", lo, lo + 1024), r("u0")], [r("SCa")], 1024, SC)
+            [r("J", lo, lo + 1024), r("u0", 0, 128)], [r("SCa")], 1024, SC)
         op("s", lambda g, e, lo=lo: g.scalar.activation(T.SCb[:, :].indirect(T.u0[:, 128 + lo // 16:128 + lo // 16 + 64]), T.J[:, lo:lo + 1024], AF.Silu),
-           [r("J", lo, lo + 1024), r("u0")], [r("SCb")], cst(1024, SC) + (1300.0 if hf == 0 else 0.0))
-    for c in range(2):
-        ts(r("p0s", 1024 * c, 1024 * c + 1024), r("p0s", 1024 * c, 1024 * c + 1024), -CENTER, None, A.add, k=0.5)
+           [r("J", lo, lo + 1024), r("u0", 128, 256)], [r("SCb")], cst(1024, SC) + (1300.0 if hf == 0 else 0.0))
+    for lo in (0, 1024):
+        more(w("p0s", lo, lo + 1024), w("p0s", lo, lo + 1024), -CENTER, 0.5)
+    ps = bank()
     for k, b in enumerate(("SCa", "SCb")):
         for i in range(16):
-            mm([[T.ps5[:, 128 * k:128 * k + 128], T.Tf[:, 16 - i:144 - i], T[b][:, i:V:16], i == 0, i == 15, 512]],
-               [r(b), r("Tf")], [r("ps5", 128 * k, 128 * k + 128)])
-    sop(r("vf", 0, 256), r("ps5", 0, 256), AF.Identity, bias=-32.0)
-    cp(r("vi", 0, 256), r("vf", 0, 256))
-    cp(r("inv", 0, 256), r("vi", 0, 256))
-    send([("inv", -1, "inv1"), ("inv", -2, "inv2")], BIG // 8)
-    cp(r("u1", 0, 256), r("tab1", 0, 256))
-    cp(r("u2", 0, 256), r("tab2", 0, 256))
-    ts(r("nz", 0, 128), r("tab2", 256, 384), -1.0, CENTER, A.mult, A.add)
-    tt(r("f3", 0, 128), r("tab2", 128, 256), r("tab2", 0, 128), A.subtract)
-    sop(r("dab", 0, 128), r("f3", 0, 128), AF.Identity, scale=0.5)
-    tt(r("a2f", 0, 128), r("tab2", 0, 128), r("dab", 0, 128), A.add)
-    for c in range(NC):
+            mm([[(ps, 128 * k, 128 * k + 128), T.Tf[:, 16 - i:144 - i], T[b][:, i:V:16], i == 0, i == 15, 512]],
+               [r(b), r("Tf")], [r(ps, 128 * k, 128 * k + 128)])
+    ts(w("vi", 0, 256), w(ps, 0, 256), -32.0, None, A.add)
+    cp(w("u0", 256, 512), w("vi", 0, 256))
+    send([([w("u0", 0, 512)], -1, w("u1", 0, 512)), ([w("u0", 0, 512)], -2, w("u2", 0, 512))], BIG // 4)
+    ts(sm("Bp"), w("tab1", 128, 256), -OFF, None, A.add)
+    ts(sm("zt"), w("tab2", 256, 384), -CENTER, None, A.add)
+    tt(sm("f3"), w("tab2", 128, 256), w("tab2", 0, 128), A.subtract)
+    times(sm("dab"), sm("f3"), 0.5)
+    tt(sm("a2f"), w("tab2", 0, 128), sm("dab"), A.add)
+    for (lo, hi, way) in pieces(PAR["ss"]):
         for k in range(2):
-            if c in PAR["ss"]:
-                gather(ch("t%d" % k, c), r("hm", 0, V), offs("u0", c, 128 * k), "s")
-                ps = bank()
-                psum(ps, c, [ch("t%d" % k, c)], [ch("h", c)])
-                sop(ch("DD", c, k * V), r(ps, 0, CH), AF.Abs)
-                evac(ch("NQ", c, k * V), r(ps, 0, CH), "s")
+            s, d = w("SS", lo, hi, V - k * V), w("DD", lo, hi, k * V)
+            if way == "s":
+                gather(w("t%d" % k, lo, hi), w("hm"), offs("u0", lo, hi, k), "s")
+                ps = bank(hi - lo)
+                psum(ps, lo, hi, [w("t%d" % k, lo, hi)], [w("h", lo, hi)])
+                sop(d, w(ps, 0, hi - lo), AF.Abs)
+                evac(s, w(ps, 0, hi - lo), "s")
             else:
-                gfuse(ch("NQ", c, k * V), r("hm", 0, V), offs("u0", c, 128 * k), ch("h", c), A.subtract)
-                sop(ch("DD", c, k * V), ch("NQ", c, k * V), AF.Abs)
-    send([("DD", -1, "DD1")], 2 * BIG)
+                gfuse(s, w("hm"), offs("u0", lo, hi, k), w("h", lo, hi), A.subtract)
+                sop(d, s, AF.Abs)
+    for lo in (0, 1024):
+        times(w("ndb", lo, lo + 1024), w("DD", lo, lo + 1024, V), -1.0, 0.5)
+    send([([w("DD"), w("ndb")], -1, w("dd1"))], BIG, True)
+    send([([w("E0"), w("DD", 0, V, V)], -1, w("O1"))], BIG)
+    send([([w("DD"), w("ndb")], -2, w("dd2"))], BIG, True)
+    send([([w("E0"), w("DD", 0, V, V)], -2, w("O2"))], BIG)
 
-    def add_gather(out, win, off, other, c, share, tmp, neg=False):
-        if c not in share:
-            return gfuse(out, win, off, other, A.subtract if neg else A.add)
-        gather(ch(tmp, c), win, off, "s")
+    def add_gather(out, win, off, other, lo, hi, way, tmp, eng="vs"):
+        if way == "v":
+            return gfuse(out, win, off, other, A.add)
+        gather(w(tmp, lo, hi), win, off, "s")
+        ps = bank(hi - lo)
+        psum(ps, lo, hi, [w(tmp, lo, hi), other])
+        return evac(out, w(ps, 0, hi - lo), eng)
+
+    for (lo, hi, way) in pieces(PAR["s0"]):
+        for k in range(2):
+            add_gather(w("YB", lo, hi, k * V), w("p0s"), offs("u0", lo, hi, k), w("DD", lo, hi, k * V), lo, hi, way, "t%d" % k)
+        ps = bank(hi - lo)
+        psum(ps, lo, hi, [w("YB", lo, hi)], [w("YB", lo, hi, V)])
+        sop(w("IND", lo, hi), w(ps, 0, hi - lo), AF.Sign, bias=-0.5)
+    for lo in (0, 64):
         ps = bank()
-        if neg:
-            psum(ps, c, [ch(tmp, c)], [other])
-        else:
-            psum(ps, c, [ch(tmp, c), other])
-        return evac(out, r(ps, 0, CH), "s")
+        tolist(ps, "IND", 16 * lo, 16 * lo + 1024, "Tl")
+        ts(w("f4", lo, lo + 64), w(ps, lo, lo + 64), 1.0, float(V), A.is_gt, A.mult)
+        tt(w("f2", lo, lo + 64), w("f4", lo, lo + 64), w("ioL", lo, lo + 64), A.add)
+        cp(w("sel", lo, lo + 64), w("f2", lo, lo + 64))
+    for (lo, hi, way) in pieces(PAR["sel0"]):
+        add_gather(w("YA", lo, hi), w("YB", 0, 2 * V), offs("sel", lo, hi), w("E0", lo, hi), lo, hi, way, "t0")
+    for lo in (0, 1024):
+        times(w("nsa", lo, lo + 1024), w("SS", lo, lo + 1024, V), -1.0, 0.5)
+    send([([w("SS", 0, 2 * V)], -1, w("SS1", 0, 2 * V))], 2 * BIG)
+    send([([w("DD", 0, 2 * V)], -2, w("DD2", 0, 2 * V))], 2 * BIG)
+    send([([w("SS"), w("nsa")], -2, w("dl2"))], BIG, True)
+    if PAR["fold"]:
+        for (lo, hi, way) in pieces(PAR["fp"]):
+            ps = bank(hi - lo)
+            psum(ps, lo, hi, [w("DD", lo, hi, V), w("E0", lo, hi)], [w("YA", lo, hi)])
+            evac(w("h", lo, hi), w(ps, 0, hi - lo))
 
-    def step(win, u, dd, share, sel, nxt, add, ws):
-        for c in share:
-            for k in range(2):
-                add_gather(ch("CC", c, k * V), r(win, 0, V), offs(u, c, 128 * k), ch(dd, c, k * V), c, share, "t%d" % k, dd == "NQ")
-        seen = []
-        for c in PAR["o1"]:
-            seen.append(c)
-            for k in range(2):
-                if c not in share:
-                    add_gather(ch("CC", c, k * V), r(win, 0, V), offs(u, c, 128 * k), ch(dd, c, k * V), c, share, "t%d" % k, dd == "NQ")
+    def step1(f, Y, O):
+        f1 = "f1" + "AB"[f % 2]
+        for (lo, hi, way) in pieces(PAR["t1"][f]):
+            add_gather(w(Y, lo, hi, V), w(Y), offs("u1", lo, hi), w("dd1", lo, hi), lo, hi, way, "t0")
+        for (lo, hi, way) in pieces(PAR["i1"]):
+            gfuse(w("IND1", lo, hi), w(Y), offs("u1", lo, hi, 1), w(Y, lo, hi, V), A.is_lt)
+        for lo in (0, 64):
             ps = bank()
-            psum(ps, c, [ch("CC", c)], [ch("CC", c, V)])
-            op("s", lambda g, e, ps=ps, c=c: g.scalar.activation(T.IND[:, 0, c * CH:(c + 1) * CH], T[ps][:, :], AF.Sign, bias=-0.5),
-               [r(ps, 0, CH)], [ch("IND", c)], cst(CH))
-            if c ^ 1 in seen:
-                lo = 64 * (c // 2)
-                pl = "ps%d" % (6 + c // 2)
-                tolist(pl, 0, "IND", 0, c // 2)
-                ts(r("f1", lo, lo + 64), r(pl, lo, lo + 64), 1.0, float(V), A.is_gt, A.mult)
-                tt(r("f2", lo, lo + 64), r("f1", lo, lo + 64), r("ioL", lo, lo + 64), A.add)
-                cp(r(sel, lo, lo + 64), r("f2", lo, lo + 64))
-        if ws:
-            for c in range(NC):
-                toblock("ps7", [lambda a, b: T.IND[:, 0, a:b]], c, 1, c == NC - 1, [ch("IND", c)])
-            sop(r(ws, 0, 128), r("ps7", 0, 128), AF.Sign, bias=-1.0)
-        for c in PAR["o1"]:
-            add_gather(ch(nxt, c), r("CC", 0, 2 * V), offs(sel, c), ch(add, c), c, PAR["sel"], "t0")
+            tolist(ps, "IND1", 16 * lo, 16 * lo + 1024, "TN")
+            tt(w(f1, lo, lo + 64), w(ps, lo, lo + 64), w("Ap", lo, lo + 64), A.min, 1.0)
+            tt(w("f2", lo, lo + 64), w(f1, lo, lo + 64), w("Bp", lo, lo + 64), A.max)
+            ts(w("sel", lo, lo + 64), w("f2", lo, lo + 64), OFF, None, A.add)
+        if f % 2:
+            ps = bank()
+            toblock(ps, [("IND1", "Tl", 0)], 0, V, True, True)
+            sop(sm("ws1"), sm(ps), AF.Sign, bias=-8.5)
+        for (lo, hi, way) in pieces(PAR["sel"][f]):
+            add_gather(w("P1", lo, hi), w(Y, 0, V + (1024 if hi <= 1024 else V)), offs("sel", lo, hi), w(O, lo, hi), lo, hi, way, "t1")
+        tt(sm("f5"), sm(f1), sm("Pp"), A.max)
+        ts(sm("sel" + "AB"[f % 2]), sm("f5"), OFF, None, A.add)
 
-    step("p0s", "u0", "DD", PAR["s0"], "sel0", "XA", "E0", None)
-    for c in range(NC):
-        ps = fbank()
-        psum(ps, c, [ch("NQ", c, V)], [ch("NQ", c)])
-        evac(ch("dl", c), r(ps, 0, CH))
-    send([("DD", -2, "DD2"), ("NQ", -1, "SS1")], 2 * BIG, "left")
-    send([("dl", -2, "dl2")], BIG)
+    def bound():
+        for (lo, hi, way) in pieces(PAR["fp"]):
+            ps = bank(hi - lo)
+            psum(ps, lo, hi, (), [w("O2", lo, hi)], [("Bc", "zt")])
+            evac(w("nU", lo, hi), w(ps, 0, hi - lo))
 
-    def last_step(first, e2, ws, lst):
-        share = PAR["s2A" if first else "s2B"]
-        rows = 3 if first else 1
-        if first and PAR["u"] == 2:
-            for c in range(NC):
-                for k in range(2):
-                    ps = fbank()
-                    psum(ps, c, [ch(e2, c), ch("DD2", c, k * V)], (), "nz")
-                    evac(ch(("to", "Ub")[k], c), r(ps, 0, CH))
-        if first and PAR["u"] == 1:
-            for c in range(NC):
-                ps = fbank()
-                psum(ps, c, [ch(e2, c)], (), "nz")
-                ts(ch("U", c), r(ps, 0, CH), -256.0, 241.0, A.max, A.min)
-        onv = (not first) and PAR["vs"]
-        order = PAR["oA" if first else "oB"]
-        for c in order:
-            cs = []
-            for k in range(2):
-                o = ch(("gx", "gy")[k], c)
-                if first and PAR["u"] == 2:
-                    o = ch(("cx", "cy")[k], c)
-                    gfuse(o, r("P1", 0, V), offs("u2", c, 128 * k), ch(("to", "Ub")[k], c), A.add)
-                    cs.append([o])
-                elif c in share:
-                    gather(o, r("P1", 0, V), offs("u2", c, 128 * k), "s")
-                    cs.append([o, ch("DD2", c, k * V)])
-                else:
-                    gfuse(o, r("P1", 0, V), offs("u2", c, 128 * k), ch("DD2", c, k * V), A.add)
-                    cs.append([o])
-            for j in range(rows):
-                ps = bank()
-                if j == 0:
-                    psum(ps, c, cs[0], cs[1])
-                elif PAR["u"] == 2:
-                    psum(ps, c, cs[j - 1])
-                elif PAR["u"]:
-                    psum(ps, c, cs[j - 1] + [ch("U", c)])
-                else:
-                    psum(ps, c, cs[j - 1] + [ch(e2, c)], (), "nz")
-                if onv and c < 2:
-                    vop(lambda v, ps=ps, c=c: v.tensor_scalar(T.IND[:, 0, c * CH:(c + 1) * CH], T[ps][:, :], 0.5, 0.5, A.is_gt, A.subtract),
-                        [r(ps, 0, CH)], [ch("IND", c)], CH)
-                else:
-                    op("s", lambda g, e, ps=ps, c=c, j=j: g.scalar.activation(T.IND[:, j, c * CH:(c + 1) * CH], T[ps][:, :], AF.Sign, bias=-0.5),
-                       [r(ps, 0, CH)], [ch("IND", c, j * V)], cst(CH))
-            if first:
-                toblock("ps7", [lambda a, b: T.IND[:, :, a:b]], c, 3, c == order[-1], [ch("IND", c, j * V) for j in range(3)], "Tl", order[0])
+    def step2a(rnd):
+        for (lo, hi, way) in pieces(PAR["r2"][rnd]):
+            a, b, u = offs("u2", lo, hi), offs("u2", lo, hi, 1), w("nU", lo, hi)
+            if way == "S":
+                gather(w("t0", lo, hi), w("P1"), a, "s")
+                t = [w("t0", lo, hi), w("dd2", lo, hi)]
             else:
-                toblock("ps7", [lambda a, b: T.IND[:, 0, a:b]], c, 1, c == order[-1], [ch("IND", c)], "T2" if onv and c < 2 else "Tl", order[0])
-        if first:
-            ts(r("b3", 0, 384), r("ps7", 0, 384), 1.0, None, A.is_gt)
-            tt(r("s1", 0, 128), r("b3", 128, 256), r("b3", 256, 384), A.add)
-            tt(r("s2", 0, 128), r("s1", 0, 128), r("b3", 0, 128), A.mult)
-            tt(r("tt", 0, 128), r("s2", 0, 128), r("b3", 128, 256), A.subtract)
-            sop(r("wr", 0, 128), r("tt", 0, 128), AF.Abs)
-            sop(r(ws, 0, 128), r("b3", 0, 128), AF.Identity, bias=-1.0, scale=2.0)
-        else:
-            sop(r(ws, 0, 128), r("ps7", 0, 128), AF.Sign, bias=-1.0)
-            tt(r("tt", 0, 128), r(ws, 0, 128), r("wr", 0, 128), A.mult)
-        for hf in range(2):
-            tolist("ps6", 0, "IND", 0, hf, "T2" if onv and hf == 0 else "Tl")
-        sop(r("f3", 0, 128), r("ps6", 0, 128), AF.Sign, bias=-1.0)
-        tt(r("f4", 0, 128), r("f3", 0, 128), r("dab", 0, 128), A.mult)
-        tt(r("f3", 0, 128), r("f4", 0, 128), r("a2f", 0, 128), A.add)
-        cp(r(lst, 0, 128), r("f3", 0, 128))
+                gfuse(w("T2", lo, hi), w("P1"), a, w("dd2", lo, hi), A.add)
+                t = [w("T2", lo, hi)]
+            by = []
+            if way == "V":
+                gfuse(w("IND", lo, hi), w("P1"), b, t[0], A.is_lt)
+                gfuse(w("IND", lo, hi, 2 * V), w("P1"), b, u, A.is_gt)
+                by = [(slide("T2w", j), w("IND", lo, hi, j * V)) for j in (0, 2)]
+                rows = [(1, t, [u])]
+            else:
+                y = w("t1", lo, hi)
+                gather(y, w("P1"), b)
+                rows = [(1, t, [u]), (0, t, [y]), (2, [y], [u])]
+            for (j, plus, minus) in rows:
+                ps = bank(hi - lo)
+                psum(ps, lo, hi, plus, minus)
+                o = over0(w("IND", lo, hi, j * V), w(ps, 0, hi - lo))
+                by.append(([lambda o=o, j=j: ap(slide("T2w" if o["e"] == "v" else "Tl", j))], w("IND", lo, hi, j * V)))
+            ps = bank(hi - lo)
+            psum(ps, lo, hi, by=by)
+            out, src = w("W2", lo, hi), w(ps, 0, hi - lo)
+            op("s", lambda g, e, out=out, src=src, way=way: g.scalar.activation(ap(out), ap(src), AF.Sign, bias=T.pf[:, 2:3] if way == "V" else -1.0),
+               [src, w("pf", 2, 3)], [out], cst(hi - lo))
 
-    def level(inv, more):
-        if PAR["wd"]:
-            dma("y", T.W[0:128:18, :], T.tt[:, :], [r("tt")], [r("W")], PAR["wd"])
-        else:
-            for c in range(NC):
-                ps = bank()
-                psum(ps, c, [], (), "tt")
-                evac(ch("W", c), r(ps, 0, CH))
-        tl = "Tr" if PAR["wd"] else "Tl"
-        cuts = PAR["cuts"]
-        for lo, hi in zip(cuts, cuts[1:]):
-            gather(r("gx", 128 * lo, 128 * hi), r("W", 0, V), r(inv, 8 * lo, 8 * hi), sign=-1)
-            gather(r("gy", 128 * lo, 128 * hi), r("W", 0, V), r(inv, 128 + 8 * lo, 128 + 8 * hi), sign=1)
-            if hi == 16 and more:
-                mm([[T.ps7[:, 0:128], T.I[:, :], T[more][:, :], False, False, 128]], [r(more), r("I")], [r("ps7", 0, 128)])
-            mm([[T.ps7[:, 0:128], T[tl][:, 16 - k:144 - k], T[x][:, 128 * k:128 * k + 128], k == 0 and x == "gx", k == 15 and x == "gy", 128]
-                for k in range(lo, hi) for x in ("gx", "gy")], [r("gx", 128 * lo, 128 * hi), r("gy", 128 * lo, 128 * hi), r(tl)], [r("ps7", 0, 128)])
+    def step2b(rnd):
+        for (lo, hi, way) in pieces(PAR["t2"][rnd]):
+            add_gather(w("T2", lo, hi), w("P1"), offs("u2", lo, hi), w("dd2", lo, hi), lo, hi, way, "t0")
+        for (lo, hi, way) in pieces(PAR["i2"]):
+            gfuse(w("IND", lo, hi), w("P1"), offs("u2", lo, hi, 1), w("T2", lo, hi), A.is_lt)
 
-    def above(out):
-        def fn(g, e):
-            if e == "v":
-                return g.vector.tensor_scalar(ap(out), T.ps7[:, 0:128], 0.25, None, A.is_gt)
-            return g.scalar.activation(ap(out), T.ps7[:, 0:128], AF.Sign)
-        return op("vs", fn, [r("ps7", 0, 128)], [out], cst(128))
+    def mx(m):
+        return w("MM", 128 * m, 128 * m + 128)
 
-    def marks(f, between):
-        level("inv2", None)
-        tt(r("tt", 0, 128), r("ps7", 0, 128), r("ws1", 0, 128), A.mult, 1.0)
-        above(r("mo%d" % f, 0, 128))
-        send([("mo%d" % f, 1, "mi%d" % f)], BIG // 16)
+    def back(f, between):
+        first = f % 2 == 0
+        src, W1 = ("W2", "W1a") if first else ("IND", "W1b")
+        cut = pieces(PAR["w1"])
+        banks = [bank(hi - lo) for (lo, hi, way) in cut]
+        out, own = bank(), bank()
+        for ps, (lo, hi, way) in zip(banks, cut):
+            if first:
+                psum(ps, lo, hi, by=[(mx(5), w("IND1", lo, hi))], stop=False)
+            else:
+                psum(ps, lo, hi, tables=[("Bw", "ws1")], by=[(mx(4), w("W1a", lo, hi))], stop=False)
+        for (lo, hi, way) in pieces(PAR["c2"]):
+            gather(w("gx", lo, hi), w(src), offs("u2", lo, hi, 2))
+            gather(w("gy", lo, hi), w(src), offs("u2", lo, hi, 3))
+        for ps, (lo, hi, way) in zip(banks, cut):
+            psum(ps, lo, hi, start=False,
+                 by=[(mx(0 if first else 2), w("gx", lo, hi)), (mx(1 if first else 3), w("gy", lo, hi))])
+            unit(w(W1, lo, hi), w(ps, 0, hi - lo))
+            toblock(out, [(W1, "TS", 320)], lo, hi, lo == 0, hi == V)
+        evac(sm("mo%d" % f), sm(out))
+        send([([sm("mo%d" % f)], 1, sm("mi%d" % f))], BIG // 16)
         between()
-        level("inv1", "mi%d" % f)
+        for (lo, hi, way) in pieces(PAR["c1"]):
+            gather(w("gx", lo, hi), w(W1), offs("u1", lo, hi, 2))
+            gather(w("gy", lo, hi), w(W1), offs("u1", lo, hi, 3))
+            if hi == V:
+                mm([[sm(own), T.I[:, :], T["mi%d" % f][:, :], False, False, 128]], [sm("mi%d" % f), r("I")], [sm(own)])
+            toblock(own, [("gx", "TS", 0), ("gy", "TS", 160)], lo, hi, lo == 0, hi == V)
+        return own
 
     outs = {"first": True}
 
     def add_out(b):
-        for hf in range(2):
-            lo = 1024 * hf
+        for lo in (0, 1024):
             first = outs["first"]
             dma("y" if first else "g", T.gain[:, lo:lo + 1024], T[b][:, lo:lo + 1024], [r(b, lo, lo + 1024)], [r("gain", lo, lo + 1024)], BIG, not first)
         outs["first"] = False
 
-    def small(ps, plus, minus=()):
-        mats = [[T[ps][:, 0:128], T.I[:, :], T[x][:, :], False, False, 128] for x in plus]
-        mats += [[T[ps][:, 0:128], T.nI[:, :], T[x][:, :], False, False, 128] for x in minus]
-        mats[0][3] = True
-        mats[-1][4] = True
-        return mm(mats, [r(x) for x in list(plus) + list(minus)] + [r("I"), r("nI")], [r(ps, 0, 128)])
+    def swap(rnd):
+        ps = bank()
+        small(ps, [("I", "wsA%d" % rnd), ("I", "nsB%d" % rnd)])
+        times(sm("qc"), sm(ps), 0.5)
+        for (lo, hi, way) in pieces(PAR["fp"]):
+            ps = bank(hi - lo)
+            psum(ps, lo, hi, tables=[("Bc", "qc")])
+            tt(w("q", lo, hi), w("dl2", lo, hi), w(ps, 0, hi - lo), A.mult, 1.0)
 
-    def wide(b, c, off=0):
-        return (b, off + c * FW, off + (c + 1) * FW)
+    ways = list(PAR["terms"])
 
-    def woffs(b, c, off=0):
-        return (b, off + c * FW // 16, off + (c + 1) * FW // 16)
+    def follow(d, way):
+        src, lst = ("hm", "lA") if d == "fA" else ("p0s", "lB")
+        for (lo, hi, x) in pieces(PAR["fg"]):
+            if way in "vV":
+                gfuse(w(d, lo, hi), w(src), offs(lst, lo, hi), w("q", lo, hi), A.add if d == "fA" else A.subtract)
+            else:
+                gather(w(d, lo, hi), w(src), offs(lst, lo, hi), turn=way in "dD" and d == "fB")
 
-    def gain0(rnd):
-        ps = fbank()
-        small(ps, ["wsA%d" % rnd], ["wsB%d" % rnd])
-        sop(r("qc", 0, 128), r(ps, 0, 128), AF.Identity, scale=0.5)
-        for c in range(NC):
-            ps = fbank()
-            psum(ps, c, [], (), "qc")
-            tt(ch("q", c), ch("dl2", c), r(ps, 0, CH), A.mult, 1.0)
-        for (d, s, x, bias) in (("dA", "XA", "J", 0.0), ("dB", "dB", "SCa", -math.log(2.0))):
-            for c in range(NC):
-                ps = fbank()
-                if d == "dA":
-                    psum(ps, c, [ch(s, c), ch("q", c)])
-                else:
-                    psum(ps, c, [ch(s, c)], [ch("q", c)])
-                sop(ch(d, c), r(ps, 0, CH), AF.Abs)
-            for c in range(V // FW):
-                sop(wide(x, c), wide(d, c), AF.Exp, bias=bias, scale=-0.125)
-            add_out(x)
+    def term(d, way):
+        x, bias, tmp = ("J", 0.0, "ndb") if d == "fA" else ("SCa", -math.log(2.0), "nsa")
+        if way in "dD":
+            dma("g", T[d][:, :], T.q[:, :], [w("q")], [w(d)], BIG, True)
+        for (lo, hi, y) in pieces(PAR["fp"]):
+            ps = bank(hi - lo)
+            if way in "DV":
+                sop(w(d, lo, hi), w(d, lo, hi), AF.Abs)
+            elif way == "p":
+                psum(ps, lo, hi, [w(d, lo, hi)] + [w("q", lo, hi)] * (d == "fA"), [w("q", lo, hi)] * (d == "fB"))
+                sop(w(d, lo, hi), w(ps, 0, hi - lo), AF.Abs)
+            else:
+                either(w(tmp, lo, hi), w(d, lo, hi), (0.0, 2.0, A.max, A.mult), AF.Relu, scale=2.0, k=0.5)
+                psum(ps, lo, hi, [w(tmp, lo, hi)], [w(d, lo, hi)])
+                sop(w(x, lo, hi), w(ps, 0, hi - lo), AF.Exp, bias=bias, scale=-0.125)
+        if way in "pDV":
+            for (lo, hi, y) in pieces(PAR["fe"]):
+                sop(w(x, lo, hi), w(d, lo, hi), AF.Exp, bias=bias, scale=-0.125)
+        add_out(x)
+
+    def edges2():
+        for (lo, hi, way) in pieces(PAR["fe"]):
+            sop(w("SCb", lo, hi), w("DD2", lo, hi), AF.Exp, bias=math.log(3.0), scale=-0.125)
+            sop(w("eb", lo, hi), w("DD2", lo, hi, V), AF.Exp, bias=-math.log(4.0), scale=-0.125)
+        add_out("SCb")
+        for (lo, hi, way) in pieces(PAR["fp"]):
+            ps = bank(hi - lo)
+            psum(ps, lo, hi, by=[(sm("If"), w("SCb", lo, hi))], k=4, stop=False)
+            psum(ps, lo, hi, by=[(sm("nIf"), w("eb", lo, hi))], k=4, start=False)
+            evac(w("eb", lo, hi), w(ps, 0, hi - lo))
 
     def gain1():
-        ps = fbank()
-        small(ps, ["wsA0", "wsA0", "wsB0", "wsA1", "wsA1", "wsB1"])
-        sop(r("cb", 0, 128), r(ps, 0, 128), AF.Identity, bias=1.5, scale=0.25)
-        sop(r("ca", 0, 128), r(ps, 0, 128), AF.Identity, bias=1.5, scale=-0.25)
-        for (x, t) in (("SCb", "ca"), ("eb", "cb")):
-            for c in range(NC):
-                ps = fbank()
-                psum(ps, c, [], (), t)
-                tt(ch(x, c), ch(x, c), r(ps, 0, CH), A.mult, 1.0)
-            add_out(x)
-
-    fill = list(PAR["fe"])
+        ps = bank()
+        small(ps, [("I", "nsB0"), ("nI", "wsA0"), ("nI", "wsA0"), ("nI", "wsA1"), ("nI", "wsA1"), ("I", "nsB1")])
+        more(sm("kp"), sm(ps), -6.0)
+        for (lo, hi, way) in pieces(PAR["fp"]):
+            ps = bank(hi - lo)
+            psum(ps, lo, hi, tables=[("Bc", "kp")])
+            tt(w("eb", lo, hi), w("eb", lo, hi), w(ps, 0, hi - lo), A.mult, 1.0)
+        add_out("eb")
 
     def pick(dst, sel):
-        e = fill.pop(0)
-        for c in range(V // FW):
-            gather(wide(dst, c), r("SS1", 0, 2 * V), woffs(sel, c), e)
+        for (lo, hi, way) in pieces(PAR["fg"]):
+            gather(w(dst, lo, hi), w("SS1", 0, 2 * V), offs(sel, lo, hi))
 
-    def follow(dst, src, lst):
-        e = fill.pop(0)
-        for c in range(V // FW):
-            gather(wide(dst, c), r(src, 0, V), woffs(lst, c), e)
+    def lists(rnd, first):
+        src, tl, to = ("W2", "TS", 480) if first else ("IND", "Tl", 0)
+        ps = bank()
+        toblock(ps, [(src, tl, to)], 0, V, True, True)
+        if first:
+            evac(sm("wsA%d" % rnd), sm(ps))
+        else:
+            sop(sm("nsB%d" % rnd), sm(ps), AF.Sign, bias=8.5, scale=-1.0)
+        ps = bank()
+        tolist(ps, src, 0, V, tl, to)
+        if first:
+            tt(sm("f4"), sm(ps), sm("dab"), A.mult, 1.0)
+        else:
+            sop(sm("f3"), sm(ps), AF.Sign, bias=-8.5)
+            tt(sm("f4"), sm("f3"), sm("dab"), A.mult)
+        tt(sm("f3"), sm("f4"), sm("a2f"), A.add)
+        cp(sm("lA" if first else "lB"), sm("f3"))
 
+    def terms(rnd):
+        a, b = ways[2 * rnd:2 * rnd + 2]
+        swap(rnd)
+        if a in "vV":
+            follow("fA", a)
+        term("fA", a)
+        follow("fB", b)
+        term("fB", b)
+
+    H = V // PAR["halves"]
     for rnd in range(2):
-        e0, e1, e2 = ("E0", "E1", "E2") if rnd == 0 else ("E0n", "E1", "E2")
-        if rnd == 0:
-            step("XA", "u1", "DD1", PAR["s1"], "selA", "P1", e1, "ws1")
-        else:
-            step("E0n", "u1", "NQ", PAR["s1"], "selA", "P1", e1, "ws1")
-        if rnd == 0:
-            for k in range(2):
-                for c in range(NC):
-                    if c in PAR["nq"]:
-                        gather(ch("d" + "AB"[k], c), r("E0", 0, V), offs("u1", c, 128 * k))
-                        ps = fbank()
-                        psum(ps, c, [ch("d" + "AB"[k], c)], [ch("CC", c, k * V)])
-                        evac(ch("NQ", c, k * V), r(ps, 0, CH))
-                    else:
-                        gfuse(ch("NQ", c, k * V), r("E0", 0, V), offs("u1", c, 128 * k), ch("CC", c, k * V), A.subtract)
-            for c in range(V // FW):
-                sop(wide("SCb", c), wide("DD2", c), AF.Exp, scale=-0.125)
-                sop(wide("eb", c), wide("DD2", c, V), AF.Exp, scale=-0.125)
-        else:
-            follow("dB", "p0s", "lB")
-            gain0(0)
-        last_step(True, e2, "wsA%d" % rnd, "lA")
-        marks(2 * rnd, lambda: None)
-        above(r("ent", 0, 128))
-        for c in range(NC):
-            ps = bank()
-            psum(ps, c, [ch(e0, c)], (), "ent", "B6", True)
-            evac(ch("Fo%d" % rnd, c), r(ps, 0, CH))
-        sop(r("ent3", 0, 128), r("ent", 0, 128), AF.Identity, scale=3.0)
-        send([("Fo%d" % rnd, -1, "E1")], BIG)
+        e0, ent, eni = ("E0", "ent0", "eni0") if rnd == 0 else ("E0n", "ent1", "eni1")
+        bound()
+        step1(2 * rnd, "YA", "O1")
+        if rnd == 1:
+            terms(0)
         pick("hm", "selA")
-        follow("XA", "hm", "lA")
-        step("Fo%d" % rnd, "u1", "NQ", PAR["s1"], "selB", "P1", "E1", "ws1")
-        pick("p0s", "selB")
-        last_step(False, None, "wsB%d" % rnd, "lB")
+        step2a(rnd)
         if rnd == 0:
-            marks(1, lambda: None)
+            edges2()
+        lists(rnd, True)
+        own = back(2 * rnd, lambda: None)
+        if ways[2 * rnd] not in "vV":
+            follow("fA", ways[2 * rnd])
+        cut = pieces(PAR["y"])
+        banks = [bank(hi - lo) for (lo, hi, way) in cut]
+        for ps, (lo, hi, way) in zip(banks, cut):
+            psum(ps, lo, hi, [w("YA", lo, hi)], stop=False)
+        marked(sm(ent), own)
+        if not PAR["fold"]:
+            send([([sm(ent)], -1, sm(eni))], BIG // 16)
+        for ps, (lo, hi, way) in zip(banks, cut):
+            psum(ps, lo, hi, tables=[("B6", ent)], start=False)
+            evac(w("YB", lo, hi), w(ps, 0, hi - lo))
+        times(sm("ent3"), sm(ent), 3.0)
+        if PAR["fold"]:
+            for lo in range(0, V, H):
+                send([([w("YB", lo, lo + H), w("h", lo, lo + H)], -1, w("nU", lo, lo + H))], BIG // PAR["halves"], rnd == 0)
         else:
-            marks(3, lambda: (gain1(), follow("dB", "p0s", "lB"), gain0(1)))
-        ts(r("s2", 0, 128), r("ps7", 0, 128), 0.25, -3.0, A.is_gt, A.mult)
-        tt(r("dm", 0, 128), r("s2", 0, 128), r("ent3", 0, 128), A.add)
-        for c in range(NC):
-            ps = bank()
-            psum(ps, c, [ch(e0, c)], (), "dm", "Bc", True)
-            if rnd == 0 and c in PAR["clip"]:
-                sop(ch("t0", c), r(ps, 0, CH), AF.Relu)
-                ts(ch("E0n", c), ch("t0", c), 63.0, None, A.min, k=0.5)
+            for (lo, hi, way) in pieces(PAR["fp"]):
+                ps = bank(hi - lo)
+                psum(ps, lo, hi, [w("O1", lo, hi)], tables=[("B6", eni)])
+                evac(w("nU", lo, hi), w(ps, 0, hi - lo))
+        step1(2 * rnd + 1, "YB", "nU")
+        pick("p0s", "selB")
+        step2b(rnd)
+        lists(rnd, False)
+        own = back(2 * rnd + 1, (lambda: None) if rnd == 0 else lambda: (gain1(), terms(1)))
+        cut = pieces(PAR["clip" if rnd == 0 else "out"])
+        banks = [bank(hi - lo) for (lo, hi, way) in cut]
+        for ps, (lo, hi, way) in zip(banks, cut):
+            psum(ps, lo, hi, [w(e0, lo, hi)], tables=[] if PAR["dm"] else [("Bc", "ent3")], stop=False)
+        ts(sm("s2"), sm(own), -5.0, -3.0, A.is_gt, A.mult)
+        if PAR["dm"]:
+            tt(sm("dm"), sm("s2"), sm("ent3"), A.add)
+        for ps, (lo, hi, way) in zip(banks, cut):
+            psum(ps, lo, hi, tables=[("Bc", "dm" if PAR["dm"] else "s2")], start=False)
+            if rnd == 0 and way == "s":
+                sop(w("t0", lo, hi), w(ps, 0, hi - lo), AF.Relu)
+                ts(w("E0n", lo, hi), w("t0", lo, hi), 63.0, None, A.min, k=0.5)
             elif rnd == 0:
-                ts(ch("E0n", c), r(ps, 0, CH), 0.0, 63.0, A.max, A.min)
+                ts(w("E0n", lo, hi), w(ps, 0, hi - lo), 0.0, 63.0, A.max, A.min)
             else:
-                ts(ch("to", c), r(ps, 0, CH), 0.0, 63.0, A.max, A.min)
-                dma("y", T.tollout[:, c * CH:(c + 1) * CH], T.to[:, c * CH:(c + 1) * CH], [ch("to", c)], [ch("tollout", c)], BIG // 2)
+                ts(w("SCb", lo, hi), w(ps, 0, hi - lo), 0.0, 63.0, A.max, A.min)
+                dma("y", T.tollout[:, lo:hi], T.SCb[:, lo:hi], [w("SCb", lo, hi)], [w("tollout", lo, hi)], 512 * (hi - lo))
         if rnd == 0:
-            send([("E0n", -1, "E1"), ("E0n", -2, "E2")], BIG)
+            for (lo, hi, way) in pieces(PAR["y"]):
+                ps = bank(hi - lo)
+                psum(ps, lo, hi, [w("YA", lo, hi)], [w("E0", lo, hi)], stop=False)
+                psum(ps, lo, hi, [w("E0n", lo, hi)], start=False)
+                evac(w("YA", lo, hi), w(ps, 0, hi - lo))
+            for lo in range(0, V, H):
+                send([([w("E0n", lo, lo + H), w("DD", lo, lo + H, V)], -1, w("O1", lo, lo + H))], BIG // PAR["halves"])
+            send([([w("E0n"), w("DD", 0, V, V)], -2, w("O2"))], BIG)
     return ops
 
 
-def schedule(ops):
-    if "shift" not in PAR:
-        rng = np.random.default_rng(1)
-        best = np.zeros(len(ops))
-        tb = schedule1(ops, best)[1]
-        for k in range(PAR["tries"]):
-            x = best + rng.normal(0.0, PAR["sigma"], len(ops)) * (rng.random(len(ops)) < 0.05)
-            t = schedule1(ops, x)[1]
-            if t <= tb:
-                best, tb = x, t
-        PAR["shift"] = best
-    return schedule1(ops, PAR["shift"])
-
-
-def schedule1(ops, shift):
+def place(ops, before, after, key, back, lean):
     n = len(ops)
-    succ = [[] for _ in ops]
-    for o in ops:
-        for d in o["deps"]:
-            succ[d].append(o["i"])
-    pr = [0.0] * n
-    for o in reversed(ops):
-        i = o["i"]
-        pr[i] = o["cost"] + o["lat"] + max([pr[s] + LAT for s in succ[i]] + [0.0])
-    pr = [p + float(x) for p, x in zip(pr, shift)]
-    left = [len(o["deps"]) for o in ops]
-    ready = [o["i"] for o in ops if not o["deps"]]
-    free = {"v": 0.0, "s": 0.0, "p": 0.0, "g": 0.0, "y": 0.0}
-    fin = [0.0] * n
-    at = [0.0] * n
-    order = []
+    left = [len(x) for x in before]
+    ready = sorted((key[i], i) for i in range(n) if not left[i])
+    busy = {e: [[], []] for e in "vspgy"}
+    at, start, fin, eng = [0.0] * n, [0.0] * n, [0.0] * n, [None] * n
     while ready:
-        best = []
-        for i in ready:
-            e = ops[i]["eng"]
-            if e is None:
-                best = [(at[i], i, None)]
-                break
-            for x in e:
-                best.append((max(at[i], free[x]), i, x))
-        t0 = min(b[0] for b in best)
-        st, i, e = max([b for b in best if b[0] <= t0 + PAR["eps"]], key=lambda b: (pr[b[1]], -b[0], b[2] == "s"))
-        soon = [b for b in best if b[2] == e and pr[b[1]] > pr[i] + PAR["gap"] and b[0] < st + PAR["ahead"] * ops[i]["cost"]]
-        if soon:
-            st, i, e = max(soon, key=lambda b: pr[b[1]] - b[0])
+        i = ready.pop(0)[1]
         o = ops[i]
-        o["e"] = e
-        o["t"] = st
+        t0 = at[i] + o["lat"] if back else at[i]
+        t, e, end = t0, None, t0
+        for x, cost in o["on"]:
+            los, his = busy[x]
+            k = m = len(his)
+            while k and his[k - 1] > t0:
+                k -= 1
+            u = t0
+            while k < m and los[k] < u + cost:
+                if his[k] > u:
+                    u = his[k]
+                k += 1
+            if e is None or u + cost <= end + lean[i]:
+                t, e, j, end = u, x, k, u + cost
         if e:
-            free[e] = st + o["cost"]
-        fin[i] = st + o["cost"] + o["lat"]
-        order.append(i)
-        ready.remove(i)
-        for s in succ[i]:
-            same = ops[s]["eng"] == e and e == "p"
-            at[s] = max(at[s], fin[i] + (0.0 if same else LAT))
+            busy[e][0].insert(j, t)
+            busy[e][1].insert(j, end)
+        start[i], eng[i] = t, e
+        fin[i] = end = end if back else end + o["lat"]
+        for s in after[i]:
+            u = end if e == "p" and ops[s]["eng"] == "p" else end + LAT
+            if u > at[s]:
+                at[s] = u
             left[s] -= 1
             if left[s] == 0:
-                ready.append(s)
-    return order, max(fin)
+                x = (key[s], s)
+                lo, hi = 0, len(ready)
+                while lo < hi:
+                    mid = (lo + hi) // 2
+                    if ready[mid] < x:
+                        lo = mid + 1
+                    else:
+                        hi = mid
+                ready.insert(lo, x)
+    if max(left):
+        raise ValueError("the instructions wait for one another in a circle")
+    return start, fin, eng
+
+
+def polish(ops, uses, home, seq, eng, rng):
+    n = len(ops)
+    pred = [[(d, 0.0 if ops[d]["eng"] == "p" and o["eng"] == "p" else LAT) for d in o["deps"]] for o in ops]
+    succ = [set() for o in ops]
+    for o in ops:
+        for d in o["deps"]:
+            succ[d].add(o["i"])
+    cost, lat = [dict(o["on"]) for o in ops], [o["lat"] for o in ops]
+    opens = {uses[u][0]: u for u in uses}
+    shuts = {uses[u][-1]: u for u in uses}
+
+    def run(seq, eng, old=None, same=0):
+        same -= same % 32
+        if same:
+            start, fin, why, banks, marks = list(old[1]), list(old[2]), list(old[3]), dict(old[4]), old[5][:same // 32]
+            free, held, last = old[5][same // 32]
+            free, held, last = dict(free), list(held), list(last)
+        else:
+            free = {e: (0.0, -1) for e in "vspgy"}
+            start, fin, why = [0.0] * n, [0.0] * n, [-1] * n
+            held, last, banks, marks = [0.0] * 8, [None] * 8, {}, []
+        for at in range(same, n):
+            if at % 32 == 0:
+                marks.append((dict(free), list(held), list(last)))
+            i = seq[at]
+            t, y = 0.0, -1
+            for d, x in pred[i]:
+                x += fin[d]
+                if x > t:
+                    t, y = x, d
+            e = eng[i]
+            if e:
+                x, d = free[e]
+                if x > t:
+                    t, y = x, d
+                if i in opens:
+                    u = opens[i]
+                    k = int(u[2])
+                    can = [(held[b] if k == 1 else max(held[b], held[b + 1]), b) for b in range(0, 8, k)]
+                    fit = [(held[b ^ 1] > t, x, b) for x, b in can if x <= t]
+                    x, b = max(fit)[1:] if fit else min(can)
+                    if x > 1e17:
+                        return None
+                    was = [last[c] for c in range(b, b + k) if last[c]]
+                    if x > t:
+                        t, y = x, max([uses[c][-1] for c in was], key=lambda d: fin[d])
+                    banks[u] = (b, was)
+                    held[b:b + k], last[b:b + k] = [1e18] * k, [u] * k
+                x = t + cost[i][e]
+                free[e] = (x, i)
+            else:
+                x = t
+            start[i], fin[i], why[i] = t, x + lat[i], y
+            if i in shuts:
+                u = shuts[i]
+                b = banks[u][0]
+                held[b:b + int(u[2])] = [x + LAT] * int(u[2])
+        return max(fin), start, fin, why, banks, marks
+
+    now = best = run(seq, eng) + (seq, eng)
+    for k in range(PAR["moves"]):
+        if k % 100 == 99:
+            seq = sorted(now[6], key=lambda i: now[1][i])
+            got = run(seq, now[7])
+            if got is not None and got[0] <= now[0]:
+                now, fresh = got + (seq, now[7]), True
+        total, start, fin, why, banks, marks, seq, eng = now
+        if k == 0 or fresh:
+            pos = [0] * n
+            for j, i in enumerate(seq):
+                pos[i] = j
+            chain, i = [], max(range(n), key=lambda i: fin[i])
+            while why[i] >= 0:
+                if why[i] not in ops[i]["deps"] or len(cost[i]) > 1:
+                    chain.append(i)
+                i = why[i]
+        i = chain[int(rng.integers(len(chain)))]
+        p, how = why[i], rng.random()
+        if how < PAR["flips"] or p in ops[i]["deps"]:
+            x = i if len(cost[i]) > 1 and (how < PAR["flips"] / 2 or len(cost[p]) < 2) else p
+            if len(cost[x]) < 2:
+                fresh = False
+                continue
+            eng = list(eng)
+            eng[x] = "s" if eng[x] == "v" else "v"
+            a = pos[x]
+        else:
+            a, b = pos[p], pos[i]
+            if how > 1.0 - PAR["far"]:
+                a = max(0, a - int(rng.integers(12)))
+            part = seq[a:b + 1]
+            if rng.random() < 0.5:
+                need = {i}
+                for j in reversed(part):
+                    if j in need or not succ[j].isdisjoint(need):
+                        need.add(j)
+                part = [j for j in part if j in need] + [j for j in part if j not in need]
+            else:
+                part = seq[pos[p]:b + 1 + (int(rng.integers(12)) if how > 1.0 - PAR["far"] else 0)]
+                a, b = pos[p], pos[p] + len(part) - 1
+                late = {p}
+                for j in part:
+                    if not late.isdisjoint(ops[j]["deps"]):
+                        late.add(j)
+                part = [j for j in part if j not in late] + [j for j in part if j in late]
+            seq = seq[:a] + part + seq[b + 1:]
+        got = run(seq, eng, now, a)
+        fresh = got is not None and got[0] <= total - PAR["heat"] * (1.0 - k / PAR["moves"]) * math.log(rng.random() + 1e-12)
+        if fresh:
+            now = got + (seq, eng)
+            if now[0] < best[0]:
+                best = now
+    total, start, fin, why, banks, marks, seq, eng = best
+    more = {}
+    for u in banks:
+        for i in uses[u][:int(u[2])]:
+            more[i] = set(j for c in banks[u][1] for j in uses[c])
+    return total, start, fin, eng, {u: banks[u][0] for u in banks}, more
+
+
+def schedule(ops):
+    n = len(ops)
+    uses, home = {}, {}
+    for o in ops:
+        for x in o["R"] + o["W"]:
+            if x[0].startswith("ps") and o["i"] not in home:
+                uses.setdefault(x[0], []).append(o["i"])
+                home[o["i"]] = x[0]
+    short = {u: len([i for i in uses[u] if ops[i]["eng"] == "p"]) <= int(u[2]) for u in uses}
+
+    def turn(pred):
+        succ = [[] for _ in ops]
+        for i in range(n):
+            for d in pred[i]:
+                succ[d].append(i)
+        return succ
+
+    def deal(start, fin):
+        last, free, banks, more = [None] * 8, [-1.0] * 8, {}, {}
+        for u in sorted(uses, key=lambda u: start[uses[u][-1]]):
+            k = int(u[2])
+            can = [(max(free[b:b + k]), b) for b in range(0, 8, k)]
+            fit = [x for x in can if x[0] + PAR["fit"] <= start[uses[u][0]]]
+            b = max(fit)[1] if fit and short[u] else min(can)[1]
+            banks[u] = b
+            for x in range(b, b + k):
+                if last[x] is not None:
+                    for i in uses[u][:k]:
+                        more.setdefault(i, set()).update(uses[last[x]])
+                last[x], free[x] = u, fin[uses[u][-1]]
+        return banks, more
+
+    if "plan" not in PAR:
+        base = [set(o["deps"]) for o in ops]
+        for i in range(n):
+            for d in ops[i]["deps"]:
+                if d in home and home[d] != home.get(i):
+                    base[i].add(uses[home[d]][-1])
+        succ = turn(base)
+        rng = np.random.default_rng(PAR["seed"])
+        lean = [PAR["lean"]] * n
+        fin = place(ops, succ, base, [-i for i in range(n)], True, lean)[1]
+        start, fin, eng = place(ops, base, succ, [-f for f in fin], False, lean)
+        best = now = None
+        for k in range(PAR["passes"]):
+            banks, more = deal(start, fin)
+            pred = [base[i] | more[i] if i in more else base[i] for i in range(n)]
+            succ = turn(pred)
+            mid, size = rng.random() * max(fin), PAR["shake"][k % len(PAR["shake"])]
+            near = (np.abs(np.array(start) - mid) < PAR["span"]) * (rng.random(n) < PAR["part"])
+            tilt = [float(x) for x in np.where(near * (rng.random(n) < PAR["flip"]), rng.choice(PAR["tilt"], n), lean)]
+            fin = place(ops, succ, pred, [float(x) for x in rng.normal(0.0, size, n) * near - np.array(fin)], True, tilt)[1]
+            start, fin, eng = place(ops, pred, succ, [-f for f in fin], False, tilt)
+            if now is None or max(fin) < now[0] + PAR["slack"] * (1.0 - k / PAR["passes"]):
+                now, lean = (max(fin), start, fin, eng, banks, more), tilt
+            if best is None or now[0] < best[0]:
+                best = now
+            start, fin = now[1:3]
+        PAR["plan"] = polish(ops, uses, home, sorted(range(n), key=lambda i: (best[1][i], i)), best[3], rng)
+    total, start, fin, eng, banks, more = PAR["plan"]
+    PAR["banks"] = banks
+    for o in ops:
+        o["t"], o["e"] = start[o["i"]], eng[o["i"]]
+        o["cost"] = dict(o["on"]).get(o["e"], 0.0)
+        for d in more.get(o["i"], ()):
+            o["deps"].setdefault(d, False)
+    return sorted(range(n), key=lambda i: (start[i], i)), total
 
 
 def rank_program(g, core, T, topo):

@@ -25,17 +25,20 @@ for _n in ("u0", "u1", "u2"):
     SCRATCH[_n] = ("sbuf", [128, 512], U16)
 for _n in ("sel", "selA", "selB", "lA", "lB"):
     SCRATCH[_n] = ("sbuf", [128, 128], U16)
-for _n in ("I", "nI", "ones", "s2", "ws1", "wsA0", "nsB0", "wsA1", "nsB1", "kp", "qc", "ent0", "ent1", "eni0", "eni1", "ent3", "dm",
+for _n in ("I", "nI", "Ik", "ones", "s1", "s2", "ws1", "wsA0", "nsB0", "wsA1", "nsB1", "kp", "qc", "ent0", "ent1", "eni0", "eni1", "ent3", "dm",
            "mo0", "mo1", "mo2", "mo3", "mi0", "mi1", "mi2", "mi3"):
     SCRATCH[_n] = ("sbuf", [128, 128], BF)
 SCRATCH["MM"] = ("sbuf", [128, 768], BF)
 SCRATCH["TS"] = ("sbuf", [128, 640], BF)
+SCRATCH["cv"] = ("sbuf", [128, 256], BF)
+SCRATCH["one5"] = ("sbuf", [128, CH], BF)
 SCRATCH["zt"] = ("sbuf", [128, 128], F16)
+SCRATCH["ioh"] = ("sbuf", [128, 128], F16)
 for _n in ("Tl", "T2w", "TN"):
     SCRATCH[_n] = ("sbuf", [128, 160], BF)
 SCRATCH["Tf"] = ("sbuf", [128, 160], F32)
 SCRATCH["g8"] = ("sbuf", [128, 32], BF)
-for _n in ("io16", "ioL", "f1A", "f1B", "f2", "f3", "f4", "f5", "a2f", "dab", "Ap", "Bp", "Pp", "If", "nIf"):
+for _n in ("io16", "ioL", "f1A", "f1B", "f2", "f3", "f4", "a2f", "dab", "Ap", "Bp"):
     SCRATCH[_n] = ("sbuf", [128, 128], F32)
 SCRATCH["vi"] = ("sbuf", [128, 256], I32)
 SCRATCH["pi"] = ("sbuf", [128, 8], I32)
@@ -45,13 +48,16 @@ SCRATCH["PS"] = ("psum", [128, 8 * CH], F32)
 
 SEMAPHORES = ["ev", "es", "ep", "eg", "sent"] + ["d%d" % _k for _k in range(40)] + ["r%d" % _k for _k in range(50)]
 
-CYC, PCY, GA, SC, LAT = 1.0, 0.5, 1.56, 3.8, 120.0
-PAR = {"moves": 30000, "heat": 100.0, "flips": 0.15, "far": 0.6, "passes": 100, "shake": (100.0, 500.0, 2000.0), "span": 3000.0, "part": 0.3,
-       "lean": 100.0, "tilt": (-1e9, 100.0, 100.0, 600.0, 1e9, 1e9), "flip": 0.3, "slack": 300.0, "fit": 1e9, "seed": 1,
-       "ss": "4v4v4v4s", "s0": "4v4v4v4s", "sel0": "4s4v4s4v",
-       "t1": ("8v4s4s",) * 4, "i1": "8v8v", "sel": ("8v4s4v",) * 4, "r2": ("4V4M4V4M",) * 2, "t2": ("8v4v4s",) * 2, "i2": "8v8v",
-       "c2": "4x4x4x4x", "w1": "4x4x4x4x", "c1": "5x5x4x2x", "y": "4x4x4x4x", "clip": "4s4v4s4v", "out": "4v4v4v4v",
-       "fg": "8x8x", "fp": "8x8x", "fe": "8s8s", "terms": "ddvv", "fold": 1, "dm": 1, "halves": 2}
+CYC, PCY, GA, SC, LAT, FAR = 1.0, 0.53, 1.35, 3.8, 200.0, 1.35
+WAITS = (PCY, GA, SC, LAT, FAR)
+SLOW = (0.5, 1.85, 3.8, 115.0, 0.9)
+PAR = {"stages": ((9000, 150.0, 1.5, WAITS, SLOW, 0.35), (75000, 130.0, 1.5, WAITS, SLOW, 0.3)), "slow": 0.5, "loose": 500.0, "blur": 1000.0, "soon": 500.0, "ways": 0.1, "rate": 400.0, "mean": 0.3, "gaps": 0.3, "room": 0.5, "wait": 20, "give": 100.0, "free": 0.5, "heat": 120.0, "flips": 0.15,
+       "far": 0.6, "passes": 100, "shake": (100.0, 500.0, 2000.0), "span": 3000.0, "part": 0.3,
+       "lean": (600.0, -200.0), "tilt": (-1e9, 100.0, 100.0, 600.0, 1e9, 1e9), "flip": 0.3, "slack": 300.0, "fit": 1e9, "seed": 14,
+       "sc": ("8v8v", "8s8s"), "ss": "4v4v8v", "s0": "8v4v4s", "sel0": "4s4v8v",
+       "t1": ("8v4s4s",) * 4, "i1": "8v4v4v", "sel": ("4s4v8v",) * 4, "r2": ("4M4M4M4V",) * 2, "t2": ("8v4s4s",) * 2, "i2": "8v8v",
+       "c2": "8x4x4x", "w1": "4x4x4x4x", "c1": "8x6x2x", "y": "4x4x4x4x", "clip": "4s4v4s4v", "out": "4s4v4v4v",
+       "fg": "8x8x", "fp": "8x8x", "fe": "8s8s", "terms": "ddpv", "fold": 1, "spare": 2000.0, "dm": 0, "halves": 4, "plain": 1, "w2": "ss", "add": "8x8x"}
 
 
 def pieces(s):
@@ -231,7 +237,7 @@ def build(T, topo, core):
         return mm([[sm(ps), T[m][:, :], T[x][:, :], k == 0, k == len(terms) - 1, 128] for k, (m, x) in enumerate(terms)],
                   [sm(x) for t in terms for x in t], [sm(ps)])
 
-    def dma(eng, out, src, R, Wr, nbytes, add=False):
+    def dma(eng, out, src, R, Wr, nbytes, add=False, spare=True):
         s = "d%d" % cnt["d"]
         cnt["d"] += 1
         if add:
@@ -240,7 +246,9 @@ def build(T, topo, core):
             fn = lambda g, e: g.sync.dma_start(out, src)
         else:
             fn = lambda g, e: g.scalar.dma_start(out, src)
-        o = op(eng, fn, R, Wr, 1000.0 if eng == "g" else 100.0, "d", 2000.0 + nbytes * (2 if add else 1) / 400.0)
+        spare = [op(None, None, R, [], 0.0, "n", PAR["spare"])] if add and spare else []
+        o = op(eng, fn, R, Wr, 1000.0 if eng == "g" else 100.0, "d", FAR * (2000.0 + nbytes * (2 if add else 1) / 600.0), extra=spare)
+        o["dq"], o["fix"] = FAR * nbytes * (2 if add else 1) / 800.0, FAR * 2000.0
         o["sem"] = s
         return o
 
@@ -273,8 +281,10 @@ def build(T, topo, core):
         srcs = [y for x in trs for y in x[0]]
         o = op("g", fn, srcs, [], 800.0, "x")
         o["inc"] = 0 if again else sum(x[6] for x in trs)
+        o["dq"] = FAR * nbytes * len(srcs) / PAR["rate"]
         for (R, Wr, s, val) in [([], [x[1]], x[5], x[6]) for x in trs] + ([(srcs, [], loc, sum(x[6] for x in trs))] if again else []):
-            a = op(None, None, R, Wr, 0.0, "a", 2500.0 + nbytes * len(srcs) / 250.0, extra=[o])
+            a = op(None, None, R, Wr, 0.0, "a", FAR * (2500.0 + nbytes * len(srcs) / 250.0), extra=[o])
+            a["fix"] = FAR * 2500.0
             a["sem"] = s
             a["val"] = val
 
@@ -289,7 +299,8 @@ def build(T, topo, core):
     dma("s", T.tab[:, 0:128], T.sa[:, :], [], [r("tab", 0, 128)], BIG // 8)
     dma("s", T.tab[:, 128:256], T.sb[:, :], [], [r("tab", 128, 256)], BIG // 8)
     dma("s", T.tab[:, 256:384], T.lim[:, :], [], [r("tab", 256, 384)], BIG // 8)
-    dma("y", T.p0s[:, :], T.p0[:, :], [], [r("p0s")], BIG)
+    fill("p0s", V, -CENTER)
+    dma("g", T.p0s[:, :], T.p0[:, :], [], [r("p0s")], BIG, True, False)
     dma("y", T.E0[:, :], T.toll[:, :], [], [r("E0")], BIG)
     for lo in (0, 1024):
         gop(lambda g, lo=lo: g.iota(T.J[:, lo:lo + 1024], [[1, 1024]], 32 + lo, 0, allow_small_or_imprecise_dtypes=True), [], [r("J", lo, lo + 1024)], 1024)
@@ -300,9 +311,13 @@ def build(T, topo, core):
     fill("Bc", V, 1.0)
     fill("MM", 768, 0.0)
     fill("TS", 640, 0.0)
+    if "c" in PAR["w2"]:
+        fill("one5", CH, 1.0)
+        fill("cv", 256, -1.0)
+        for k in (128, 130):
+            gop(lambda g, k=k: g.iota(T.cv[:, k:256:16], [[0, 8]], -17, 0, allow_small_or_imprecise_dtypes=True), [], [r("cv")], 8)
     gop(lambda g: g.affine_select(T.I[:, :], T.ones[:, :], [[-1, 128]], A.is_equal, 0.0, 0, 1), [r("ones")], [r("I")], 128)
-    for (b, val) in (("nI", -1.0), ("If", 1.0 / 12), ("nIf", -1.0)):
-        gop(lambda g, b=b, val=val: g.affine_select(T[b][:, :], T.I[:, :], [[-1, 128]], A.not_equal, val, 0, 1), [r("I")], [r(b)], 128)
+    gop(lambda g: g.affine_select(T.nI[:, :], T.I[:, :], [[-1, 128]], A.not_equal, -1.0, 0, 1), [r("I")], [r("nI")], 128)
     gop(lambda g: g.affine_select(T.g8[:, 0:8], T.ones[:, 0:8], [[-16, 8]], A.is_ge, 0.0, 0, 1), [r("ones")], [r("g8", 0, 8)], 8)
     gop(lambda g: g.affine_select(T.g8[:, 8:16], T.g8[:, 0:8], [[16, 8]], A.is_ge, 0.0, 15, -1), [r("g8", 0, 8)], [r("g8", 8, 16)], 8)
     gop(lambda g: g.affine_select(T.Tl[:, 16:144:16], T.g8[:, 8:16], [[0, 8]], A.is_ge, 0.0, 0, 0), [r("g8", 8, 16)], [r("Tl")], 8)
@@ -343,16 +358,20 @@ def build(T, topo, core):
     more(w("pf", 2, 3), w("pf", 1, 2), -17.0)
     op("s", lambda g, e: g.scalar.activation(T.ioL[:, :], T.io16[:, :], AF.Identity, bias=T.pf[:, 0:1]), [r("io16"), r("pf", 0, 1)], [r("ioL")], cst(128))
     more(sm("Ap"), sm("ioL"), V - OFF)
-    more(sm("Pp"), sm("ioL"), -OFF)
+    cp(sm("ioh"), sm("ioL"))
+    gop(lambda g: g.affine_select(T.Ik[:, :], T.I[:, :], [[-1, 128]], A.not_equal, V / 2, 0, 1), [r("I")], [r("Ik")], 128)
     cp(w("u0", 0, 256), w("tab", 0, 256))
-    for hf in range(2):
-        lo = 1024 * hf
-        vop(lambda v, lo=lo: v.tensor_copy(T.SCa[:, :].indirect(T.u0[:, lo // 16:lo // 16 + 64]), T.J[:, lo:lo + 1024]),
-            [r("J", lo, lo + 1024), r("u0", 0, 128)], [r("SCa")], 1024, SC)
-        op("s", lambda g, e, lo=lo: g.scalar.activation(T.SCb[:, :].indirect(T.u0[:, 128 + lo // 16:128 + lo // 16 + 64]), T.J[:, lo:lo + 1024], AF.Silu),
-           [r("J", lo, lo + 1024), r("u0", 128, 256)], [r("SCb")], cst(1024, SC) + (1300.0 if hf == 0 else 0.0))
-    for lo in (0, 1024):
-        more(w("p0s", lo, lo + 1024), w("p0s", lo, lo + 1024), -CENTER, 0.5)
+    send([([w("u0", 0, 256)], -1, w("u1", 0, 256)), ([w("u0", 0, 256)], -2, w("u2", 0, 256))], BIG // 8)
+    table = 1300.0
+    for k, b in enumerate(("SCa", "SCb")):
+        for (lo, hi, way) in pieces(PAR["sc"][k]):
+            out, src = ind(w(b), offs("u0", lo, hi, k)), w("J", lo, hi)
+            if way == "v":
+                vop(lambda v, out=out, src=src: v.tensor_copy(out, ap(src)), [src, offs("u0", lo, hi, k)], [w(b)], hi - lo, SC)["sc"] = hi - lo
+            else:
+                op("s", lambda g, e, out=out, src=src: g.scalar.activation(out, ap(src), AF.Silu), [src, offs("u0", lo, hi, k)], [w(b)],
+                   cst(hi - lo, SC) + table)["sc"] = hi - lo
+                table = 0.0
     ps = bank()
     for k, b in enumerate(("SCa", "SCb")):
         for i in range(16):
@@ -360,7 +379,7 @@ def build(T, topo, core):
                [r(b), r("Tf")], [r(ps, 128 * k, 128 * k + 128)])
     ts(w("vi", 0, 256), w(ps, 0, 256), -32.0, None, A.add)
     cp(w("u0", 256, 512), w("vi", 0, 256))
-    send([([w("u0", 0, 512)], -1, w("u1", 0, 512)), ([w("u0", 0, 512)], -2, w("u2", 0, 512))], BIG // 4)
+    send([([w("u0", 256, 512)], -1, w("u1", 256, 512)), ([w("u0", 256, 512)], -2, w("u2", 256, 512))], BIG // 8)
     ts(sm("Bp"), w("tab1", 128, 256), -OFF, None, A.add)
     ts(sm("zt"), w("tab2", 256, 384), -CENTER, None, A.add)
     tt(sm("f3"), w("tab2", 128, 256), w("tab2", 0, 128), A.subtract)
@@ -388,10 +407,16 @@ def build(T, topo, core):
     def add_gather(out, win, off, other, lo, hi, way, tmp, eng="vs"):
         if way == "v":
             return gfuse(out, win, off, other, A.add)
+        at = len(ops)
         gather(w(tmp, lo, hi), win, off, "s")
         ps = bank(hi - lo)
         psum(ps, lo, hi, [w(tmp, lo, hi), other])
-        return evac(out, w(ps, 0, hi - lo), eng)
+        evac(out, w(ps, 0, hi - lo), eng)
+        if way != "s":
+            gfuse(out, win, off, other, A.add)
+            for o in ops[at:]:
+                o["alt"] = list(range(at, len(ops)))
+                o["off"] = (o is ops[-1]) == (way == "y")
 
     for (lo, hi, way) in pieces(PAR["s0"]):
         for k in range(2):
@@ -436,13 +461,15 @@ def build(T, topo, core):
             sop(sm("ws1"), sm(ps), AF.Sign, bias=-8.5)
         for (lo, hi, way) in pieces(PAR["sel"][f]):
             add_gather(w("P1", lo, hi), w(Y, 0, V + (1024 if hi <= 1024 else V)), offs("sel", lo, hi), w(O, lo, hi), lo, hi, way, "t1")
-        tt(sm("f5"), sm(f1), sm("Pp"), A.max)
-        ts(sm("sel" + "AB"[f % 2]), sm("f5"), OFF, None, A.add)
+        sop(sm("s1"), sm(f1), AF.Sign, bias=OFF)
+        ps = bank()
+        small(ps, [("Ik", "s1"), ("I", "ioh")])
+        ts(sm("sel" + "AB"[f % 2]), sm(ps), V / 2, None, A.add)
 
-    def bound():
+    def bound(plain):
         for (lo, hi, way) in pieces(PAR["fp"]):
             ps = bank(hi - lo)
-            psum(ps, lo, hi, (), [w("O2", lo, hi)], [("Bc", "zt")])
+            psum(ps, lo, hi, (), [w("DD2", lo, hi, V)] * plain + [w("O2", lo, hi)], [("Bc", "zt")])
             evac(w("nU", lo, hi), w(ps, 0, hi - lo))
 
     def step2a(rnd):
@@ -470,10 +497,17 @@ def build(T, topo, core):
                 o = over0(w("IND", lo, hi, j * V), w(ps, 0, hi - lo))
                 by.append(([lambda o=o, j=j: ap(slide("T2w" if o["e"] == "v" else "Tl", j))], w("IND", lo, hi, j * V)))
             ps = bank(hi - lo)
-            psum(ps, lo, hi, by=by)
             out, src = w("W2", lo, hi), w(ps, 0, hi - lo)
-            op("s", lambda g, e, out=out, src=src, way=way: g.scalar.activation(ap(out), ap(src), AF.Sign, bias=T.pf[:, 2:3] if way == "V" else -1.0),
-               [src, w("pf", 2, 3)], [out], cst(hi - lo))
+            if PAR["w2"][rnd] == "s":
+                psum(ps, lo, hi, by=by)
+                op("s", lambda g, e, out=out, src=src, way=way: g.scalar.activation(ap(out), ap(src), AF.Sign, bias=T.pf[:, 2:3] if way == "V" else -1.0),
+                   [src, w("pf", 2, 3)], [out], cst(hi - lo))
+            else:
+                k = 128 * (way == "V")
+                for a in range(0, hi - lo, CH):
+                    mm([[(ps, a, a + CH), T.cv[0:1, k:k + 128], T.one5[0:1, :], True, False, CH]], [r("cv"), r("one5")], [(ps, a, a + CH)])
+                psum(ps, lo, hi, by=by, start=False)
+                unit(out, src)
 
     def step2b(rnd):
         for (lo, hi, way) in pieces(PAR["t2"][rnd]):
@@ -514,13 +548,13 @@ def build(T, topo, core):
             toblock(own, [("gx", "TS", 0), ("gy", "TS", 160)], lo, hi, lo == 0, hi == V)
         return own
 
-    outs = {"first": True}
+    outs = {"n": 0}
 
     def add_out(b):
-        for lo in (0, 1024):
-            first = outs["first"]
-            dma("y" if first else "g", T.gain[:, lo:lo + 1024], T[b][:, lo:lo + 1024], [r(b, lo, lo + 1024)], [r("gain", lo, lo + 1024)], BIG, not first)
-        outs["first"] = False
+        first, late = outs["n"] == 0, outs["n"] >= 5
+        for (lo, hi, way) in pieces(PAR["add"] if late else "16x"):
+            dma("y" if first else "g", T.gain[:, lo:hi], T[b][:, lo:hi], [r(b, lo, hi)], [r("gain", lo, hi)], 512 * (hi - lo), not first, not late)
+        outs["n"] += 1
 
     def swap(rnd):
         ps = bank()
@@ -563,19 +597,17 @@ def build(T, topo, core):
 
     def edges2():
         for (lo, hi, way) in pieces(PAR["fe"]):
-            sop(w("SCb", lo, hi), w("DD2", lo, hi), AF.Exp, bias=math.log(3.0), scale=-0.125)
-            sop(w("eb", lo, hi), w("DD2", lo, hi, V), AF.Exp, bias=-math.log(4.0), scale=-0.125)
-        add_out("SCb")
-        for (lo, hi, way) in pieces(PAR["fp"]):
-            ps = bank(hi - lo)
-            psum(ps, lo, hi, by=[(sm("If"), w("SCb", lo, hi))], k=4, stop=False)
-            psum(ps, lo, hi, by=[(sm("nIf"), w("eb", lo, hi))], k=4, start=False)
-            evac(w("eb", lo, hi), w(ps, 0, hi - lo))
+            sop(w("SCb", lo, hi), w("DD2", lo, hi), AF.Exp, scale=-0.125)
+            sop(w("eb", lo, hi), w("DD2", lo, hi, V), AF.Exp, scale=-0.125)
+            times(w("eb", lo, hi), w("eb", lo, hi), -1.0)
+        for k in range(3):
+            add_out("SCb")
+        dma("g", T.eb[:, :], T.SCb[:, :], [w("SCb")], [w("eb")], 2 * BIG, True)
 
     def gain1():
         ps = bank()
         small(ps, [("I", "nsB0"), ("nI", "wsA0"), ("nI", "wsA0"), ("nI", "wsA1"), ("nI", "wsA1"), ("I", "nsB1")])
-        more(sm("kp"), sm(ps), -6.0)
+        either(sm("kp"), sm(ps), (0.25, -1.5, A.mult, A.add), AF.Identity, bias=-1.5, scale=0.25)
         for (lo, hi, way) in pieces(PAR["fp"]):
             ps = bank(hi - lo)
             psum(ps, lo, hi, tables=[("Bc", "kp")])
@@ -616,7 +648,7 @@ def build(T, topo, core):
     H = V // PAR["halves"]
     for rnd in range(2):
         e0, ent, eni = ("E0", "ent0", "eni0") if rnd == 0 else ("E0n", "ent1", "eni1")
-        bound()
+        bound(rnd * PAR["plain"])
         step1(2 * rnd, "YA", "O1")
         if rnd == 1:
             terms(0)
@@ -667,7 +699,11 @@ def build(T, topo, core):
             elif rnd == 0:
                 ts(w("E0n", lo, hi), w(ps, 0, hi - lo), 0.0, 63.0, A.max, A.min)
             else:
-                ts(w("SCb", lo, hi), w(ps, 0, hi - lo), 0.0, 63.0, A.max, A.min)
+                if way == "s":
+                    sop(w("t0", lo, hi), w(ps, 0, hi - lo), AF.Relu, bias=63.0, scale=-1.0)
+                    sop(w("SCb", lo, hi), w("t0", lo, hi), AF.Relu, bias=63.0, scale=-1.0)
+                else:
+                    ts(w("SCb", lo, hi), w(ps, 0, hi - lo), 0.0, 63.0, A.max, A.min)
                 dma("y", T.tollout[:, lo:hi], T.SCb[:, lo:hi], [w("SCb", lo, hi)], [w("tollout", lo, hi)], 512 * (hi - lo))
         if rnd == 0:
             for (lo, hi, way) in pieces(PAR["y"]):
@@ -677,7 +713,8 @@ def build(T, topo, core):
                 evac(w("YA", lo, hi), w(ps, 0, hi - lo))
             for lo in range(0, V, H):
                 send([([w("E0n", lo, lo + H), w("DD", lo, lo + H, V)], -1, w("O1", lo, lo + H))], BIG // PAR["halves"])
-            send([([w("E0n"), w("DD", 0, V, V)], -2, w("O2"))], BIG)
+            for lo in (0, 1024):
+                send([([w("E0n", lo, lo + 1024)] + [w("DD", lo, lo + 1024, V)] * (1 - PAR["plain"]), -2, w("O2", lo, lo + 1024))], BIG // 2)
     return ops
 
 
@@ -692,7 +729,7 @@ def place(ops, before, after, key, back, lean):
         o = ops[i]
         t0 = at[i] + o["lat"] if back else at[i]
         t, e, end = t0, None, t0
-        for x, cost in o["on"]:
+        for x, cost in [] if o.get("off") else o["on"]:
             los, his = busy[x]
             k = m = len(his)
             while k and his[k - 1] > t0:
@@ -729,41 +766,67 @@ def place(ops, before, after, key, back, lean):
     return start, fin, eng
 
 
-def polish(ops, uses, home, seq, eng, rng):
-    n = len(ops)
-    pred = [[(d, 0.0 if ops[d]["eng"] == "p" and o["eng"] == "p" else LAT) for d in o["deps"]] for o in ops]
+def polish(ops, uses, home, seq, eng, rng, moves, heat, both, FAST, SLOW, anew):
+    n, LAT = len(ops), FAST[3]
+    pred, above = [], []
     succ = [set() for o in ops]
     for o in ops:
+        far = 0
         for d in o["deps"]:
             succ[d].add(o["i"])
-    cost, lat = [dict(o["on"]) for o in ops], [o["lat"] for o in ops]
+            far |= above[d]
+        pred.append([(d, 0.0 if ops[d]["eng"] == "p" and o["eng"] == "p" else LAT, n + d, 0.0 if ops[d]["eng"] == "p" and o["eng"] == "p" else SLOW[3])
+                     for d in o["deps"] if not far >> d & 1])
+        above.append(far | sum(1 << d for d in o["deps"]))
+    cost, cost2 = [[{e: c * x[0] / PCY if e == "p" and x[0] != PCY else c + o.get("ga", 0) * (x[1] - GA) + o.get("sc", 0) * (x[2] - SC) for e, c in o["on"]} for o in ops]
+                   for x in (FAST, SLOW)]
+    lat, lat2 = [[o["lat"] * x[4] / FAR if x[4] != FAR else o["lat"] for o in ops] for x in (FAST, SLOW)]
+    dq = [o.get("dq", 0.0) / FAR if anew else 0.0 for o in ops]
+    if anew:
+        lat, lat2 = [[o.get("fix", o["lat"]) * x[4] / FAR for o in ops] for x in (FAST, SLOW)]
+    alts = [o["alt"] for o in ops if o.get("alt", [0])[0] == o["i"] and "alt" in o]
     opens = {uses[u][0]: u for u in uses}
     shuts = {uses[u][-1]: u for u in uses}
 
-    def run(seq, eng, old=None, same=0):
+    def run(seq, eng, old=None, same=0, until=1 << 30, allow=0.0):
         same -= same % 32
         if same:
             start, fin, why, banks, marks = list(old[1]), list(old[2]), list(old[3]), dict(old[4]), old[5][:same // 32]
             free, held, last = old[5][same // 32]
             free, held, last = dict(free), list(held), list(last)
         else:
-            free = {e: (0.0, -1) for e in "vspgy"}
-            start, fin, why = [0.0] * n, [0.0] * n, [-1] * n
+            free = {e: (0.0, -1, 0.0) for e in "vspgyq"}
+            start, fin, why = [0.0] * n, [0.0] * (2 * n), [-1] * (2 * n)
             held, last, banks, marks = [0.0] * 8, [None] * 8, {}, []
         for at in range(same, n):
             if at % 32 == 0:
+                if at > until:
+                    was = old[5][at // 32]
+                    if min(free[e][0] - was[0][e][0] for e in "vsp") + min(free[e][2] - was[0][e][2] for e in "vsp") > allow:
+                        return None
+                    if (free, held, last) == was and fin == old[2]:
+                        return old[0], start, fin, why, banks, marks + old[5][at // 32:]
                 marks.append((dict(free), list(held), list(last)))
             i = seq[at]
-            t, y = 0.0, -1
-            for d, x in pred[i]:
+            t = t2 = 0.0
+            y = y2 = -1
+            for d, x, d2, x2 in pred[i]:
                 x += fin[d]
                 if x > t:
                     t, y = x, d
+                x2 += fin[d2]
+                if x2 > t2:
+                    t2, y2 = x2, d
             e = eng[i]
+            if e == "-":
+                start[i], fin[i], why[i], fin[n + i], why[n + i] = t, t - LAT, y, t2 - SLOW[3], y2
+                continue
             if e:
-                x, d = free[e]
+                x, d, x2 = free[e]
                 if x > t:
                     t, y = x, d
+                if x2 > t2:
+                    t2, y2 = x2, d
                 if i in opens:
                     u = opens[i]
                     k = int(u[2])
@@ -775,21 +838,37 @@ def polish(ops, uses, home, seq, eng, rng):
                     was = [last[c] for c in range(b, b + k) if last[c]]
                     if x > t:
                         t, y = x, max([uses[c][-1] for c in was], key=lambda d: fin[d])
+                    for c in was:
+                        d = uses[c][-1]
+                        if fin[n + d] + SLOW[3] > t2:
+                            t2, y2 = fin[n + d] + SLOW[3], d
                     banks[u] = (b, was)
                     held[b:b + k], last[b:b + k] = [1e18] * k, [u] * k
                 x = t + cost[i][e]
-                free[e] = (x, i)
+                t2 += cost2[i][e]
+                free[e] = (x, i, t2)
+                if dq[i]:
+                    x, t2 = max(x, free["q"][0]) + dq[i] * FAST[4], max(t2, free["q"][2]) + dq[i] * SLOW[4]
+                    free["q"] = (x, i, t2)
             else:
                 x = t
-            start[i], fin[i], why[i] = t, x + lat[i], y
+            start[i], fin[i], why[i], fin[n + i], why[n + i] = t, x + lat[i], y, t2 + lat2[i], y2
             if i in shuts:
                 u = shuts[i]
                 b = banks[u][0]
                 held[b:b + int(u[2])] = [x + LAT] * int(u[2])
-        return max(fin), start, fin, why, banks, marks
+        return max(fin[:n]) + both * max(fin[n:]) + PAR["mean"] * sum(fin) / n, start, fin, why, banks, marks
 
+    for k in range(40):
+        if run(seq, eng) is not None:
+            break
+        late = [i for u in uses for i in uses[u][-2::-1] if (k > 20 or i == uses[u][0] and ops[uses[u][1]]["eng"] == "p") and rng.random() < 0.3]
+        for i in late:
+            a = seq.index(i)
+            b = min(seq.index(j) for j in succ[i])
+            seq = seq[:a] + seq[a + 1:b] + [i] + seq[b:]
     now = best = run(seq, eng) + (seq, eng)
-    for k in range(PAR["moves"]):
+    for k in range(moves):
         if k % 100 == 99:
             seq = sorted(now[6], key=lambda i: now[1][i])
             got = run(seq, now[7])
@@ -800,21 +879,103 @@ def polish(ops, uses, home, seq, eng, rng):
             pos = [0] * n
             for j, i in enumerate(seq):
                 pos[i] = j
-            chain, i = [], max(range(n), key=lambda i: fin[i])
-            while why[i] >= 0:
-                if why[i] not in ops[i]["deps"] or len(cost[i]) > 1:
-                    chain.append(i)
-                i = why[i]
-        i = chain[int(rng.integers(len(chain)))]
-        p, how = why[i], rng.random()
-        if how < PAR["flips"] or p in ops[i]["deps"]:
+            chain, tails = [], {0: None, n: None}
+            for m in (0, n):
+                i = max(range(n), key=lambda i: fin[m + i])
+                while why[m + i] >= 0:
+                    if why[m + i] not in ops[i]["deps"] or len(cost[i]) > 1:
+                        chain.append((i, why[m + i]))
+                    i = why[m + i]
+        i, p = chain[int(rng.integers(len(chain)))]
+        how = rng.random()
+        if anew and rng.random() < anew:
+            a = 32 * int(rng.integers(n // 32))
+            b = min(n - 1, a + int(rng.integers(24, 90)))
+            m = n if how < PAR["slow"] else 0
+            cs, wait = (cost2, SLOW[3]) if m else (cost, LAT)
+            if tails[m] is None:
+                tail, nxt = [0.0] * n, {}
+                for j in reversed(seq):
+                    x = max([tail[d] + wait for d in succ[j]] + [0.0]) + lat[j]
+                    if eng[j] in cs[j]:
+                        x = max(x, nxt.get(eng[j], 0.0) - PAR["loose"]) + cs[j][eng[j]]
+                        nxt[eng[j]] = x
+                    tail[j] = x
+                tails[m] = tail
+            part, eng = set(seq[a:b + 1]), list(eng)
+            urge = {j: tails[m][j] + float(x) for j, x in zip(seq[a:b + 1], rng.normal(0.0, PAR["blur"], b + 1 - a))}
+            free = {e: x[2 if m else 0] for e, x in marks[a // 32][0].items()}
+            end, new, soon = {}, [], rng.random() * PAR["soon"]
+            left = {j: len([d for d in ops[j]["deps"] if d in part]) for j in part}
+            ready = {j: max([fin[m + x[0]] + wait for x in pred[j]] + [0.0]) for j in seq[a:b + 1] if not left[j]}
+            while ready:
+                can = [(max(t, free[e]), j, e) for j, t in ready.items() for e in (cs[j] if eng[j] in cs[j] else ())]
+                idle = [j for j in ready if eng[j] not in cs[j]]
+                if idle:
+                    j = idle[0]
+                    end[j] = ready[j] + (lat[j] if eng[j] is None else -wait)
+                else:
+                    t0 = min(can)[0] + soon
+                    t, j, e = max([x for x in can if x[0] <= t0], key=lambda x: (urge[x[1]], -x[0]))
+                    eng[j], free[e] = e, t + cs[j][e]
+                    end[j] = free[e] + lat[j]
+                new.append(j)
+                del ready[j]
+                for d in succ[j]:
+                    if d in part:
+                        left[d] -= 1
+                        if not left[d]:
+                            ready[d] = max([end.get(x[0], fin[m + x[0]]) + wait for x in pred[d]] + [0.0])
+            seq = seq[:a] + new + seq[b + 1:]
+        elif alts and rng.random() < PAR["ways"]:
+            x = alts[int(rng.integers(len(alts)))]
+            eng = list(eng)
+            for j in x:
+                eng[j] = "-" if eng[j] != "-" else ops[j]["eng"][int(rng.integers(len(ops[j]["eng"])))]
+            a, b = min(pos[j] for j in x), min(pos[j] for j in succ[x[-1]]) - 1
+            rest = [j for j in seq[a:b + 1] if j not in x]
+            at = 0
+            for j in x:
+                lo = max([at] + [m + 1 for m, d in enumerate(rest) if d in ops[j]["deps"]])
+                hi = min([len(rest)] + [m for m, d in enumerate(rest) if d in succ[j]])
+                at = lo + int(rng.integers(min(hi - lo, 10) + 1))
+                rest.insert(at, j)
+                at += 1
+            seq = seq[:a] + rest + seq[b + 1:]
+        elif rng.random() < PAR["free"]:
+            b = int(rng.integers(n))
+            i, a = seq[b], max(0, b - int(rng.integers(1, 60)))
+            if eng[i] == "-":
+                fresh = False
+                continue
+            e = ("s" if eng[i] == "v" else "v") if len(cost[i]) > 1 and how < 0.5 else eng[i]
+            if e and rng.random() < PAR["gaps"]:
+                ready, end, can = max([fin[x[0]] + x[1] for x in pred[i]] + [0.0]), 0.0, []
+                for j in seq[:b]:
+                    if eng[j] == e:
+                        if start[j] - max(end, ready) > PAR["room"] * cost[i][e]:
+                            can.append(j)
+                        end = fin[j] - lat[j]
+                if not can:
+                    fresh = False
+                    continue
+                a = pos[can[int(rng.integers(len(can)))]]
+            need, part = {i}, seq[a:b + 1]
+            for j in reversed(part):
+                if not succ[j].isdisjoint(need):
+                    need.add(j)
+            seq = seq[:a] + [j for j in part if j in need] + [j for j in part if j not in need] + seq[b + 1:]
+            if e != eng[i]:
+                eng = list(eng)
+                eng[i] = e
+        elif how < PAR["flips"] or p in ops[i]["deps"]:
             x = i if len(cost[i]) > 1 and (how < PAR["flips"] / 2 or len(cost[p]) < 2) else p
-            if len(cost[x]) < 2:
+            if len(cost[x]) < 2 or eng[x] == "-":
                 fresh = False
                 continue
             eng = list(eng)
             eng[x] = "s" if eng[x] == "v" else "v"
-            a = pos[x]
+            a = b = pos[x]
         else:
             a, b = pos[p], pos[i]
             if how > 1.0 - PAR["far"]:
@@ -835,18 +996,19 @@ def polish(ops, uses, home, seq, eng, rng):
                         late.add(j)
                 part = [j for j in part if j not in late] + [j for j in part if j in late]
             seq = seq[:a] + part + seq[b + 1:]
-        got = run(seq, eng, now, a)
-        fresh = got is not None and got[0] <= total - PAR["heat"] * (1.0 - k / PAR["moves"]) * math.log(rng.random() + 1e-12)
+        allow = -heat * (1.0 - k / moves) * math.log(rng.random() + 1e-12)
+        got = run(seq, eng, now, a, b + PAR["wait"], allow + PAR["give"])
+        fresh = got is not None and got[0] <= total + allow
         if fresh:
             now = got + (seq, eng)
             if now[0] < best[0]:
                 best = now
     total, start, fin, why, banks, marks, seq, eng = best
-    more = {}
+    more, banks = {}, {u: banks[u] for u in banks if eng[uses[u][0]] != "-"}
     for u in banks:
         for i in uses[u][:int(u[2])]:
             more[i] = set(j for c in banks[u][1] for j in uses[c])
-    return total, start, fin, eng, {u: banks[u][0] for u in banks}, more
+    return max(fin[:n]), start, fin, eng, {u: banks[u][0] for u in banks}, more
 
 
 def schedule(ops):
@@ -869,6 +1031,8 @@ def schedule(ops):
     def deal(start, fin):
         last, free, banks, more = [None] * 8, [-1.0] * 8, {}, {}
         for u in sorted(uses, key=lambda u: start[uses[u][-1]]):
+            if ops[uses[u][0]].get("off"):
+                continue
             k = int(u[2])
             can = [(max(free[b:b + k]), b) for b in range(0, 8, k)]
             fit = [x for x in can if x[0] + PAR["fit"] <= start[uses[u][0]]]
@@ -889,7 +1053,7 @@ def schedule(ops):
                     base[i].add(uses[home[d]][-1])
         succ = turn(base)
         rng = np.random.default_rng(PAR["seed"])
-        lean = [PAR["lean"]] * n
+        lean = [PAR["lean"][0 if o.get("ga") else 1] for o in ops]
         fin = place(ops, succ, base, [-i for i in range(n)], True, lean)[1]
         start, fin, eng = place(ops, base, succ, [-f for f in fin], False, lean)
         best = now = None
@@ -907,14 +1071,23 @@ def schedule(ops):
             if best is None or now[0] < best[0]:
                 best = now
             start, fin = now[1:3]
-        PAR["plan"] = polish(ops, uses, home, sorted(range(n), key=lambda i: (best[1][i], i)), best[3], rng)
+        best = best[:3] + (["-" if o.get("off") else e for o, e in zip(ops, best[3])],)
+        for stage in PAR["stages"]:
+            best = polish(ops, uses, home, sorted(range(n), key=lambda i: (best[1][i], i)), best[3], rng, *stage)
+        PAR["plan"] = best
     total, start, fin, eng, banks, more = PAR["plan"]
     PAR["banks"] = banks
     for o in ops:
         o["t"], o["e"] = start[o["i"]], eng[o["i"]]
         o["cost"] = dict(o["on"]).get(o["e"], 0.0)
+        for d in list(o["deps"]):
+            if eng[d] == "-":
+                o["deps"].pop(d)
+                o["deps"].update({x: True for x in ops[d]["deps"]})
         for d in more.get(o["i"], ()):
             o["deps"].setdefault(d, False)
+        if o["e"] == "-":
+            o["e"] = None
     return sorted(range(n), key=lambda i: (start[i], i)), total
 
 
@@ -937,6 +1110,8 @@ def rank_program(g, core, T, topo):
         top = {}
         for d, hard in o["deps"].items():
             p = ops[d]
+            if p["kind"] == "n":
+                continue
             if p["kind"] in "da":
                 if d not in seen[e]:
                     seen[e][d] = True

import math
import numpy as np
from concourse.bass import DstId, RemoteDMATransfer
from concourse.mybir import AluOpType as A, ActivationFunctionType as AF

V = 2048
CH = 512
CENTER = 220.0
STEEP = 8192.0
OFF = 8.5 * STEEP
BF, F32, I32, U16, F16 = "bfloat16", "float32", "int32", "uint16", "float16"

SCRATCH = {}
for _n in ("h", "hm", "p0s", "E0", "E0n", "O1", "O2", "nU", "ndb", "nsa", "dd1", "dd2", "dl2", "P1", "T2", "IND1",
           "W2", "W1a", "W1b", "gx", "gy", "Bc", "B6", "Bw", "fA", "fB", "q", "t0", "t1"):
    SCRATCH[_n] = ("sbuf", [128, V], BF)
for _n in ("SS", "DD", "SS1", "DD2", "YA", "YB"):
    SCRATCH[_n] = ("sbuf", [128, 2 * V], BF)
SCRATCH["IND"] = ("sbuf", [128, 3 * V], BF)
for _n in ("J", "SCa", "SCb", "eb"):
    SCRATCH[_n] = ("sbuf", [128, V], F32)
for _n in ("tab", "tab1", "tab2"):
    SCRATCH[_n] = ("sbuf", [128, 384], I32)
for _n in ("u0", "u1", "u2"):
    SCRATCH[_n] = ("sbuf", [128, 512], U16)
for _n in ("sel", "selA", "selB", "lA", "lB"):
    SCRATCH[_n] = ("sbuf", [128, 128], U16)
for _n in ("I", "nI", "Ik", "ones", "s1", "s2", "ws1", "wsA0", "nsB0", "wsA1", "nsB1", "kp", "qc", "ent0", "ent1", "eni0", "eni1", "ent3", "dm",
           "mo0", "mo1", "mo2", "mo3", "mi0", "mi1", "mi2", "mi3"):
    SCRATCH[_n] = ("sbuf", [128, 128], BF)
SCRATCH["MM"] = ("sbuf", [128, 768], BF)
SCRATCH["TS"] = ("sbuf", [128, 640], BF)
SCRATCH["cv"] = ("sbuf", [128, 256], BF)
SCRATCH["one5"] = ("sbuf", [128, CH], BF)
SCRATCH["zt"] = ("sbuf", [128, 128], F16)
SCRATCH["ioh"] = ("sbuf", [128, 128], F16)
for _n in ("Tl", "T2w", "TN"):
    SCRATCH[_n] = ("sbuf", [128, 160], BF)
SCRATCH["Tf"] = ("sbuf", [128, 160], F32)
SCRATCH["g8"] = ("sbuf", [128, 32], BF)
for _n in ("io16", "ioL", "f1A", "f1B", "f2", "f3", "f4", "a2f", "dab", "Ap", "Bp"):
    SCRATCH[_n] = ("sbuf", [128, 128], F32)
SCRATCH["vi"] = ("sbuf", [128, 256], I32)
SCRATCH["pi"] = ("sbuf", [128, 8], I32)
SCRATCH["pm"] = ("sbuf", [128, 8], I32)
SCRATCH["pf"] = ("sbuf", [128, 8], F32)
SCRATCH["PS"] = ("psum", [128, 8 * CH], F32)

SEMAPHORES = ["ev", "es", "ep", "eg", "sent"] + ["d%d" % _k for _k in range(40)] + ["r%d" % _k for _k in range(50)]

CYC, PCY, GA, SC, LAT, FAR = 1.0, 0.53, 1.35, 3.8, 200.0, 1.35
WAITS = (PCY, GA, SC, LAT, FAR)
SLOW = (0.5, 1.85, 3.8, 115.0, 0.9)
PAR = {"stages": ((9000, 150.0, 1.5, WAITS, SLOW, 0.35), (75000, 130.0, 1.5, WAITS, SLOW, 0.3)), "slow": 0.5, "loose": 500.0, "blur": 1000.0, "soon": 500.0, "ways": 0.1, "rate": 400.0, "mean": 0.3, "gaps": 0.3, "room": 0.5, "wait": 20, "give": 100.0, "free": 0.5, "heat": 120.0, "flips": 0.15,
       "far": 0.6, "passes": 100, "shake": (100.0, 500.0, 2000.0), "span": 3000.0, "part": 0.3,
       "lean": (600.0, -200.0), "tilt": (-1e9, 100.0, 100.0, 600.0, 1e9, 1e9), "flip": 0.3, "slack": 300.0, "fit": 1e9, "seed": 14,
       "sc": ("8v8v", "8s8s"), "ss": "4v4v8v", "s0": "8v4v4s", "sel0": "4s4v8v",
       "t1": ("8v4s4s",) * 4, "i1": "8v4v4v", "sel": ("4s4v8v",) * 4, "r2": ("4M4M4M4V",) * 2, "t2": ("8v4s4s",) * 2, "i2": "8v8v",
       "c2": "8x4x4x", "w1": "4x4x4x4x", "c1": "8x6x2x", "y": "4x4x4x4x", "clip": "4s4v4s4v", "out": "4s4v4v4v",
       "fg": "8x8x", "fp": "8x8x", "fe": "8s8s", "terms": "ddpv", "fold": 1, "spare": 2000.0, "dm": 0, "halves": 4, "plain": 1, "w2": "ss", "add": "8x8x"}


def pieces(s):
    out, at, k = [], 0, ""
    for x in s:
        if x.isdigit():
            k += x
        else:
            out.append((at, at + 128 * int(k), x))
            at, k = at + 128 * int(k), ""
    return out


def build(T, topo, core):
    ops = []
    acc = {}
    cnt = {"d": 0, "r": 0, "ps": 0}
    rank = T.rank_of(core)
    n = len(T.cores)

    def op(eng, fn, R, Wr, cost, kind="c", lat=0.0, extra=()):
        on = [(e, cost[e] if isinstance(cost, dict) else cost) for e in eng or ""]
        o = {"i": len(ops), "eng": eng, "fn": fn, "on": on, "kind": kind, "lat": lat, "deps": {}, "R": R, "W": Wr}
        for e in extra:
            o["deps"][e["i"]] = True
        for lst, isw in ((R, False), (Wr, True)):
            for (b, lo, hi) in lst:
                ps = b.startswith("ps")
                keep = []
                for (p, l2, h2, w2) in acc.get(b, []):
                    over = l2 < hi and lo < h2
                    if p is not o and (over or ps):
                        if over and (isw or w2):
                            o["deps"][p["i"]] = True
                        elif ps and p["i"] not in o["deps"]:
                            o["deps"][p["i"]] = False
                    if not (isw and lo <= l2 and h2 <= hi and p is not o):
                        keep.append((p, l2, h2, w2))
                keep.append((o, lo, hi, isw))
                acc[b] = keep
        ops.append(o)
        return o

    def r(b, lo=0, hi=1 << 20):
        return (b, lo, hi)

    def w(b, lo=0, hi=V, off=0):
        return (b, off + lo, off + hi)

    def sm(b):
        return (b, 0, 128)

    def ap(x):
        b, lo, hi = x
        if b.startswith("ps"):
            at = CH * PAR["banks"][b]
            return T.PS[:, at + lo:at + hi]
        return T[b][:, lo:hi]

    def bank(width=CH):
        cnt["ps"] += 1
        return "ps%d#%d" % (1 if width <= CH else 2, cnt["ps"])

    def cst(nel, k=1.0):
        return 60.0 + max(64.0, nel * k) * CYC

    def vop(fn, R, Wr, nel, k=1.0):
        return op("v", lambda g, e: fn(g.vector), R, Wr, cst(nel, k))

    def sop(out, src, func, bias=0.0, scale=1.0):
        return op("s", lambda g, e: g.scalar.activation(ap(out), ap(src), func, bias=bias, scale=scale), [src], [out], cst(out[2] - out[1]))

    def ts(out, src, s1, s2, o0, o1=None, k=1.0):
        if o1 is None:
            return vop(lambda v: v.tensor_scalar(ap(out), ap(src), s1, None, o0), [src], [out], out[2] - out[1], k)
        return vop(lambda v: v.tensor_scalar(ap(out), ap(src), s1, s2, o0, o1), [src], [out], out[2] - out[1], k)

    def tt(out, a, b, o, k=2.0):
        return vop(lambda v: v.tensor_tensor(ap(out), ap(a), ap(b), o), [a, b], [out], out[2] - out[1], k)

    def cp(out, src):
        return vop(lambda v: v.tensor_copy(ap(out), ap(src)), [src], [out], out[2] - out[1])

    def either(out, src, onv, func, bias=0.0, scale=1.0, eng="vs", k=1.0):
        def fn(g, e):
            if e == "s":
                return g.scalar.activation(ap(out), ap(src), func, bias=bias, scale=scale)
            if onv is None:
                return g.vector.tensor_copy(ap(out), ap(src))
            if len(onv) == 2:
                return g.vector.tensor_scalar(ap(out), ap(src), onv[0], None, onv[1])
            return g.vector.tensor_scalar(ap(out), ap(src), onv[0], onv[1], onv[2], onv[3])
        return op(eng, fn, [src], [out], {"v": cst(out[2] - out[1], k), "s": cst(out[2] - out[1])})

    def evac(out, src, eng="vs"):
        return either(out, src, None, AF.Copy, eng=eng)

    def times(out, src, x, k=1.0):
        return either(out, src, (x, A.mult), AF.Identity, scale=x, k=k)

    def more(out, src, x, k=1.0):
        return either(out, src, (x, A.add), AF.Identity, bias=x, k=k)

    def unit(out, src):
        return either(out, src, (-1.0, 1.0, A.max, A.min), AF.Sign)

    def over0(out, src):
        return either(out, src, (0.5, 0.5, A.is_gt, A.subtract), AF.Sign, bias=-0.5)

    def marked(out, ps):
        return either(out, sm(ps), (-5.0, A.is_gt), AF.Sign, bias=6.0)

    def ind(win, off):
        return ap(win).indirect(ap(off))

    def offs(b, lo, hi, k=0):
        return (b, 128 * k + lo // 16, 128 * k + hi // 16)

    def gather(out, win, off, eng="vs", turn=False):
        def fn(g, e):
            if e == "s":
                return g.scalar.activation(ap(out), ind(win, off), AF.Identity if turn else AF.Copy, scale=-1.0 if turn else 1.0)
            if turn:
                return g.vector.tensor_scalar(ap(out), ind(win, off), -1.0, None, A.mult)
            return g.vector.tensor_copy(ap(out), ind(win, off))
        o = op(eng, fn, [win, off], [out], cst(out[2] - out[1], GA))
        o["ga"] = out[2] - out[1]
        return o

    def gfuse(out, win, off, other, how):
        o = vop(lambda v: v.tensor_tensor(ap(out), ind(win, off), ap(other), how), [win, off, other], [out], out[2] - out[1], GA)
        o["ga"] = out[2] - out[1]
        return o

    def mm(mats, R, Wr):
        def fn(g, e):
            last = None
            for (o, l, x, st, sp, nn) in mats:
                last = g.tensor.matmul(ap(o), l[0]() if isinstance(l, list) else l, x, st, sp)
            return last
        return op("p", fn, R, Wr, sum(max(64, m[5]) * PCY + 10.0 for m in mats))

    def slide(b, i, off=0):
        return (b, off + 16 - i, off + 144 - i)

    def psum(ps, lo, hi, plus=(), minus=(), tables=(), by=(), start=True, stop=True, k=1):
        full = [(sm("I"), x) for x in plus] + [(sm("nI"), x) for x in minus] + list(by)
        for a in range(0, hi - lo, CH):
            b = min(a + CH, hi - lo)
            mats, R = [], []
            for (l, x) in full:
                x = (x[0], x[1] + a, x[1] + b)
                mats.append([(ps, a, b), l if isinstance(l, list) else ap(l), ap(x), False, False, (b - a) * k])
                R += [x] + ([r("Tl"), r("T2w")] if isinstance(l, list) else [l])
            alone = start and stop and not mats
            for j in range(a, b, 128):
                for t, (bc, table) in enumerate(tables):
                    R += [sm(table), r(bc)]
                    mats.append([(ps, j, j + 128), T[bc][:, lo + j:lo + j + 128], T[table][:, :], alone and t == 0, alone and t == len(tables) - 1, 128])
            mats[0][3] = start
            if stop:
                mats[-1][4] = True
            mm(mats, R, [(ps, a, b)])

    def tolist(ps, src, lo, hi, tl, to=0):
        out = (ps, lo // 16, hi // 16)
        mats = [[out, ap(slide(tl, i, to)), T[src][:, lo + i:hi:16], i == 0, i == 15, (hi - lo) // 16] for i in range(16)]
        return mm(mats, [r(src, lo, hi), r(tl)], [out])

    def toblock(ps, srcs, lo, hi, start, stop):
        mats = [[sm(ps), ap(slide(tl, k // 128, to)), T[b][:, k:k + 128], False, False, 128] for k in range(lo, hi, 128) for (b, tl, to) in srcs]
        mats[0][3] = start
        mats[-1][4] = stop
        return mm(mats, [r(b, lo, hi) for (b, tl, to) in srcs] + [r(tl) for (b, tl, to) in srcs], [sm(ps)])

    def small(ps, terms):
        return mm([[sm(ps), T[m][:, :], T[x][:, :], k == 0, k == len(terms) - 1, 128] for k, (m, x) in enumerate(terms)],
                  [sm(x) for t in terms for x in t], [sm(ps)])

    def dma(eng, out, src, R, Wr, nbytes, add=False, spare=True):
        s = "d%d" % cnt["d"]
        cnt["d"] += 1
        if add:
            fn = lambda g, e: g.dma_start(out, src, accum_op=A.add)
        elif eng == "y":
            fn = lambda g, e: g.sync.dma_start(out, src)
        else:
            fn = lambda g, e: g.scalar.dma_start(out, src)
        spare = [op(None, None, R, [], 0.0, "n", PAR["spare"])] if add and spare else []
        o = op(eng, fn, R, Wr, 1000.0 if eng == "g" else 100.0, "d", FAR * (2000.0 + nbytes * (2 if add else 1) / 600.0), extra=spare)
        o["dq"], o["fix"] = FAR * nbytes * (2 if add else 1) / 800.0, FAR * 2000.0
        o["sem"] = s
        return o

    def rsem():
        cnt["r"] += 1
        return "r%d" % cnt["r"]

    def send(items, nbytes, again=False):
        trs = []
        loc = rsem() if again else "sent"
        for k, (srcs, sh, dst) in enumerate(items):
            to = T.cores[(rank + sh) % n]
            en = topo.engines(core, to)
            per = len(en) // len(items)
            mask = sum(1 << x for x in en[k * per:(k + 1) * per])
            rid, pid = topo.addr(to)[:2]
            trs.append((srcs, dst, mask, rid, pid, rsem(), per))

        def one(srcs, dst, mask, rid, pid, s, per):
            if len(srcs) == 1:
                return RemoteDMATransfer(dst_ids=[DstId(rid=rid, pnc=pid)], dma_engine_mask=mask, remote_sem=T.sem[s], src=ap(srcs[0]), dst=ap(dst))
            return RemoteDMATransfer(dst_ids=[DstId(rid=rid, pnc=pid)], dma_engine_mask=mask, remote_sem=T.sem[s],
                                     srcs=[ap(x) for x in srcs], dsts=[ap(dst)], alu_op=1)

        def fn(g, e):
            if len(trs) == 1 and len(trs[0][0]) == 1:
                srcs, dst, mask, rid, pid, s, per = trs[0]
                return g.remote_dma(ap(dst), ap(srcs[0]), T.sem[s], T.sem[loc], pid, rid, mask)
            return g.remote_dma_fused([one(*x) for x in trs], local_sem=T.sem[loc])
        srcs = [y for x in trs for y in x[0]]
        o = op("g", fn, srcs, [], 800.0, "x")
        o["inc"] = 0 if again else sum(x[6] for x in trs)
        o["dq"] = FAR * nbytes * len(srcs) / PAR["rate"]
        for (R, Wr, s, val) in [([], [x[1]], x[5], x[6]) for x in trs] + ([(srcs, [], loc, sum(x[6] for x in trs))] if again else []):
            a = op(None, None, R, Wr, 0.0, "a", FAR * (2500.0 + nbytes * len(srcs) / 250.0), extra=[o])
            a["fix"] = FAR * 2500.0
            a["sem"] = s
            a["val"] = val

    def gop(fn, R, Wr, nel):
        return op("g", lambda g, e: fn(g), R, Wr, 170.0 + 2.0 * nel * CYC)

    def fill(b, hi, val):
        return vop(lambda v: v.memset(T[b][:, 0:hi], val), [], [r(b)], hi, 0.5)

    BIG = 128 * V * 2
    dma("y", T.h[:, :], T.hf[:, :], [], [r("h")], BIG)
    dma("s", T.tab[:, 0:128], T.sa[:, :], [], [r("tab", 0, 128)], BIG // 8)
    dma("s", T.tab[:, 128:256], T.sb[:, :], [], [r("tab", 128, 256)], BIG // 8)
    dma("s", T.tab[:, 256:384], T.lim[:, :], [], [r("tab", 256, 384)], BIG // 8)
    fill("p0s", V, -CENTER)
    dma("g", T.p0s[:, :], T.p0[:, :], [], [r("p0s")], BIG, True, False)
    dma("y", T.E0[:, :], T.toll[:, :], [], [r("E0")], BIG)
    for lo in (0, 1024):
        gop(lambda g, lo=lo: g.iota(T.J[:, lo:lo + 1024], [[1, 1024]], 32 + lo, 0, allow_small_or_imprecise_dtypes=True), [], [r("J", lo, lo + 1024)], 1024)
    send([([w("h")], 1, w("hm"))], BIG, True)
    send([([w("tab", 0, 384)], -1, w("tab1", 0, 384)), ([w("tab", 0, 384)], -2, w("tab2", 0, 384))], BIG // 3)
    fill("ones", 128, 1.0)
    fill("Tl", 160, 0.0)
    fill("Bc", V, 1.0)
    fill("MM", 768, 0.0)
    fill("TS", 640, 0.0)
    if "c" in PAR["w2"]:
        fill("one5", CH, 1.0)
        fill("cv", 256, -1.0)
        for k in (128, 130):
            gop(lambda g, k=k: g.iota(T.cv[:, k:256:16], [[0, 8]], -17, 0, allow_small_or_imprecise_dtypes=True), [], [r("cv")], 8)
    gop(lambda g: g.affine_select(T.I[:, :], T.ones[:, :], [[-1, 128]], A.is_equal, 0.0, 0, 1), [r("ones")], [r("I")], 128)
    gop(lambda g: g.affine_select(T.nI[:, :], T.I[:, :], [[-1, 128]], A.not_equal, -1.0, 0, 1), [r("I")], [r("nI")], 128)
    gop(lambda g: g.affine_select(T.g8[:, 0:8], T.ones[:, 0:8], [[-16, 8]], A.is_ge, 0.0, 0, 1), [r("ones")], [r("g8", 0, 8)], 8)
    gop(lambda g: g.affine_select(T.g8[:, 8:16], T.g8[:, 0:8], [[16, 8]], A.is_ge, 0.0, 15, -1), [r("g8", 0, 8)], [r("g8", 8, 16)], 8)
    gop(lambda g: g.affine_select(T.Tl[:, 16:144:16], T.g8[:, 8:16], [[0, 8]], A.is_ge, 0.0, 0, 0), [r("g8", 8, 16)], [r("Tl")], 8)
    gop(lambda g: g.iota(T.pi[:, 0:1], [[0, 1]], 0, 1), [], [r("pi")], 1)
    gop(lambda g: g.iota(T.io16[:, :], [[16, 128]], 0, 0, allow_small_or_imprecise_dtypes=True), [], [r("io16")], 128)
    for (b, x) in (("Tf", 1.0 / 16), ("T2w", 2.0), ("TN", -STEEP)):
        times(w(b, 0, 160), w("Tl", 0, 160), x)
    times(w("g8", 16, 24), w("g8", 8, 16), -2.0)
    for (b, src, cmp, val, base) in (("Bc", "Bc", A.is_equal, 0.0, 0), ("B6", "Bc", A.not_equal, 6.0, 0),
                                     ("B6", "B6", A.not_equal, 5.0, -16), ("B6", "B6", A.not_equal, 5.0, 112)):
        for hf in range(4):
            lo, hi = 512 * hf, 512 * hf + 512
            gop(lambda g, b=b, src=src, lo=lo, hi=hi, cmp=cmp, val=val, base=base - 4 * hf:
                g.affine_select(T[b][:, lo:hi], T[src][:, lo:hi], [[-1, 4], [-16, 8], [0, 16]], cmp, val, base, 1), [r(src, lo, hi)], [r(b, lo, hi)], 512)
    for k, val in enumerate((-16.0, 16.0, 0.0, 0.0)):
        gop(lambda g, k=k, val=val: g.affine_select(T.Bw[:, k:V:4], T.Bc[:, k:V:4], [[-1, 16], [-16, 8], [0, 4]], A.not_equal, val, 0, 1),
            [r("Bc")], [r("Bw")], 512)
    for (m, i, width, j, val) in ((0, 1, 4, 0, 16.0), (0, 0, 4, 0, -16.0), (0, 2, 1, 10, 16.0), (0, 0, 1, 10, 16.0), (0, 11, 16, 0, 24.0), (0, 11, 1, 11, -1.0),
                                  (0, 11, 1, 0, 15.0), (0, 11, 1, 4, 15.0), (0, 11, 1, 1, 49.0), (0, 11, 1, 5, 49.0),
                                  (1, 2, 4, 1, 16.0), (1, 0, 4, 1, 16.0), (1, 1, 1, 14, 16.0), (1, 0, 1, 14, -16.0),
                                  (4, 2, 4, 0, 16.0), (4, 10, 4, 0, 16.0), (4, 6, 4, 1, 16.0), (4, 14, 4, 1, 16.0),
                                  (4, 11, 2, 0, 1.0), (4, 11, 2, 1, 17.0), (4, 11, 2, 2, -33.0), (4, 11, 2, 3, -17.0)):
        x = w("MM", 128 * m, 128 * m + 128)
        gop(lambda g, x=x, i=i, width=width, j=j, val=val:
            g.affine_select(ap(x), ap(x), [[-16, 8], [200, 16 // width], [0, width]], A.not_equal, val, -i - 200 * j, 1), [x], [x], 128)
    for (m, j, src) in ([(m, j, T.g8[:, 16:24]) for (m, j) in ((2, 0), (2, 1), (2, 2), (5, 0), (5, 4))] +
                        [(m, j, T.T2w[:, 16:144:16]) for (m, j) in ((3, 4), (3, 5), (3, 6), (5, 1), (5, 5))]):
        x = w("MM", 128 * m, 128 * m + 128)
        gop(lambda g, m=m, j=j, src=src: g.affine_select(T.MM[:, 128 * m + j:128 * m + 128:16], src, [[0, 8]], A.is_ge, 0.0, 0, 0),
            [r("g8"), r("T2w")], [x], 8)
    for (m, i) in ((0, 0), (0, 4), (1, 1), (1, 5), (2, 2), (2, 6), (3, 0)):
        x = w("TS", 160 * m, 160 * m + 160)
        gop(lambda g, m=m, i=i: g.affine_select(T.TS[:, 160 * m + 16:160 * m + 144:16], T.TS[:, 160 * m + 16:160 * m + 144:16], [[-16, 8]], A.not_equal, 1.0, -i, 1),
            [x], [x], 8)
    ts(w("pm", 0, 1), w("pi", 0, 1), 15, None, A.bitwise_and)
    cp(w("pf", 0, 1), w("pm", 0, 1))
    ts(w("pf", 1, 2), w("pf", 0, 1), 1.0, 16.0, A.is_equal, A.mult)
    more(w("pf", 2, 3), w("pf", 1, 2), -17.0)
    op("s", lambda g, e: g.scalar.activation(T.ioL[:, :], T.io16[:, :], AF.Identity, bias=T.pf[:, 0:1]), [r("io16"), r("pf", 0, 1)], [r("ioL")], cst(128))
    more(sm("Ap"), sm("ioL"), V - OFF)
    cp(sm("ioh"), sm("ioL"))
    gop(lambda g: g.affine_select(T.Ik[:, :], T.I[:, :], [[-1, 128]], A.not_equal, V / 2, 0, 1), [r("I")], [r("Ik")], 128)
    cp(w("u0", 0, 256), w("tab", 0, 256))
    send([([w("u0", 0, 256)], -1, w("u1", 0, 256)), ([w("u0", 0, 256)], -2, w("u2", 0, 256))], BIG // 8)
    table = 1300.0
    for k, b in enumerate(("SCa", "SCb")):
        for (lo, hi, way) in pieces(PAR["sc"][k]):
            out, src = ind(w(b), offs("u0", lo, hi, k)), w("J", lo, hi)
            if way == "v":
                vop(lambda v, out=out, src=src: v.tensor_copy(out, ap(src)), [src, offs("u0", lo, hi, k)], [w(b)], hi - lo, SC)["sc"] = hi - lo
            else:
                op("s", lambda g, e, out=out, src=src: g.scalar.activation(out, ap(src), AF.Silu), [src, offs("u0", lo, hi, k)], [w(b)],
                   cst(hi - lo, SC) + table)["sc"] = hi - lo
                table = 0.0
    ps = bank()
    for k, b in enumerate(("SCa", "SCb")):
        for i in range(16):
            mm([[(ps, 128 * k, 128 * k + 128), T.Tf[:, 16 - i:144 - i], T[b][:, i:V:16], i == 0, i == 15, 512]],
               [r(b), r("Tf")], [r(ps, 128 * k, 128 * k + 128)])
    ts(w("vi", 0, 256), w(ps, 0, 256), -32.0, None, A.add)
    cp(w("u0", 256, 512), w("vi", 0, 256))
    send([([w("u0", 256, 512)], -1, w("u1", 256, 512)), ([w("u0", 256, 512)], -2, w("u2", 256, 512))], BIG // 8)
    ts(sm("Bp"), w("tab1", 128, 256), -OFF, None, A.add)
    ts(sm("zt"), w("tab2", 256, 384), -CENTER, None, A.add)
    tt(sm("f3"), w("tab2", 128, 256), w("tab2", 0, 128), A.subtract)
    times(sm("dab"), sm("f3"), 0.5)
    tt(sm("a2f"), w("tab2", 0, 128), sm("dab"), A.add)
    for (lo, hi, way) in pieces(PAR["ss"]):
        for k in range(2):
            s, d = w("SS", lo, hi, V - k * V), w("DD", lo, hi, k * V)
            if way == "s":
                gather(w("t%d" % k, lo, hi), w("hm"), offs("u0", lo, hi, k), "s")
                ps = bank(hi - lo)
                psum(ps, lo, hi, [w("t%d" % k, lo, hi)], [w("h", lo, hi)])
                sop(d, w(ps, 0, hi - lo), AF.Abs)
                evac(s, w(ps, 0, hi - lo), "s")
            else:
                gfuse(s, w("hm"), offs("u0", lo, hi, k), w("h", lo, hi), A.subtract)
                sop(d, s, AF.Abs)
    for lo in (0, 1024):
        times(w("ndb", lo, lo + 1024), w("DD", lo, lo + 1024, V), -1.0, 0.5)
    send([([w("DD"), w("ndb")], -1, w("dd1"))], BIG, True)
    send([([w("E0"), w("DD", 0, V, V)], -1, w("O1"))], BIG)
    send([([w("DD"), w("ndb")], -2, w("dd2"))], BIG, True)
    send([([w("E0"), w("DD", 0, V, V)], -2, w("O2"))], BIG)

    def add_gather(out, win, off, other, lo, hi, way, tmp, eng="vs"):
        if way == "v":
            return gfuse(out, win, off, other, A.add)
        at = len(ops)
        gather(w(tmp, lo, hi), win, off, "s")
        ps = bank(hi - lo)
        psum(ps, lo, hi, [w(tmp, lo, hi), other])
        evac(out, w(ps, 0, hi - lo), eng)
        if way != "s":
            gfuse(out, win, off, other, A.add)
            for o in ops[at:]:
                o["alt"] = list(range(at, len(ops)))
                o["off"] = (o is ops[-1]) == (way == "y")

    for (lo, hi, way) in pieces(PAR["s0"]):
        for k in range(2):
            add_gather(w("YB", lo, hi, k * V), w("p0s"), offs("u0", lo, hi, k), w("DD", lo, hi, k * V), lo, hi, way, "t%d" % k)
        ps = bank(hi - lo)
        psum(ps, lo, hi, [w("YB", lo, hi)], [w("YB", lo, hi, V)])
        sop(w("IND", lo, hi), w(ps, 0, hi - lo), AF.Sign, bias=-0.5)
    for lo in (0, 64):
        ps = bank()
        tolist(ps, "IND", 16 * lo, 16 * lo + 1024, "Tl")
        ts(w("f4", lo, lo + 64), w(ps, lo, lo + 64), 1.0, float(V), A.is_gt, A.mult)
        tt(w("f2", lo, lo + 64), w("f4", lo, lo + 64), w("ioL", lo, lo + 64), A.add)
        cp(w("sel", lo, lo + 64), w("f2", lo, lo + 64))
    for (lo, hi, way) in pieces(PAR["sel0"]):
        add_gather(w("YA", lo, hi), w("YB", 0, 2 * V), offs("sel", lo, hi), w("E0", lo, hi), lo, hi, way, "t0")
    for lo in (0, 1024):
        times(w("nsa", lo, lo + 1024), w("SS", lo, lo + 1024, V), -1.0, 0.5)
    send([([w("SS", 0, 2 * V)], -1, w("SS1", 0, 2 * V))], 2 * BIG)
    send([([w("DD", 0, 2 * V)], -2, w("DD2", 0, 2 * V))], 2 * BIG)
    send([([w("SS"), w("nsa")], -2, w("dl2"))], BIG, True)
    if PAR["fold"]:
        for (lo, hi, way) in pieces(PAR["fp"]):
            ps = bank(hi - lo)
            psum(ps, lo, hi, [w("DD", lo, hi, V), w("E0", lo, hi)], [w("YA", lo, hi)])
            evac(w("h", lo, hi), w(ps, 0, hi - lo))

    def step1(f, Y, O):
        f1 = "f1" + "AB"[f % 2]
        for (lo, hi, way) in pieces(PAR["t1"][f]):
            add_gather(w(Y, lo, hi, V), w(Y), offs("u1", lo, hi), w("dd1", lo, hi), lo, hi, way, "t0")
        for (lo, hi, way) in pieces(PAR["i1"]):
            gfuse(w("IND1", lo, hi), w(Y), offs("u1", lo, hi, 1), w(Y, lo, hi, V), A.is_lt)
        for lo in (0, 64):
            ps = bank()
            tolist(ps, "IND1", 16 * lo, 16 * lo + 1024, "TN")
            tt(w(f1, lo, lo + 64), w(ps, lo, lo + 64), w("Ap", lo, lo + 64), A.min, 1.0)
            tt(w("f2", lo, lo + 64), w(f1, lo, lo + 64), w("Bp", lo, lo + 64), A.max)
            ts(w("sel", lo, lo + 64), w("f2", lo, lo + 64), OFF, None, A.add)
        if f % 2:
            ps = bank()
            toblock(ps, [("IND1", "Tl", 0)], 0, V, True, True)
            sop(sm("ws1"), sm(ps), AF.Sign, bias=-8.5)
        for (lo, hi, way) in pieces(PAR["sel"][f]):
            add_gather(w("P1", lo, hi), w(Y, 0, V + (1024 if hi <= 1024 else V)), offs("sel", lo, hi), w(O, lo, hi), lo, hi, way, "t1")
        sop(sm("s1"), sm(f1), AF.Sign, bias=OFF)
        ps = bank()
        small(ps, [("Ik", "s1"), ("I", "ioh")])
        ts(sm("sel" + "AB"[f % 2]), sm(ps), V / 2, None, A.add)

    def bound(plain):
        for (lo, hi, way) in pieces(PAR["fp"]):
            ps = bank(hi - lo)
            psum(ps, lo, hi, (), [w("DD2", lo, hi, V)] * plain + [w("O2", lo, hi)], [("Bc", "zt")])
            evac(w("nU", lo, hi), w(ps, 0, hi - lo))

    def step2a(rnd):
        for (lo, hi, way) in pieces(PAR["r2"][rnd]):
            a, b, u = offs("u2", lo, hi), offs("u2", lo, hi, 1), w("nU", lo, hi)
            if way == "S":
                gather(w("t0", lo, hi), w("P1"), a, "s")
                t = [w("t0", lo, hi), w("dd2", lo, hi)]
            else:
                gfuse(w("T2", lo, hi), w("P1"), a, w("dd2", lo, hi), A.add)
                t = [w("T2", lo, hi)]
            by = []
            if way == "V":
                gfuse(w("IND", lo, hi), w("P1"), b, t[0], A.is_lt)
                gfuse(w("IND", lo, hi, 2 * V), w("P1"), b, u, A.is_gt)
                by = [(slide("T2w", j), w("IND", lo, hi, j * V)) for j in (0, 2)]
                rows = [(1, t, [u])]
            else:
                y = w("t1", lo, hi)
                gather(y, w("P1"), b)
                rows = [(1, t, [u]), (0, t, [y]), (2, [y], [u])]
            for (j, plus, minus) in rows:
                ps = bank(hi - lo)
                psum(ps, lo, hi, plus, minus)
                o = over0(w("IND", lo, hi, j * V), w(ps, 0, hi - lo))
                by.append(([lambda o=o, j=j: ap(slide("T2w" if o["e"] == "v" else "Tl", j))], w("IND", lo, hi, j * V)))
            ps = bank(hi - lo)
            out, src = w("W2", lo, hi), w(ps, 0, hi - lo)
            if PAR["w2"][rnd] == "s":
                psum(ps, lo, hi, by=by)
                op("s", lambda g, e, out=out, src=src, way=way: g.scalar.activation(ap(out), ap(src), AF.Sign, bias=T.pf[:, 2:3] if way == "V" else -1.0),
                   [src, w("pf", 2, 3)], [out], cst(hi - lo))
            else:
                k = 128 * (way == "V")
                for a in range(0, hi - lo, CH):
                    mm([[(ps, a, a + CH), T.cv[0:1, k:k + 128], T.one5[0:1, :], True, False, CH]], [r("cv"), r("one5")], [(ps, a, a + CH)])
                psum(ps, lo, hi, by=by, start=False)
                unit(out, src)

    def step2b(rnd):
        for (lo, hi, way) in pieces(PAR["t2"][rnd]):
            add_gather(w("T2", lo, hi), w("P1"), offs("u2", lo, hi), w("dd2", lo, hi), lo, hi, way, "t0")
        for (lo, hi, way) in pieces(PAR["i2"]):
            gfuse(w("IND", lo, hi), w("P1"), offs("u2", lo, hi, 1), w("T2", lo, hi), A.is_lt)

    def mx(m):
        return w("MM", 128 * m, 128 * m + 128)

    def back(f, between):
        first = f % 2 == 0
        src, W1 = ("W2", "W1a") if first else ("IND", "W1b")
        cut = pieces(PAR["w1"])
        banks = [bank(hi - lo) for (lo, hi, way) in cut]
        out, own = bank(), bank()
        for ps, (lo, hi, way) in zip(banks, cut):
            if first:
                psum(ps, lo, hi, by=[(mx(5), w("IND1", lo, hi))], stop=False)
            else:
                psum(ps, lo, hi, tables=[("Bw", "ws1")], by=[(mx(4), w("W1a", lo, hi))], stop=False)
        for (lo, hi, way) in pieces(PAR["c2"]):
            gather(w("gx", lo, hi), w(src), offs("u2", lo, hi, 2))
            gather(w("gy", lo, hi), w(src), offs("u2", lo, hi, 3))
        for ps, (lo, hi, way) in zip(banks, cut):
            psum(ps, lo, hi, start=False,
                 by=[(mx(0 if first else 2), w("gx", lo, hi)), (mx(1 if first else 3), w("gy", lo, hi))])
            unit(w(W1, lo, hi), w(ps, 0, hi - lo))
            toblock(out, [(W1, "TS", 320)], lo, hi, lo == 0, hi == V)
        evac(sm("mo%d" % f), sm(out))
        send([([sm("mo%d" % f)], 1, sm("mi%d" % f))], BIG // 16)
        between()
        for (lo, hi, way) in pieces(PAR["c1"]):
            gather(w("gx", lo, hi), w(W1), offs("u1", lo, hi, 2))
            gather(w("gy", lo, hi), w(W1), offs("u1", lo, hi, 3))
            if hi == V:
                mm([[sm(own), T.I[:, :], T["mi%d" % f][:, :], False, False, 128]], [sm("mi%d" % f), r("I")], [sm(own)])
            toblock(own, [("gx", "TS", 0), ("gy", "TS", 160)], lo, hi, lo == 0, hi == V)
        return own

    outs = {"n": 0}

    def add_out(b):
        first, late = outs["n"] == 0, outs["n"] >= 5
        for (lo, hi, way) in pieces(PAR["add"] if late else "16x"):
            dma("y" if first else "g", T.gain[:, lo:hi], T[b][:, lo:hi], [r(b, lo, hi)], [r("gain", lo, hi)], 512 * (hi - lo), not first, not late)
        outs["n"] += 1

    def swap(rnd):
        ps = bank()
        small(ps, [("I", "wsA%d" % rnd), ("I", "nsB%d" % rnd)])
        times(sm("qc"), sm(ps), 0.5)
        for (lo, hi, way) in pieces(PAR["fp"]):
            ps = bank(hi - lo)
            psum(ps, lo, hi, tables=[("Bc", "qc")])
            tt(w("q", lo, hi), w("dl2", lo, hi), w(ps, 0, hi - lo), A.mult, 1.0)

    ways = list(PAR["terms"])

    def follow(d, way):
        src, lst = ("hm", "lA") if d == "fA" else ("p0s", "lB")
        for (lo, hi, x) in pieces(PAR["fg"]):
            if way in "vV":
                gfuse(w(d, lo, hi), w(src), offs(lst, lo, hi), w("q", lo, hi), A.add if d == "fA" else A.subtract)
            else:
                gather(w(d, lo, hi), w(src), offs(lst, lo, hi), turn=way in "dD" and d == "fB")

    def term(d, way):
        x, bias, tmp = ("J", 0.0, "ndb") if d == "fA" else ("SCa", -math.log(2.0), "nsa")
        if way in "dD":
            dma("g", T[d][:, :], T.q[:, :], [w("q")], [w(d)], BIG, True)
        for (lo, hi, y) in pieces(PAR["fp"]):
            ps = bank(hi - lo)
            if way in "DV":
                sop(w(d, lo, hi), w(d, lo, hi), AF.Abs)
            elif way == "p":
                psum(ps, lo, hi, [w(d, lo, hi)] + [w("q", lo, hi)] * (d == "fA"), [w("q", lo, hi)] * (d == "fB"))
                sop(w(d, lo, hi), w(ps, 0, hi - lo), AF.Abs)
            else:
                either(w(tmp, lo, hi), w(d, lo, hi), (0.0, 2.0, A.max, A.mult), AF.Relu, scale=2.0, k=0.5)
                psum(ps, lo, hi, [w(tmp, lo, hi)], [w(d, lo, hi)])
                sop(w(x, lo, hi), w(ps, 0, hi - lo), AF.Exp, bias=bias, scale=-0.125)
        if way in "pDV":
            for (lo, hi, y) in pieces(PAR["fe"]):
                sop(w(x, lo, hi), w(d, lo, hi), AF.Exp, bias=bias, scale=-0.125)
        add_out(x)

    def edges2():
        for (lo, hi, way) in pieces(PAR["fe"]):
            sop(w("SCb", lo, hi), w("DD2", lo, hi), AF.Exp, scale=-0.125)
            sop(w("eb", lo, hi), w("DD2", lo, hi, V), AF.Exp, scale=-0.125)
            times(w("eb", lo, hi), w("eb", lo, hi), -1.0)
        for k in range(3):
            add_out("SCb")
        dma("g", T.eb[:, :], T.SCb[:, :], [w("SCb")], [w("eb")], 2 * BIG, True)

    def gain1():
        ps = bank()
        small(ps, [("I", "nsB0"), ("nI", "wsA0"), ("nI", "wsA0"), ("nI", "wsA1"), ("nI", "wsA1"), ("I", "nsB1")])
        either(sm("kp"), sm(ps), (0.25, -1.5, A.mult, A.add), AF.Identity, bias=-1.5, scale=0.25)
        for (lo, hi, way) in pieces(PAR["fp"]):
            ps = bank(hi - lo)
            psum(ps, lo, hi, tables=[("Bc", "kp")])
            tt(w("eb", lo, hi), w("eb", lo, hi), w(ps, 0, hi - lo), A.mult, 1.0)
        add_out("eb")

    def pick(dst, sel):
        for (lo, hi, way) in pieces(PAR["fg"]):
            gather(w(dst, lo, hi), w("SS1", 0, 2 * V), offs(sel, lo, hi))

    def lists(rnd, first):
        src, tl, to = ("W2", "TS", 480) if first else ("IND", "Tl", 0)
        ps = bank()
        toblock(ps, [(src, tl, to)], 0, V, True, True)
        if first:
            evac(sm("wsA%d" % rnd), sm(ps))
        else:
            sop(sm("nsB%d" % rnd), sm(ps), AF.Sign, bias=8.5, scale=-1.0)
        ps = bank()
        tolist(ps, src, 0, V, tl, to)
        if first:
            tt(sm("f4"), sm(ps), sm("dab"), A.mult, 1.0)
        else:
            sop(sm("f3"), sm(ps), AF.Sign, bias=-8.5)
            tt(sm("f4"), sm("f3"), sm("dab"), A.mult)
        tt(sm("f3"), sm("f4"), sm("a2f"), A.add)
        cp(sm("lA" if first else "lB"), sm("f3"))

    def terms(rnd):
        a, b = ways[2 * rnd:2 * rnd + 2]
        swap(rnd)
        if a in "vV":
            follow("fA", a)
        term("fA", a)
        follow("fB", b)
        term("fB", b)

    H = V // PAR["halves"]
    for rnd in range(2):
        e0, ent, eni = ("E0", "ent0", "eni0") if rnd == 0 else ("E0n", "ent1", "eni1")
        bound(rnd * PAR["plain"])
        step1(2 * rnd, "YA", "O1")
        if rnd == 1:
            terms(0)
        pick("hm", "selA")
        step2a(rnd)
        if rnd == 0:
            edges2()
        lists(rnd, True)
        own = back(2 * rnd, lambda: None)
        if ways[2 * rnd] not in "vV":
            follow("fA", ways[2 * rnd])
        cut = pieces(PAR["y"])
        banks = [bank(hi - lo) for (lo, hi, way) in cut]
        for ps, (lo, hi, way) in zip(banks, cut):
            psum(ps, lo, hi, [w("YA", lo, hi)], stop=False)
        marked(sm(ent), own)
        if not PAR["fold"]:
            send([([sm(ent)], -1, sm(eni))], BIG // 16)
        for ps, (lo, hi, way) in zip(banks, cut):
            psum(ps, lo, hi, tables=[("B6", ent)], start=False)
            evac(w("YB", lo, hi), w(ps, 0, hi - lo))
        times(sm("ent3"), sm(ent), 3.0)
        if PAR["fold"]:
            for lo in range(0, V, H):
                send([([w("YB", lo, lo + H), w("h", lo, lo + H)], -1, w("nU", lo, lo + H))], BIG // PAR["halves"], rnd == 0)
        else:
            for (lo, hi, way) in pieces(PAR["fp"]):
                ps = bank(hi - lo)
                psum(ps, lo, hi, [w("O1", lo, hi)], tables=[("B6", eni)])
                evac(w("nU", lo, hi), w(ps, 0, hi - lo))
        step1(2 * rnd + 1, "YB", "nU")
        pick("p0s", "selB")
        step2b(rnd)
        lists(rnd, False)
        own = back(2 * rnd + 1, (lambda: None) if rnd == 0 else lambda: (gain1(), terms(1)))
        cut = pieces(PAR["clip" if rnd == 0 else "out"])
        banks = [bank(hi - lo) for (lo, hi, way) in cut]
        for ps, (lo, hi, way) in zip(banks, cut):
            psum(ps, lo, hi, [w(e0, lo, hi)], tables=[] if PAR["dm"] else [("Bc", "ent3")], stop=False)
        ts(sm("s2"), sm(own), -5.0, -3.0, A.is_gt, A.mult)
        if PAR["dm"]:
            tt(sm("dm"), sm("s2"), sm("ent3"), A.add)
        for ps, (lo, hi, way) in zip(banks, cut):
            psum(ps, lo, hi, tables=[("Bc", "dm" if PAR["dm"] else "s2")], start=False)
            if rnd == 0 and way == "s":
                sop(w("t0", lo, hi), w(ps, 0, hi - lo), AF.Relu)
                ts(w("E0n", lo, hi), w("t0", lo, hi), 63.0, None, A.min, k=0.5)
            elif rnd == 0:
                ts(w("E0n", lo, hi), w(ps, 0, hi - lo), 0.0, 63.0, A.max, A.min)
            else:
                if way == "s":
                    sop(w("t0", lo, hi), w(ps, 0, hi - lo), AF.Relu, bias=63.0, scale=-1.0)
                    sop(w("SCb", lo, hi), w("t0", lo, hi), AF.Relu, bias=63.0, scale=-1.0)
                else:
                    ts(w("SCb", lo, hi), w(ps, 0, hi - lo), 0.0, 63.0, A.max, A.min)
                dma("y", T.tollout[:, lo:hi], T.SCb[:, lo:hi], [w("SCb", lo, hi)], [w("tollout", lo, hi)], 512 * (hi - lo))
        if rnd == 0:
            for (lo, hi, way) in pieces(PAR["y"]):
                ps = bank(hi - lo)
                psum(ps, lo, hi, [w("YA", lo, hi)], [w("E0", lo, hi)], stop=False)
                psum(ps, lo, hi, [w("E0n", lo, hi)], start=False)
                evac(w("YA", lo, hi), w(ps, 0, hi - lo))
            for lo in range(0, V, H):
                send([([w("E0n", lo, lo + H), w("DD", lo, lo + H, V)], -1, w("O1", lo, lo + H))], BIG // PAR["halves"])
            for lo in (0, 1024):
                send([([w("E0n", lo, lo + 1024)] + [w("DD", lo, lo + 1024, V)] * (1 - PAR["plain"]), -2, w("O2", lo, lo + 1024))], BIG // 2)
    return ops


def place(ops, before, after, key, back, lean):
    n = len(ops)
    left = [len(x) for x in before]
    ready = sorted((key[i], i) for i in range(n) if not left[i])
    busy = {e: [[], []] for e in "vspgy"}
    at, start, fin, eng = [0.0] * n, [0.0] * n, [0.0] * n, [None] * n
    while ready:
        i = ready.pop(0)[1]
        o = ops[i]
        t0 = at[i] + o["lat"] if back else at[i]
        t, e, end = t0, None, t0
        for x, cost in [] if o.get("off") else o["on"]:
            los, his = busy[x]
            k = m = len(his)
            while k and his[k - 1] > t0:
                k -= 1
            u = t0
            while k < m and los[k] < u + cost:
                if his[k] > u:
                    u = his[k]
                k += 1
            if e is None or u + cost <= end + lean[i]:
                t, e, j, end = u, x, k, u + cost
        if e:
            busy[e][0].insert(j, t)
            busy[e][1].insert(j, end)
        start[i], eng[i] = t, e
        fin[i] = end = end if back else end + o["lat"]
        for s in after[i]:
            u = end if e == "p" and ops[s]["eng"] == "p" else end + LAT
            if u > at[s]:
                at[s] = u
            left[s] -= 1
            if left[s] == 0:
                x = (key[s], s)
                lo, hi = 0, len(ready)
                while lo < hi:
                    mid = (lo + hi) // 2
                    if ready[mid] < x:
                        lo = mid + 1
                    else:
                        hi = mid
                ready.insert(lo, x)
    if max(left):
        raise ValueError("the instructions wait for one another in a circle")
    return start, fin, eng


def polish(ops, uses, home, seq, eng, rng, moves, heat, both, FAST, SLOW, anew):
    n, LAT = len(ops), FAST[3]
    pred, above = [], []
    succ = [set() for o in ops]
    for o in ops:
        far = 0
        for d in o["deps"]:
            succ[d].add(o["i"])
            far |= above[d]
        pred.append([(d, 0.0 if ops[d]["eng"] == "p" and o["eng"] == "p" else LAT, n + d, 0.0 if ops[d]["eng"] == "p" and o["eng"] == "p" else SLOW[3])
                     for d in o["deps"] if not far >> d & 1])
        above.append(far | sum(1 << d for d in o["deps"]))
    cost, cost2 = [[{e: c * x[0] / PCY if e == "p" and x[0] != PCY else c + o.get("ga", 0) * (x[1] - GA) + o.get("sc", 0) * (x[2] - SC) for e, c in o["on"]} for o in ops]
                   for x in (FAST, SLOW)]
    lat, lat2 = [[o["lat"] * x[4] / FAR if x[4] != FAR else o["lat"] for o in ops] for x in (FAST, SLOW)]
    dq = [o.get("dq", 0.0) / FAR if anew else 0.0 for o in ops]
    if anew:
        lat, lat2 = [[o.get("fix", o["lat"]) * x[4] / FAR for o in ops] for x in (FAST, SLOW)]
    alts = [o["alt"] for o in ops if o.get("alt", [0])[0] == o["i"] and "alt" in o]
    opens = {uses[u][0]: u for u in uses}
    shuts = {uses[u][-1]: u for u in uses}

    def run(seq, eng, old=None, same=0, until=1 << 30, allow=0.0):
        same -= same % 32
        if same:
            start, fin, why, banks, marks = list(old[1]), list(old[2]), list(old[3]), dict(old[4]), old[5][:same // 32]
            free, held, last = old[5][same // 32]
            free, held, last = dict(free), list(held), list(last)
        else:
            free = {e: (0.0, -1, 0.0) for e in "vspgyq"}
            start, fin, why = [0.0] * n, [0.0] * (2 * n), [-1] * (2 * n)
            held, last, banks, marks = [0.0] * 8, [None] * 8, {}, []
        for at in range(same, n):
            if at % 32 == 0:
                if at > until:
                    was = old[5][at // 32]
                    if min(free[e][0] - was[0][e][0] for e in "vsp") + min(free[e][2] - was[0][e][2] for e in "vsp") > allow:
                        return None
                    if (free, held, last) == was and fin == old[2]:
                        return old[0], start, fin, why, banks, marks + old[5][at // 32:]
                marks.append((dict(free), list(held), list(last)))
            i = seq[at]
            t = t2 = 0.0
            y = y2 = -1
            for d, x, d2, x2 in pred[i]:
                x += fin[d]
                if x > t:
                    t, y = x, d
                x2 += fin[d2]
                if x2 > t2:
                    t2, y2 = x2, d
            e = eng[i]
            if e == "-":
                start[i], fin[i], why[i], fin[n + i], why[n + i] = t, t - LAT, y, t2 - SLOW[3], y2
                continue
            if e:
                x, d, x2 = free[e]
                if x > t:
                    t, y = x, d
                if x2 > t2:
                    t2, y2 = x2, d
                if i in opens:
                    u = opens[i]
                    k = int(u[2])
                    can = [(held[b] if k == 1 else max(held[b], held[b + 1]), b) for b in range(0, 8, k)]
                    fit = [(held[b ^ 1] > t, x, b) for x, b in can if x <= t]
                    x, b = max(fit)[1:] if fit else min(can)
                    if x > 1e17:
                        return None
                    was = [last[c] for c in range(b, b + k) if last[c]]
                    if x > t:
                        t, y = x, max([uses[c][-1] for c in was], key=lambda d: fin[d])
                    for c in was:
                        d = uses[c][-1]
                        if fin[n + d] + SLOW[3] > t2:
                            t2, y2 = fin[n + d] + SLOW[3], d
                    banks[u] = (b, was)
                    held[b:b + k], last[b:b + k] = [1e18] * k, [u] * k
                x = t + cost[i][e]
                t2 += cost2[i][e]
                free[e] = (x, i, t2)
                if dq[i]:
                    x, t2 = max(x, free["q"][0]) + dq[i] * FAST[4], max(t2, free["q"][2]) + dq[i] * SLOW[4]
                    free["q"] = (x, i, t2)
            else:
                x = t
            start[i], fin[i], why[i], fin[n + i], why[n + i] = t, x + lat[i], y, t2 + lat2[i], y2
            if i in shuts:
                u = shuts[i]
                b = banks[u][0]
                held[b:b + int(u[2])] = [x + LAT] * int(u[2])
        return max(fin[:n]) + both * max(fin[n:]) + PAR["mean"] * sum(fin) / n, start, fin, why, banks, marks

    for k in range(40):
        if run(seq, eng) is not None:
            break
        late = [i for u in uses for i in uses[u][-2::-1] if (k > 20 or i == uses[u][0] and ops[uses[u][1]]["eng"] == "p") and rng.random() < 0.3]
        for i in late:
            a = seq.index(i)
            b = min(seq.index(j) for j in succ[i])
            seq = seq[:a] + seq[a + 1:b] + [i] + seq[b:]
    now = best = run(seq, eng) + (seq, eng)
    for k in range(moves):
        if k % 100 == 99:
            seq = sorted(now[6], key=lambda i: now[1][i])
            got = run(seq, now[7])
            if got is not None and got[0] <= now[0]:
                now, fresh = got + (seq, now[7]), True
        total, start, fin, why, banks, marks, seq, eng = now
        if k == 0 or fresh:
            pos = [0] * n
            for j, i in enumerate(seq):
                pos[i] = j
            chain, tails = [], {0: None, n: None}
            for m in (0, n):
                i = max(range(n), key=lambda i: fin[m + i])
                while why[m + i] >= 0:
                    if why[m + i] not in ops[i]["deps"] or len(cost[i]) > 1:
                        chain.append((i, why[m + i]))
                    i = why[m + i]
        i, p = chain[int(rng.integers(len(chain)))]
        how = rng.random()
        if anew and rng.random() < anew:
            a = 32 * int(rng.integers(n // 32))
            b = min(n - 1, a + int(rng.integers(24, 90)))
            m = n if how < PAR["slow"] else 0
            cs, wait = (cost2, SLOW[3]) if m else (cost, LAT)
            if tails[m] is None:
                tail, nxt = [0.0] * n, {}
                for j in reversed(seq):
                    x = max([tail[d] + wait for d in succ[j]] + [0.0]) + lat[j]
                    if eng[j] in cs[j]:
                        x = max(x, nxt.get(eng[j], 0.0) - PAR["loose"]) + cs[j][eng[j]]
                        nxt[eng[j]] = x
                    tail[j] = x
                tails[m] = tail
            part, eng = set(seq[a:b + 1]), list(eng)
            urge = {j: tails[m][j] + float(x) for j, x in zip(seq[a:b + 1], rng.normal(0.0, PAR["blur"], b + 1 - a))}
            free = {e: x[2 if m else 0] for e, x in marks[a // 32][0].items()}
            end, new, soon = {}, [], rng.random() * PAR["soon"]
            left = {j: len([d for d in ops[j]["deps"] if d in part]) for j in part}
            ready = {j: max([fin[m + x[0]] + wait for x in pred[j]] + [0.0]) for j in seq[a:b + 1] if not left[j]}
            while ready:
                can = [(max(t, free[e]), j, e) for j, t in ready.items() for e in (cs[j] if eng[j] in cs[j] else ())]
                idle = [j for j in ready if eng[j] not in cs[j]]
                if idle:
                    j = idle[0]
                    end[j] = ready[j] + (lat[j] if eng[j] is None else -wait)
                else:
                    t0 = min(can)[0] + soon
                    t, j, e = max([x for x in can if x[0] <= t0], key=lambda x: (urge[x[1]], -x[0]))
                    eng[j], free[e] = e, t + cs[j][e]
                    end[j] = free[e] + lat[j]
                new.append(j)
                del ready[j]
                for d in succ[j]:
                    if d in part:
                        left[d] -= 1
                        if not left[d]:
                            ready[d] = max([end.get(x[0], fin[m + x[0]]) + wait for x in pred[d]] + [0.0])
            seq = seq[:a] + new + seq[b + 1:]
        elif alts and rng.random() < PAR["ways"]:
            x = alts[int(rng.integers(len(alts)))]
            eng = list(eng)
            for j in x:
                eng[j] = "-" if eng[j] != "-" else ops[j]["eng"][int(rng.integers(len(ops[j]["eng"])))]
            a, b = min(pos[j] for j in x), min(pos[j] for j in succ[x[-1]]) - 1
            rest = [j for j in seq[a:b + 1] if j not in x]
            at = 0
            for j in x:
                lo = max([at] + [m + 1 for m, d in enumerate(rest) if d in ops[j]["deps"]])
                hi = min([len(rest)] + [m for m, d in enumerate(rest) if d in succ[j]])
                at = lo + int(rng.integers(min(hi - lo, 10) + 1))
                rest.insert(at, j)
                at += 1
            seq = seq[:a] + rest + seq[b + 1:]
        elif rng.random() < PAR["free"]:
            b = int(rng.integers(n))
            i, a = seq[b], max(0, b - int(rng.integers(1, 60)))
            if eng[i] == "-":
                fresh = False
                continue
            e = ("s" if eng[i] == "v" else "v") if len(cost[i]) > 1 and how < 0.5 else eng[i]
            if e and rng.random() < PAR["gaps"]:
                ready, end, can = max([fin[x[0]] + x[1] for x in pred[i]] + [0.0]), 0.0, []
                for j in seq[:b]:
                    if eng[j] == e:
                        if start[j] - max(end, ready) > PAR["room"] * cost[i][e]:
                            can.append(j)
                        end = fin[j] - lat[j]
                if not can:
                    fresh = False
                    continue
                a = pos[can[int(rng.integers(len(can)))]]
            need, part = {i}, seq[a:b + 1]
            for j in reversed(part):
                if not succ[j].isdisjoint(need):
                    need.add(j)
            seq = seq[:a] + [j for j in part if j in need] + [j for j in part if j not in need] + seq[b + 1:]
            if e != eng[i]:
                eng = list(eng)
                eng[i] = e
        elif how < PAR["flips"] or p in ops[i]["deps"]:
            x = i if len(cost[i]) > 1 and (how < PAR["flips"] / 2 or len(cost[p]) < 2) else p
            if len(cost[x]) < 2 or eng[x] == "-":
                fresh = False
                continue
            eng = list(eng)
            eng[x] = "s" if eng[x] == "v" else "v"
            a = b = pos[x]
        else:
            a, b = pos[p], pos[i]
            if how > 1.0 - PAR["far"]:
                a = max(0, a - int(rng.integers(12)))
            part = seq[a:b + 1]
            if rng.random() < 0.5:
                need = {i}
                for j in reversed(part):
                    if j in need or not succ[j].isdisjoint(need):
                        need.add(j)
                part = [j for j in part if j in need] + [j for j in part if j not in need]
            else:
                part = seq[pos[p]:b + 1 + (int(rng.integers(12)) if how > 1.0 - PAR["far"] else 0)]
                a, b = pos[p], pos[p] + len(part) - 1
                late = {p}
                for j in part:
                    if not late.isdisjoint(ops[j]["deps"]):
                        late.add(j)
                part = [j for j in part if j not in late] + [j for j in part if j in late]
            seq = seq[:a] + part + seq[b + 1:]
        allow = -heat * (1.0 - k / moves) * math.log(rng.random() + 1e-12)
        got = run(seq, eng, now, a, b + PAR["wait"], allow + PAR["give"])
        fresh = got is not None and got[0] <= total + allow
        if fresh:
            now = got + (seq, eng)
            if now[0] < best[0]:
                best = now
    total, start, fin, why, banks, marks, seq, eng = best
    more, banks = {}, {u: banks[u] for u in banks if eng[uses[u][0]] != "-"}
    for u in banks:
        for i in uses[u][:int(u[2])]:
            more[i] = set(j for c in banks[u][1] for j in uses[c])
    return max(fin[:n]), start, fin, eng, {u: banks[u][0] for u in banks}, more


def schedule(ops):
    n = len(ops)
    uses, home = {}, {}
    for o in ops:
        for x in o["R"] + o["W"]:
            if x[0].startswith("ps") and o["i"] not in home:
                uses.setdefault(x[0], []).append(o["i"])
                home[o["i"]] = x[0]
    short = {u: len([i for i in uses[u] if ops[i]["eng"] == "p"]) <= int(u[2]) for u in uses}

    def turn(pred):
        succ = [[] for _ in ops]
        for i in range(n):
            for d in pred[i]:
                succ[d].append(i)
        return succ

    def deal(start, fin):
        last, free, banks, more = [None] * 8, [-1.0] * 8, {}, {}
        for u in sorted(uses, key=lambda u: start[uses[u][-1]]):
            if ops[uses[u][0]].get("off"):
                continue
            k = int(u[2])
            can = [(max(free[b:b + k]), b) for b in range(0, 8, k)]
            fit = [x for x in can if x[0] + PAR["fit"] <= start[uses[u][0]]]
            b = max(fit)[1] if fit and short[u] else min(can)[1]
            banks[u] = b
            for x in range(b, b + k):
                if last[x] is not None:
                    for i in uses[u][:k]:
                        more.setdefault(i, set()).update(uses[last[x]])
                last[x], free[x] = u, fin[uses[u][-1]]
        return banks, more

    if "plan" not in PAR:
        base = [set(o["deps"]) for o in ops]
        for i in range(n):
            for d in ops[i]["deps"]:
                if d in home and home[d] != home.get(i):
                    base[i].add(uses[home[d]][-1])
        succ = turn(base)
        rng = np.random.default_rng(PAR["seed"])
        lean = [PAR["lean"][0 if o.get("ga") else 1] for o in ops]
        fin = place(ops, succ, base, [-i for i in range(n)], True, lean)[1]
        start, fin, eng = place(ops, base, succ, [-f for f in fin], False, lean)
        best = now = None
        for k in range(PAR["passes"]):
            banks, more = deal(start, fin)
            pred = [base[i] | more[i] if i in more else base[i] for i in range(n)]
            succ = turn(pred)
            mid, size = rng.random() * max(fin), PAR["shake"][k % len(PAR["shake"])]
            near = (np.abs(np.array(start) - mid) < PAR["span"]) * (rng.random(n) < PAR["part"])
            tilt = [float(x) for x in np.where(near * (rng.random(n) < PAR["flip"]), rng.choice(PAR["tilt"], n), lean)]
            fin = place(ops, succ, pred, [float(x) for x in rng.normal(0.0, size, n) * near - np.array(fin)], True, tilt)[1]
            start, fin, eng = place(ops, pred, succ, [-f for f in fin], False, tilt)
            if now is None or max(fin) < now[0] + PAR["slack"] * (1.0 - k / PAR["passes"]):
                now, lean = (max(fin), start, fin, eng, banks, more), tilt
            if best is None or now[0] < best[0]:
                best = now
            start, fin = now[1:3]
        best = best[:3] + (["-" if o.get("off") else e for o, e in zip(ops, best[3])],)
        for stage in PAR["stages"]:
            best = polish(ops, uses, home, sorted(range(n), key=lambda i: (best[1][i], i)), best[3], rng, *stage)
        PAR["plan"] = best
    total, start, fin, eng, banks, more = PAR["plan"]
    PAR["banks"] = banks
    for o in ops:
        o["t"], o["e"] = start[o["i"]], eng[o["i"]]
        o["cost"] = dict(o["on"]).get(o["e"], 0.0)
        for d in list(o["deps"]):
            if eng[d] == "-":
                o["deps"].pop(d)
                o["deps"].update({x: True for x in ops[d]["deps"]})
        for d in more.get(o["i"], ()):
            o["deps"].setdefault(d, False)
        if o["e"] == "-":
            o["e"] = None
    return sorted(range(n), key=lambda i: (start[i], i)), total


def rank_program(g, core, T, topo):
    if T.rank_of(core) is None:
        return
    ops = build(T, topo, core)
    order, total = schedule(ops)
    Q = {"v": g.vector, "s": g.scalar, "p": g.tensor, "g": g, "y": g.sync}
    pos = {i: k for k, i in enumerate(order)}
    seen = {e: {} for e in Q}
    need = set()
    waits = {}
    for i in order:
        o = ops[i]
        e = o["e"]
        if e is None:
            continue
        w = []
        top = {}
        for d, hard in o["deps"].items():
            p = ops[d]
            if p["kind"] == "n":
                continue
            if p["kind"] in "da":
                if d not in seen[e]:
                    seen[e][d] = True
                    w.append(d)
            elif p["kind"] == "x":
                if p["inc"]:
                    raise ValueError("a buffer that is being sent is written again")
            elif p["e"] != e or (hard and e != "p"):
                if p["e"] not in top or pos[d] > pos[top[p["e"]]]:
                    top[p["e"]] = d
        for x, d in top.items():
            if pos[d] > seen[e].get(x, -1):
                seen[e][x] = pos[d]
                w.append(d)
                need.add(d)
        waits[i] = w
    count = {e: 0 for e in Q}
    val = {}
    sent = 0
    for i in order:
        o = ops[i]
        e = o["e"]
        if e is None:
            continue
        for d in waits[i]:
            p = ops[d]
            if p["kind"] == "d":
                Q[e].wait_ge(T.sem[p["sem"]], 16)
            elif p["kind"] == "a":
                Q[e].wait_ge(T.sem[p["sem"]], p["val"])
            else:
                Q[e].wait_ge(T.sem["e" + p["e"]], val[d])
        ins = o["fn"](g, e)
        if o["kind"] == "d":
            ins.then_inc(T.sem[o["sem"]], 16)
        elif o["kind"] == "x":
            sent += o["inc"]
        elif i in need:
            count[e] += 1
            val[i] = count[e]
            ins.then_inc(T.sem["e" + e], 1)
    g.wait_ge(T.sem.sent, sent)
    for o in ops:
        if o["kind"] == "d":
            g.wait_ge(T.sem[o["sem"]], 16)
        elif o["kind"] == "a":
            g.wait_ge(T.sem[o["sem"]], o["val"])
